import numpy as np, ml_dtypes
CORES = [16,17,18,19,32,33,34,35]
N = 8
import mx_ref
BF = ml_dtypes.bfloat16
def gcols(t, e):
    v = np.concatenate([t.reshape(8, 16, -1, 4), np.zeros((8, 16, 1, 4), BF)], axis=2)
    return np.ascontiguousarray(np.stack([v[g][:, e[g]] for g in range(8)])).reshape(128, -1)
def tile(rs):
    return np.stack(rs, axis=2).reshape(128, -1).astype(BF)
def pick(q, e):
    c = np.concatenate([q[0].reshape(128, -1, 4), np.zeros((128, 1, 4), np.uint8)], axis=1); s = np.concatenate([q[1], np.ones((16, 1), np.uint8)], axis=1)
    return (np.ascontiguousarray(c[:, e].reshape(128, -1)), np.ascontiguousarray(s[:, e]))
def join(*qs):
    return (np.concatenate([q[0] for q in qs], axis=1), np.concatenate([q[1] for q in qs], axis=1))
def put(q, e, v):
    c, s = q[0].reshape(128, -1, 4).copy(), q[1].copy(); c[:, e] = v[0].reshape(128, -1, 4); s[:, e] = v[1]
    return (c.reshape(128, -1), s)
def pk(c, s):
    return (np.ascontiguousarray(c), mx_ref.live(s))
def emit(q):
    return q[0], q[1]
def packed(v, rng):
    q = [mx_ref.quantize(np.ascontiguousarray(v[r])) for r in range(N)]
    return np.stack([a for a, b in q]), np.stack([mx_ref.plane(b, rng) for a, b in q])
def values_of_codes():
    e, c = np.zeros((128, 128, 4), np.float32), np.zeros((128, 2, 4), np.uint8)
    e[np.arange(128), np.arange(128), 0] = 1
    c[:127, :, 0] = np.arange(256).reshape(2, 128).T[:127]
    return mx_ref.matmul(mx_ref.quantize(e.reshape(128, 512).astype(BF)), (c.reshape(128, 8), np.full((16, 2), 127, np.uint8))).T.reshape(-1).astype(np.float64)
CODE_VALUE, SCALE_VALUE = values_of_codes(), 2.0 ** (np.arange(256) - 127.0)
def decode(q):
    return (CODE_VALUE[q[0]].reshape(16, 8, -1, 4) * SCALE_VALUE[q[1]][:, None, :, None] + 0.0).reshape(128, -1).astype(np.float32)
def f(rng, *shape):
    return mx_ref.flush((rng.standard_normal(shape, dtype=np.float32) * np.exp2(rng.integers(-2, 3, shape[:-1] + (1,)))).astype(BF))
def wide(rng, *shape, cols=0):
    v = rng.standard_normal(shape, dtype=np.float32) * np.exp2(rng.integers(-12, 13, shape)).astype(np.float32)
    if cols: v *= np.repeat(np.exp2(rng.integers(-cols, cols + 1, shape[:-2] + (1, shape[-1] // 4))) * (rng.random(shape[:-2] + (1, shape[-1] // 4)) > 0.0625), 4, axis=-1).astype(np.float32)
    return mx_ref.flush(v.astype(BF))
C, R, SWEEPS = 384, 2, 12
def order(p):
    return np.argsort(-(p[::16] + np.float32(0.0)), axis=1, kind="stable")
def matched(a, b):
    gap = np.abs(a.reshape(8, C // 16, 16, 1) - b.reshape(8, C // 16, 1, 16))
    l = np.arange(16)
    k = np.zeros((8, C // 16, 16), np.int64)
    for s in range(SWEEPS):
        at = (l // 2) ^ k
        here = at[:, :, :, None] == l
        best = np.argmin(np.where(here, gap, np.float32(np.inf)), axis=2)
        stays = np.take_along_axis(best, at, axis=2) == l
        k = k + ~stays
    left = np.argsort(here.any(axis=2), axis=2, kind="stable")
    turn = np.argsort(np.argsort(stays, axis=2, kind="stable"), axis=2)
    m = np.where(stays, at, np.take_along_axis(left, turn, axis=2))
    return (m + 16 * np.arange(C // 16)[:, None]).reshape(8, C)
def same(u):
    return np.stack([u] * N)
def numbers_of(rng):
    return {"x": np.array(f(rng, N, 128, 4 * C)), "u": same(np.array(f(rng, 128, 512))), "v": np.array(f(rng, N, 128, 512))}
def packed_layer(w):
    return w.reshape(N, 128, 2048)
def weights(rng, w):
    c, p = packed(packed_layer(w), rng)
    return {"wc": c, "ws": p}
def apart(rng, free):
    w = np.array(f(rng, N, 128, 2048)).reshape(N, 8, 16, 4, 8, 16, 4)
    w[:, :, ~free] = 0
    w[:, :, :, :, :, ~free] = 0
    return weights(rng, w)
def digits(n, k):
    return n[..., None] & (1 << np.arange(k))
def deciding(rng, a, b, k):
    u = np.array(f(rng, 128, 512)).reshape(128, 128, 4)
    for h, m in ((0, a), (1, b)):
        u[:, h::16] = 0
        for g in range(8): u[16 * g:16 * g + 16, 16 * g + h] = (m * k[g]).astype(np.float32).astype(BF)
    return same(u.reshape(128, 512))
def setup_inputs(rng):
    return {**numbers_of(rng), **weights(rng, f(rng, N, 128, 2048))}
def setup_inputs_ties(rng):
    d = numbers_of(rng)
    e = rng.permutation(N)
    x = d["x"].reshape(N, 8, 16, C, 4)
    for r in range(N):
        k = np.zeros(C, int) if r == e[0] else rng.permutation(C) % 3
        a = x[r][:, :8, :3].copy()
        a[:, :, 2] = 0
        x[r][:, :8] = a[:, :, k]
    x[e[1]] = 0
    u = d["u"][0].reshape(8, 16, 128, 4)
    u[:, 8:, ::16] = 0
    u[:, 8:, 1::16] = 0
    w = np.array(f(rng, N, 128, 2048)).reshape(N, 8, 16, 4, 8, 16, 4)
    w[:, :, 8:, :, :, :8] = 0
    return {"x": x.reshape(N, 128, 4 * C), "u": same(u.reshape(128, 512)), "v": d["v"], **weights(rng, w)}
def setup_inputs_near(rng):
    d = numbers_of(rng)
    x = d["x"].astype(np.float32).reshape(N, 8, 16, C, 4)
    s = digits(np.arange(C) // 2, 8) * 2.0 ** -23
    e = digits(rng.integers(0, 24, (N, 8, C)), 8) * 2.0 ** -23
    m = ((np.arange(N) + rng.integers(2)) % 2 * 2.0 - 1.0)[:, None, None]
    x[:, :, :2] = 0
    x[:, :, 0, :, 0] = rng.choice([-1.0, 1.0], (N, 8, 1))
    x[:, :, 0, :, 1] = m * 2.0 ** -9
    x[:, :, 1, :, 0] = m
    x[:, :, 2:8] = rng.integers(4, 8, (N, 8, 6, C, 4)) * rng.choice([-1.0, 1.0], (N, 8, 6, C, 4)) * 0.25
    x[:, :, 8] = s[:, :4]
    x[:, :, 9] = s[:, 4:]
    x[:, :, 10] = e[..., :4]
    x[:, :, 11] = e[..., 4:]
    x[:, :, 12:] = rng.integers(4, 8, (N, 8, 4, C, 4)) * rng.choice([-1.0, 1.0], (N, 8, 4, C, 4)) * 2.0 ** -20
    x *= np.float32(2.0 ** -7)
    a, b = np.zeros((16, 4)), np.zeros((16, 4))
    a[0, 0] = 1
    a[8:10] = 1
    b[0, 1] = 1
    b[1, 0] = 1
    b[10:12] = 1
    i = np.arange(16)
    return {"x": x.reshape(N, 128, 4 * C).astype(BF), "u": deciding(rng, a, b, np.where(rng.permutation(8) < 4, 2.0 ** -30, 1.0)), "v": d["v"], **apart(rng, (i >= 2) & (i < 8))}
def setup_inputs_jilts(rng):
    d = numbers_of(rng)
    i = np.argsort(rng.random((N, 8, C)), axis=2)
    q = 1 + np.argsort(rng.random((N, 8, C // 16, 2, 8)), axis=4)
    q[:, :, :, 0] += 8
    q = q.reshape(N, 8, C // 16, 16)
    q[:, :, 1::3] = 1 + np.argsort(rng.random((N, 8, C // 16, 16)), axis=3)[:, :, 1::3]
    q[:, :, 2::3] = 8
    m = np.take_along_axis(q.reshape(N, 8, C), i, axis=2) * ((np.arange(N) + rng.integers(2)) % 2)[:, None, None]
    x = d["x"].astype(np.float32).reshape(N, 8, 16, C, 4)
    n = rng.integers(1, 64, (N, 8, C, 32)) * rng.choice([-0.0625, 0.0625], (N, 8, C, 32))
    np.put_along_axis(n, rng.integers(0, 32, (N, 8, C, 1)), -32640.0, axis=3)
    x[:, :, :8] = n.reshape(N, 8, C, 8, 4).transpose(0, 1, 3, 2, 4)
    x[:, :, 8:] = 0
    s = digits(C - 1 - i, 12)
    for k in range(3): x[:, :, 8 + k] = s[..., 4 * k:4 * k + 4]
    s = digits(m, 8) * rng.choice([-1.0, 1.0], (N, 8, C, 1))
    for k in range(2): x[:, :, 12 + k] = s[..., 4 * k:4 * k + 4]
    a, b = np.zeros((16, 4)), np.zeros((16, 4))
    a[8:11] = 1
    b[12:14] = 1
    return {"x": x.reshape(N, 128, 4 * C).astype(BF), "u": deciding(rng, a, b, np.ones(8)), "v": d["v"], **apart(rng, np.arange(16) < 8)}
def setup_inputs_huge(rng):
    d = numbers_of(rng)
    x = 2.0 ** 30 * (0.9 + 0.1 * rng.random((N, 8, 16, C, 4)))
    c = np.stack([rng.permutation(C) % 2 * 2.0 - 1.0 for r in range(N)])
    c[rng.permutation(N) < N // 2] = 1
    x[:, :, :6] *= c[:, None, None, :, None]
    x[:, :, 6:] *= ((np.arange(N) + rng.integers(2)) % 2 * 2.0 - 1.0)[:, None, None, None, None]
    u = d["u"][0].reshape(8, 16, 128, 4)
    for h, i, j in ((0, 0, 6), (1, 6, 16)):
        a = 2.0 ** 30 * (1 - 0.05 * rng.random((8, j - i, 8, 4))) * (rng.permutation(8) % 2 * 2.0 - 1.0)[:, None]
        u[:, :, h::16] = 0
        u[:, i:j, h::16] = a.astype(np.float32).astype(BF)
    w = np.zeros((N, 128, 4, 128, 4), np.float32)
    i = np.flatnonzero(np.arange(128) % 16 >= 14)
    for b in range(4): w[:, i, b, i, b] = 8
    return {"x": x.astype(np.float32).reshape(N, 128, 4 * C).astype(BF), "u": same(u.reshape(128, 512)), "v": d["v"], **weights(rng, w.astype(BF))}
def setup_inputs_spread(rng):
    d = setup_inputs(rng)
    d["x"] = wide(rng, N, 128, 4 * C, cols=6)
    return d
def check_inputs(d):
    b = []
    for k in ("x", "u", "v"):
        a = np.abs(d[k].astype(np.float32))
        if not (np.isfinite(a).all() and ((a == 0) | (a >= 2.0 ** -30) & (a <= 2.0 ** 30)).all()): b.append("a value of " + k)
    if (d["u"].astype(np.float32) != d["u"][:1].astype(np.float32)).any(): b.append("u differs between ranks")
    if ((d["wc"] & 127) == 127).any(): b.append("a code of wc")
    return b
def reference(x, u, v, wc, ws):
    qu = mx_ref.quantize(u[0])
    lay = [pk(wc[r], ws[r]) for r in range(N)]
    now = [mx_ref.quantize(x[r]) for r in range(N)]
    for t in range(R):
        o, mark, num, wed = [], [], [], []
        for r in range(N):
            p = mx_ref.matmul(qu, now[r])
            o.append(order(p))
            mark.append(np.take_along_axis(p[1::16], o[r], axis=1))
            num.append(decode(now[r]).astype(BF))
        for r in range(N):
            e = (r + 1) % N
            w = np.zeros((8, C), np.int64)
            np.put_along_axis(w, o[r], np.take_along_axis(o[e], matched(mark[r], mark[e]), axis=1), axis=1)
            wed.append(w)
        came = [decode(mx_ref.quantize(gcols(num[r], np.argsort(wed[r], axis=1)))) for r in range(N)]
        for r in range(N):
            wives = gcols(num[(r + 1) % N], wed[r]).astype(np.float32)
            q = mx_ref.quantize(np.maximum(wives, came[(r - 1) % N]).astype(BF))
            a = num[r].astype(np.float32).reshape(128, C, 4)
            now[r] = mx_ref.quantize(tile([a[:, :, b] + mx_ref.matmul(pick(lay[r], np.arange(128 * b, 128 * b + 128)), q) * np.float32(0.03125) for b in range(4)]))
    y, ol = np.zeros((N, 128, C), np.float32), np.zeros((N, 8, C), np.float32)
    oc, osc = np.zeros((N, 128, 4 * C), np.uint8), np.zeros((N, 16, C), np.uint8)
    for r in range(N):
        y[r] = mx_ref.matmul(mx_ref.quantize(v[r]), now[r])
        ol[r] = wed[r]
        oc[r], osc[r] = emit(now[r])
    return {"y": y, "ol": ol, "oc": oc, "osc": osc}

@@ -1,0 +1,633 @@
+from concourse.bass import DstId, RemoteDMATransfer
+from concourse.mybir import dt, AluOpType, ActivationFunctionType
+
+A = AluOpType
+F = ActivationFunctionType
+C = 384
+H = 192
+R = 2
+SW = 12
+W = 112
+B = 2.0 ** 30
+DS = 2.0 ** -42
+BIG = 2.0 ** 90
+TN = [384, 320, 256, 192, 128, 128]
+TO = [0, 384, 704, 960, 1152, 1280]
+KS = (23, 22, 21)
+LU, LM, LE, LA0, LA1, LBL, LBU, LSW, LH, LO0, LO1 = 0, 16, 142, 32, 46, 60, 74, 88, 112, 114, 128
+
+Q4, U8, F32, BF, I32, U16 = "float8_e4m3fn_x4", "uint8", "float32", "bfloat16", "int32", "uint16"
+SCRATCH = {"ps": ("psum", [128, 4096], F32)}
+
+
+def _sb(name, n, d):
+    SCRATCH[name] = ("sbuf", [128, n], d)
+
+
+for _n, _w in (("qu", 128), ("qus", 256), ("qv", 128), ("qw", 512), ("qx0", C), ("qx1", C), ("qx2", C), ("qn0", C), ("qn1", C),
+               ("qp0", C), ("qp1", C), ("qg", C), ("qz", C), ("qc", 1408), ("qt0", 130), ("qt1", 130), ("qe", 512), ("qs", 640)):
+    _sb(_n, _w, Q4)
+    _sb("s" + _n[1:], _w, U8)
+for _n, _w in (("xt", 4 * C), ("ut", 512), ("vt", 512), ("xn", 4 * C), ("gt", 4 * C), ("zt", 4 * C), ("ct", 4 * 1408), ("tt0", 520), ("tt1", 520),
+               ("et", 516), ("st", 2560), ("dn", 4 * C), ("dp", 4 * C), ("vg", 4 * C), ("sgn", 3 * C), ("junk", 3360)):
+    _sb(_n, _w, BF)
+for _n, _w in (("iof", C), ("cap", C), ("rho", C), ("mu", C), ("c0", 24), ("cf", 16), ("jm", 128), ("b16", 128), ("b8", 128), ("kb", W), ("kb1", W),
+               ("ky", 144), ("slot", 136), ("rst", 2 * W), ("mw", 2 * W), ("tf", 192), ("y1", C), ("fs", C), ("seg", C), ("rsum", 24), ("t1", 24),
+               ("t2", 24), ("y2", C), ("f2", C), ("ma", C), ("mb", C), ("aS", 416), ("oS", 416), ("ons", C), ("ta", 2 * W), ("tb", 2 * W),
+               ("tc", 2 * W), ("td", 2 * W), ("aa", 2 * W), ("oa", 240), ("dl", 2 * W), ("ee", 4 * W), ("dd", 4 * W), ("vv", 4 * W), ("ff", 4 * W),
+               ("fw", 4 * W), ("yy", 2 * W), ("rr", 2 * W), ("ro", 2 * W), ("ep", 2 * W), ("g2", 2 * W), ("gu", 2 * W), ("pr", 4 * W), ("hs", 4 * W),
+               ("wr", C), ("hr", C), ("yo", C)):
+    _sb(_n, _w, F32)
+for _n, _w in (("ii", C), ("ci", 16), ("lr", 34), ("kx", 108), ("ti", 64), ("pi", 24), ("pj", 72)):
+    _sb(_n, _w, I32)
+for _n, _w in (("lst", 160), ("pl", 24), ("ow0", 24), ("ow1", 24), ("on0", 24), ("on1", 24), ("hw0", 32), ("hw1", 32), ("hp0", 24), ("hp1", 24),
+               ("sp", 24), ("wl", 24), ("hl", 24)):
+    _sb(_n, _w, U16)
+
+ENG = ("v", "a", "t", "g", "s")
+DMAS = ["dx", "dx2", "du", "dv", "dw", "dw2", "out_s", "out_a"]
+ARR = ["an0", "an1", "ap0", "ap1", "al0", "al1", "ah0", "ah1"]
+SEMAPHORES = ["ev", "ea", "et", "eg", "sent"] + DMAS + ARR
+
+
+def rank_program(g, core, T, topo):
+    rank = T.rank_of(core)
+    if rank is None:
+        return
+    n = len(T.cores)
+    nxt, prv = T.cores[(rank + 1) % n], T.cores[(rank - 1) % n]
+    Q = {"v": g.vector, "a": g.scalar, "t": g.tensor, "g": g, "s": g.sync}
+    V, S, P = g.vector, g.scalar, g.tensor
+
+    ops, last_w, readers, sent = [], {}, {}, [0]
+
+    def add(eng, fn, rd=(), wr=(), sem=None, cnt=None):
+        deps = set()
+        for k in rd:
+            if k in last_w:
+                deps.add(last_w[k])
+            if k[0] == "#":
+                deps.update(i for i in readers.get(k, ()) if ops[i][0] != eng)
+        for k in wr:
+            if k in last_w:
+                deps.add(last_w[k])
+            deps.update(readers.get(k, ()))
+        if eng == "t":
+            deps = {i for i in deps if ops[i][0] != "t"}
+        me = len(ops)
+        ops.append((eng, fn, deps, sem, cnt))
+        for k in rd:
+            readers.setdefault(k, []).append(me)
+        for k in wr:
+            last_w[k] = me
+            readers[k] = []
+        return me
+
+    def arrive(key, sem, cnt):
+        last_w[key] = len(ops)
+        ops.append(("x", None, set(), sem, cnt))
+
+    def tt(out, a, b, op, rd, wr):
+        add("v", lambda: V.tensor_tensor(out, a, b, op), rd, wr)
+
+    def ts(out, a, s1, op0, rd, wr, s2=None, op1=None):
+        if op1 is None:
+            add("v", lambda: V.tensor_scalar(out, a, s1, None, op0), rd, wr)
+        else:
+            add("v", lambda: V.tensor_scalar(out, a, s1, s2, op0, op1), rd, wr)
+
+    def cp(out, a, rd, wr):
+        add("v", lambda: V.tensor_copy(out, a), rd, wr)
+
+    def scan(out, d0, d1, init, op0, op1, rd, wr):
+        add("v", lambda: V.tensor_tensor_scan(out, d0, d1, init, op0, op1), rd, wr)
+
+    def ms(ap, c, wr):
+        add("v", lambda: V.memset(ap, c), (), wr)
+
+    def act(out, a, f, rd, wr, **kw):
+        add("a", lambda: S.activation(out, a, f, **kw), rd, wr)
+
+    def qz(name, c0, c1, src, rd, wr):
+        add("v", lambda: V.quantize_mx(T["q" + name][:, c0:c1], T["s" + name][:, c0:c1], src), rd, wr)
+
+    def mm(bk, st, s0, mv, m0, m, start, stop, rd):
+        add("t", lambda: P.matmul_mx(T.ps[:, 512 * bk:512 * bk + m], T["q" + st][:, s0:s0 + 128], T["s" + st][:, s0:s0 + 128],
+                                     T["q" + mv][:, m0:m0 + m], T["s" + mv][:, m0:m0 + m], start, stop), rd, ["#%d" % bk])
+
+    def iota(out, pat, base, cm, wr, fl=False):
+        if fl:
+            add("g", lambda: g.iota(out, pat, base, cm, allow_small_or_imprecise_dtypes=True), (), wr)
+        else:
+            add("g", lambda: g.iota(out, pat, base, cm), (), wr)
+
+    def sel(out, a, pat, op, fill, base, cm, rd, wr):
+        add("g", lambda: g.affine_select(out, a, pat, op, fill, base, cm), rd, wr)
+
+    def dma(eng, out, a, sem, rd, wr):
+        add(eng, lambda: Q[eng].dma_start(out, a), rd, wr, sem, 16)
+
+    def bank(b, m):
+        return T.ps[:, 512 * b:512 * b + m]
+
+    def L(c, k):
+        return T.lst[:, c:c + k]
+
+    first, second = sorted((prv, nxt), key=lambda d: len(topo.engines(core, d)))
+    e1 = topo.engines(core, first)[:8]
+    e2 = [e for e in topo.engines(core, second) if e not in e1][:8]
+    mask = {first: sum(1 << e for e in e1), second: sum(1 << e for e in e2)}
+    assert len(e1) == 8 and len(e2) == 8
+
+    def send(items, rd):
+        def fn():
+            tr = []
+            for dst, src, land, sem in items:
+                rid, pid, _se = topo.addr(dst)
+                tr.append(RemoteDMATransfer(dst_ids=[DstId(rid=rid, pnc=pid)], dma_engine_mask=mask[dst], remote_sem=T.sem[sem], src=src, dst=land))
+            g.remote_dma_fused(tr, local_sem=T.sem.sent)
+        add("g", fn, rd, (), "-")
+        sent[0] += 8 * len(items)
+
+    col = lambda i: T.cf[:, i:i + 1]
+    lane_of = lambda k, t: T.st[:, 512 * k + t:512 * (k + 1):4]
+    tf = lambda i, k=14: T.tf[:, 16 * i:16 * i + k]
+
+    dma("s", T.xt[:, 0:768], T.x[:, 0:768], "dx", (), ["xt0"])
+    dma("a", T.ut[:], T.u[:], "du", (), ["ut"])
+    dma("a", T.xt[:, 768:1536], T.x[:, 768:1536], "dx2", (), ["xt1"])
+
+    iota(T.ci[:, 0:1], [[0, 1]], 0, 1, ["ci0"])
+    iota(T.ti[:, 0:16], [[1, 2], [16, 8]], 0, 0, ["ti0"])
+    iota(T.ii[:], [[0, 24], [1, 16]], 0, 0, ["ii"])
+    iota(T.jm[:], [[1, 8], [0, 16]], 0, 0, ["jm"], True)
+    iota(T.c0[:], [[16, 24]], 15, 0, ["c0"], True)
+    iota(T.tf[:, 128:152], [[32, 12], [8, 2]], 0, 0, ["tfs"], True)
+    iota(T.tf[:, 0:14], [[16, 14]], 0, 0, ["tf0"], True)
+    iota(T.iof[:], [[1, C]], 0, 0, ["iof"], True)
+    for q in range(6):
+        lo = TN[q] - (112 if q == 5 else 48)
+        ms(T.ct[:, 4 * (TO[q] + lo):4 * (TO[q] + TN[q])], 0.0, ["ct%d" % (4 * q + i) for i in range(4)])
+    for i, (sh, an) in enumerate(((0, 15), (4, 7), (3, 15), (3, 1), (0, 1), (1, 1), (2, 1), (0, 7))):
+        ts(T.ci[:, i + 1:i + 2], T.ci[:, 0:1], sh, A.arith_shift_right, ["ci0"], ["ci%d" % (i + 1)], an, A.bitwise_and)
+    cp(L(LU, 16), T.ti[:, 0:16], ["ti0"], ["LU"])
+    cp(T.cf[:, 0:9], T.ci[:, 0:9], ["ci%d" % i for i in range(9)], ["cf"])
+    ts(T.mu[:], T.ii[:], 0.0, A.is_gt, ["ii"], ["mu"])
+    ts(T.y2[:], T.ii[:], col(1), A.is_equal, ["ii", "cf"], ["y2"], 2 * BIG, A.mult)
+    ts(T.b16[:], T.jm[:], col(2), A.is_equal, ["jm", "cf"], ["b16"])
+    ms(T.rsum[:, 0:1], 0.0, ["rs0"])
+    ts(T.c0[:], T.c0[:], col(1), A.subtract, ["c0", "cf"], ["c0"])
+    ts(T.cf[:, 12:13], col(4), 8.0, A.mult, ["cf"], ["cf12"], col(1), A.add)
+    ms(T.et[:], 0.0, ["et"])
+    ms(T.b8[:], 0.0, ["b8"])
+    ts(L(LSW, 24), T.tf[:, 128:152], col(12), A.add, ["tfs", "cf12"], ["LSW"])
+    ms(T.tt0[:], 0.0, ["t0l0", "t0l1", "t0l2", "t0l3"])
+    ms(T.tt1[:], 0.0, ["t1l0", "t1l1", "t1l2", "t1l3"])
+    act(T.rho[:], T.mu[:], F.Identity, ["mu"], ["rho"], scale=2 * BIG, bias=-BIG)
+    act(T.cap[:], T.y2[:], F.Identity, ["y2"], ["cap"], bias=-BIG)
+    for t in range(4):
+        act(lane_of(0, t), T.b16[:], F.Copy, ["b16"], ["st0%d" % t])
+    qz("u", 0, 128, T.ut[:], ["ut"], ["qu"])
+    cp(T.qus[:].bitcast(dt.uint32), T.qu[:].bitcast(dt.uint32).indirect(L(LU, 16)), ["qu", "LU"], ["qus"])
+    act(T.sus[:], T.su[:].indirect(L(LU, 16)), F.Copy, ["qu", "LU"], ["sus"])
+    qz("x0", 0, C, T.xt[:], ["xt0", "xt1"], ["qx0"])
+    for k, t in ((1, 1), (1, 3), (2, 1), (2, 3), (3, 1), (3, 3), (4, 0), (4, 1), (4, 3)):
+        act(lane_of(k, t), T.b16[:], F.Copy, ["b16"], ["st%d%d" % (k, t)], scale=0.0)
+    qz("s", 0, 128, T.st[:, 0:512], ["st0%d" % t for t in range(4)], ["qs0"])
+
+    def constants_g():
+        iota(T.lr[:], [[1, 17], [0, 2]], -1, 0, ["lr"])
+        iota(T.slot[:], [[0, 4], [1, 17], [0, 2]], 0, 0, ["slot"], True)
+        eye = [[-1, 128]]
+        sel(T.b8[:], T.b8[:], [[8, 16], [0, 8]], A.is_gt, 1.0, 0, -1, ["b8"], ["b8"])
+        sel(T.b8[:], T.b8[:], [[8, 16], [0, 8]], A.is_ge, 0.0, 7, -1, ["b8"], ["b8"])
+        sel(lane_of(2, 1), lane_of(2, 1), eye, A.not_equal, B, 0, 1, ["st21"], ["st21"])
+        sel(lane_of(3, 3), lane_of(3, 3), eye, A.not_equal, B, 0, 1, ["st33"], ["st33"])
+        sel(T.et[:, 3:515:4], T.et[:, 3:515:4], eye, A.not_equal, 32.0, 0, 1, ["et"], ["et"])
+        sel(T.jm[:], T.b8[:], [[1, 128]], A.is_ge, 0.0, 0, -1, ["b8"], ["jm"])
+        sel(lane_of(4, 2), T.jm[:], eye, A.not_equal, 16.0, 0, 1, ["jm"], ["st42"])
+
+    def constants_a():
+        for k, sg in ((1, B), (2, -B), (3, -B)):
+            for t in (0, 2):
+                act(lane_of(k, t), T.b8[:], F.Copy, ["b8"], ["st%d%d" % (k, t)], scale=sg)
+        for h in range(2):
+            act(T.mw[:, h * W:(h + 1) * W], T.slot[:, 0:W], F.Sign, ["slot"], ["mw%d" % h])
+        act(T.rst[:], T.mw[:], F.Identity, ["mw0", "mw1"], ["rst"], scale=-B, bias=B)
+
+    def lists_v():
+        ts(tf(0), tf(0), col(1), A.add, ["tf0", "cf"], ["tf0"])
+        ts(T.cf[:, 13:14], col(5), 32.0, A.mult, ["cf"], ["cf13"])
+        ts(T.cf[:, 10:11], col(4), -1.0, A.mult, ["cf"], ["cf10"], 1.0, A.add)
+        ts(tf(10), tf(0), 112.0, A.is_ge, ["tf0"], ["tf10"], -112.0, A.mult)
+        ts(tf(2), tf(0), 112.0, A.is_ge, ["tf0"], ["tf2"], 192.0, A.mult)
+        ms(T.aS[:, C:416], 2 * B, ["aSx"])
+        tt(tf(1), tf(10), tf(0), A.add, ["tf10", "tf0"], ["tf1"])
+        ts(tf(2), tf(2), col(13), A.add, ["tf2", "cf13"], ["tf2"])
+        ms(T.oS[:, C:416], 0.0, ["oSx"])
+        ts(tf(3), tf(1), 34.0, A.is_ge, ["tf1"], ["tf3"])
+        ts(tf(4), tf(1), 68.0, A.is_ge, ["tf1"], ["tf4"])
+        ts(T.kx[:, 0:34], T.lr[:], 1, A.arith_shift_right, ["lr"], ["kx0"], 1, A.bitwise_and)
+        tt(tf(3), tf(3), tf(4), A.add, ["tf3", "tf4"], ["tf3"])
+        ts(T.kx[:, 36:70], T.lr[:], 2, A.arith_shift_right, ["lr"], ["kx1"], 1, A.bitwise_and)
+        ts(tf(4), tf(3), 34.0, A.mult, ["tf3", "cf"], ["tf4"], col(5), A.add)
+        ts(tf(5), tf(3), 64.0, A.mult, ["tf3"], ["tf5"])
+        ts(T.kx[:, 72:106], T.lr[:], 3, A.arith_shift_right, ["lr"], ["kx2"], 1, A.bitwise_and)
+        tt(tf(6), tf(1), tf(4), A.subtract, ["tf1", "tf4"], ["tf6"])
+        tt(tf(5), tf(5), tf(2), A.add, ["tf5", "tf2"], ["tf5"])
+        for b in range(2):
+            ts(T.ky[:, 36 * b:36 * b + 34], T.kx[:, 36 * b:36 * b + 34], col(5 + b), A.not_equal, ["kx%d" % b, "cf"], ["ky%d" % b], B * 2 ** b, A.mult)
+        ts(tf(1), tf(6), 0.0, A.is_equal, ["tf6"], ["tf1"], 384.0, A.mult)
+        ts(tf(2), tf(6), 0.5, A.mult, ["tf6"], ["tf2"], -1.0, A.add)
+        ts(tf(3), tf(6), 18.0, A.is_ge, ["tf6"], ["tf3"], 8.0, A.mult)
+        ts(T.ky[:, 72:106], T.kx[:, 72:106], col(7), A.not_equal, ["kx2", "cf"], ["ky2"], B * 4, A.mult)
+        tt(tf(2), tf(2), tf(5), A.add, ["tf2", "tf5"], ["tf2"])
+        tt(T.ky[:, 0:34], T.ky[:, 0:34], T.ky[:, 36:70], A.add, ["ky0", "ky1"], ["ky0"])
+        ts(L(LBL, 14), tf(5), 15.0, A.add, ["tf5"], ["LB"])
+        tt(tf(2), tf(2), tf(1), A.max, ["tf2", "tf1"], ["tf2"])
+        tt(T.ky[:, 0:34], T.ky[:, 0:34], T.ky[:, 72:106], A.add, ["ky0", "ky2"], ["ky0"])
+        ts(L(LBU, 14), tf(5), 31.0, A.add, ["tf5"], ["LB2"])
+        tt(tf(3), tf(3), tf(2), A.add, ["tf3", "tf2"], ["tf3"])
+        cp(L(LO0, 14), tf(2), ["tf2"], ["LO0"])
+        ts(L(LO1, 14), tf(2), 16.0, A.add, ["tf2"], ["LO1"])
+        cp(L(LA0, 14), tf(3), ["tf3"], ["LA0"])
+        ts(L(LA1, 14), tf(3), 8.0, A.add, ["tf3"], ["LA1"])
+        ts(L(LM, 7), tf(4, 7), 32.0, A.add, ["tf4"], ["LM"])
+        qz("s", 128, 640, T.st[:, 512:2560], ["st%d%d" % (k, t) for k in range(1, 5) for t in range(4)], ["qs1"])
+
+    def late_lists(step):
+        if step == 0:
+            ts(tf(7, 2), tf(0, 2), 12.0, A.is_ge, ["tf0"], ["tf7"], 122.0, A.mult)
+            cp(T.ti[:, 16:18], tf(0, 2), ["tf0"], ["ti1"])
+        elif step == 1:
+            ts(T.cf[:, 14:15], col(5), 112.0, A.mult, ["cf"], ["cf14"], col(6), A.add)
+            ts(T.ti[:, 18:20], T.ti[:, 16:18], 2, A.arith_shift_right, ["ti1"], ["ti2"])
+        elif step == 2:
+            ts(T.tf[:, 116:118], T.ti[:, 18:20], 34.0, A.mult, ["ti2", "cf14"], ["tf7b"], col(14), A.add)
+            tt(tf(10), tf(4), tf(10), A.subtract, ["tf4", "tf10"], ["tf10"])
+        elif step == 3:
+            tt(tf(7, 2), tf(7, 2), T.tf[:, 116:118], A.add, ["tf7", "tf7b"], ["tf7"])
+            cp(L(LE, 14), tf(10), ["tf10"], ["LE"])
+        elif step == 4:
+            ts(L(LH, 2), tf(7, 2), 32.0, A.add, ["tf7"], ["LH"], 447.0, A.min)
+            ts(T.cf[:, 11:12], col(8), 1.0, A.add, ["cf"], ["cf11"])
+
+    def seat_of_place(step):
+        if step == 0:
+            ts(T.pj[:, 0:24], T.pi[:], 3, A.arith_shift_right, ["pi"], ["pj0"], 1, A.bitwise_and)
+            ts(T.pj[:, 24:48], T.pi[:], 4, A.arith_shift_right, ["pi"], ["pj1"], 1, A.bitwise_and)
+        elif step == 1:
+            tt(T.pj[:, 48:72], T.pj[:, 0:24], T.pj[:, 24:48], A.subtract, ["pj0", "pj1"], ["pj2"])
+        elif step == 2:
+            ts(T.t2[:], T.pj[:, 48:72], 8.0, A.mult, ["pj2"], ["t2"])
+        elif step == 3:
+            tt(T.t2[:], T.t2[:], T.pi[:], A.add, ["t2", "pi"], ["t2"])
+        else:
+            cp(T.sp[:], T.t2[:], ["t2"], ["sp"])
+
+    def decode_mm(src, b, key):
+        mm(4 + b, "e", 128 * b, src, 0, C, True, True, ["qe%d" % b, key])
+
+    for r in range(R):
+        X, XN, XP = "x%d" % r, "n%d" % r, "p%d" % r
+        KX = ["q%s0" % X, "q%s1" % X] if r else ["qx0"]
+        mm(0, "us", 0, X, 0, C, True, True, ["qus", "sus"] + KX)
+        mm(1, "us", 0, X, 0, C, True, True, ["qus", "sus"] + KX)
+        mm(2, "us", 128, X, 0, C, True, True, ["qus", "sus"] + KX)
+        u8 = lambda nm: T[nm][:].bitcast(dt.uint8)
+        send([(prv, u8("q" + X), u8("q" + XN), "an%d" % r), (nxt, u8("q" + X), u8("q" + XP), "ap%d" % r)], KX)
+        send([(prv, T["s" + X][:], T["s" + XN][:], "an%d" % r), (nxt, T["s" + X][:], T["s" + XP][:], "ap%d" % r)], KX)
+        arrive("q" + XN, "an%d" % r, 16)
+        arrive("q" + XP, "ap%d" % r, 16)
+        if r == 0:
+            constants_g()
+        tt(T.y1[:], bank(0, C), T.cap[:], A.min, ["#0", "cap"], ["y1"])
+        act(T.ma[:], bank(2, C), F.Copy, ["#2"], ["ma"], scale=DS)
+        scan(T.fs[:], T.rho[:], T.y1[:], -BIG, A.min, A.max, ["rho", "y1"], ["fs"])
+        lane = lambda k, m: T.ct[:, 4 * TO[(24 - k) // 4] + (24 - k) % 4:4 * (TO[(24 - k) // 4] + m):4]
+        key = lambda k: "ct%d" % (24 - k)
+        for i, k in enumerate(KS):
+            act(T.sgn[:, C * i:C * i + 16 * k], bank(1, 16 * k), F.Sign, ["#1", "fs"], ["sg%d" % i], scale=-1.0, bias=T.fs[:, 16 * k + 15:16 * k + 16])
+        for i, k in enumerate(KS):
+            act(lane(k, 16 * k), T.sgn[:, C * i:C * i + 16 * k], F.Relu, ["sg%d" % i], [key(k), "rs%d" % k], accum_out=T.rsum[:, k:k + 1])
+
+        def cmp(k):
+            ts(lane(k, 16 * k), bank(0, 16 * k), T.fs[:, 16 * k + 15:16 * k + 16], A.is_lt, ["#0", "fs"], [key(k)])
+            act(T.junk[:, 8 * k * (k - 1):8 * k * (k + 1)], lane(k, 16 * k), F.Copy, [key(k)], ["rs%d" % k], accum_out=T.rsum[:, k:k + 1])
+
+        def tile(q):
+            qz("c", TO[q], TO[q] + TN[q], T.ct[:, 4 * TO[q]:4 * (TO[q] + TN[q])], ["ct%d" % (4 * q + i) for i in range(4)], ["qc%d" % q])
+
+        for k in range(20, 12, -1):
+            cmp(k)
+        tt(lane(24, C), T.fs[:], bank(0, C), A.is_ge, ["#0", "fs"], [key(24)])
+        tile(1)
+        for k in range(12, 8, -1):
+            cmp(k)
+        tile(2)
+        tile(0)
+        for k in range(8, 0, -1):
+            cmp(k)
+        tile(3)
+        tile(4)
+        tile(5)
+        for q in range(6):
+            mm(4, "s", 0, "c", TO[q], TN[q], q == 0, q == 5, ["qs0", "qc%d" % q])
+        mm(3, "us", 128, XN, 0, C, True, True, ["qus", "sus", "q" + XN])
+        scan(T.seg[:], T.mu[:], lane(24, C), 0.0, A.mult, A.add, ["mu", key(24)], ["seg"])
+        tt(T.y2[:], bank(4, C), T.cap[:], A.min, ["#4", "cap"], ["y2"])
+        tt(T.t1[:], T.c0[:], T.seg[:, 15:C:16], A.subtract, ["c0", "seg"], ["t1"])
+        scan(T.f2[:], T.rho[:], T.y2[:], -BIG, A.min, A.max, ["rho", "y2"], ["f2"])
+        tt(T.t1[:], T.t1[:], T.rsum[:], A.subtract, ["t1"] + ["rs%d" % k for k in range(24)], ["t1"])
+        tt(T.pi[:], T.t1[:], T.f2[:, 15:C:16], A.add, ["t1", "f2"], ["pi"])
+        OW, ON, HW, HP = "ow%d" % r, "on%d" % r, "hw%d" % r, "hp%d" % r
+        cp(T.pl[:], T.pi[:], ["pi"], ["pl"])
+        if r == 0:
+            constants_a()
+            dma("s", T.qw[:].bitcast(dt.uint8), T.wc[:], "dw", ["pl"], ["qw"])
+            dma("s", T.sw[:], T.ws[:], "dw2", (), ["sw"])
+            dma("s", T.vt[:], T.v[:], "dv", (), ["vt"])
+        cp(T.oS[:, 0:C].indirect(T.pl[:]), T.iof[:], ["iof", "pl"], ["oS"])
+        tt(T.y1[:], T.oS[:, 0:C].indirect(L(LSW, 24)), T.cap[:], A.min, ["oS", "LSW", "cap"], ["y1"])
+        scan(T.fs[:], T.rho[:], T.y1[:], -BIG, A.min, A.max, ["rho", "y1"], ["fs"])
+        cp(T[OW][:], T.fs[:, 15:C:16], ["fs"], [OW])
+        send([(prv, T[OW][:], T[ON][:], "al%d" % r)], [OW])
+        arrive(ON, "al%d" % r, 8)
+        if r:
+            act(T.tc[:], T.oS[:].indirect(L(LO0, 14)), F.Identity, ["oS", "oSx", "LO0", "cf10"], ["tc"], scale=col(10))
+            act(T.td[:], T.oS[:].indirect(L(LO1, 14)), F.Identity, ["oS", "oSx", "LO1", "cf"], ["td"], scale=col(4))
+        act(T.aS[:, 0:C], T.ma[:].indirect(T[OW][:]), F.Copy, ["ma", OW], ["aS"])
+        if r == 0:
+            lists_v()
+            act(T.mb[:], bank(3, C), F.Copy, ["#3"], ["mb"], scale=DS)
+        else:
+            seat_of_place(0)
+            tt(T.oa[:, 0:2 * W], T.tc[:], T.td[:], A.add, ["tc", "td"], ["oa"])
+            seat_of_place(1)
+        act(T.ta[:], T.aS[:].indirect(L(LA0, 14)), F.Identity, ["aS", "aSx", "LA0", "cf10"], ["ta"], scale=col(10))
+        act(T.tb[:], T.aS[:].indirect(L(LA1, 14)), F.Identity, ["aS", "aSx", "LA1", "cf"], ["tb"], scale=col(4))
+        if r == 0:
+            for q in range(4):
+                m = min(34, W - 34 * q)
+                act(T.kb[:, 34 * q:34 * q + m], T.ky[:, 0:m], F.Copy, ["ky0"], ["kb%d" % q])
+            act(T.kb1[:], T.kb[:], F.Identity, ["kb0", "kb1", "kb2", "kb3"], ["kbm"], bias=-B)
+            ms(T.oa[:, 2 * W:240], 0.0, ["oax"])
+        else:
+            act(T.mb[:], bank(3, C), F.Copy, ["#3"], ["mb"], scale=DS)
+            tt(T.dl[:], T.oa[:, 2:2 * W + 2], T.oa[:, 0:2 * W], A.subtract, ["oa", "oax"], ["dl"])
+            for i in (2, 3, 4):
+                seat_of_place(i)
+            tt(T.aa[:], T.ta[:], T.tb[:], A.add, ["ta", "tb"], ["aa"])
+            for b in range(4):
+                decode_mm(XP, b, "q" + XP)
+        tt(T.y2[:], T.mb[:].indirect(T[ON][:]), T.cap[:], A.min, ["mb", ON, "cap"], ["y2"])
+        if r == 0:
+            tt(T.aa[:], T.ta[:], T.tb[:], A.add, ["ta", "tb"], ["aa"])
+        scan(T.f2[:], T.rho[:], T.y2[:], -BIG, A.min, A.max, ["rho", "y2"], ["f2"])
+        tt(T.ee[:, 0:2 * W], T.f2[:].indirect(L(LBL, 14)), T.aa[:], A.subtract, ["f2", "LB", "aa"], ["eeL"])
+        tt(T.ee[:, 2 * W:4 * W], T.f2[:].indirect(L(LBU, 14)), T.aa[:], A.subtract, ["f2", "LB2", "aa"], ["eeU"])
+        for u, nm in ((0, "L"), (1, "U")):
+            for s in range(2):
+                act(T.dd[:, (2 * s + u) * W:(2 * s + u + 1) * W], T.ee[:, (2 * u + s) * W:(2 * u + s + 1) * W], F.Abs, ["ee" + nm], ["d%s%d" % (nm, s)])
+        if r == 0:
+            act(T.tc[:], T.oS[:].indirect(L(LO0, 14)), F.Identity, ["oS", "oSx", "LO0", "cf10"], ["tc"], scale=col(10))
+            act(T.td[:], T.oS[:].indirect(L(LO1, 14)), F.Identity, ["oS", "oSx", "LO1", "cf"], ["td"], scale=col(4))
+        act(T.ons[:], T.iof[:].indirect(T[ON][:]), F.Copy, ["iof", ON], ["ons"])
+
+        def zl(s, t):
+            return T["tt%d" % s][:, 8 + t:8 + 4 * W:4]
+
+        def head(w, s):
+            o, up = 2 * s * W, w >= 8
+            vL, dL = T.vv[:, o:o + W], T.dd[:, o:o + W]
+            XL, XU = "#%d" % (2 * s), "#%d" % (2 * s + 1)
+            if w == 0:
+                tt(vL, dL, T.kb[:], A.max, ["dL%d" % s, "kb0", "kb1", "kb2", "kb3"], ["vL%d" % s])
+            elif w == 1:
+                y = T.yy[:, s * W:(s + 1) * W]
+                tt(y, bank(2 * s, W), T.kb1[:], A.add, [XL, "kbm"], ["yy%d" % s])
+                act(zl(s, 1), y, F.Identity, ["yy%d" % s], ["t%dl1" % s], scale=1 / B, bias=-1.0)
+                tt(vL, y, dL, A.max, ["yy%d" % s, "dL%d" % s], ["vL%d" % s])
+            else:
+                tt(vL, bank(2 * s, W), dL, A.max, [XL, "dL%d" % s], ["vL%d" % s])
+                if w == SW - 1:
+                    act(zl(s, 1), dL, F.Copy, ["dL%d" % s], ["t%dl1" % s], scale=0.0)
+                else:
+                    act(zl(s, 1), bank(2 * s, W), F.Identity, [XL], ["t%dl1" % s], scale=1 / B, bias=-1.0)
+                    if w >= 7:
+                        act(zl(s, 3), bank(2 * s, W), F.Identity, [XL], ["t%dl3" % s], scale=1 / B, bias=7.0)
+                if up:
+                    tt(T.vv[:, o + W:o + 2 * W], bank(2 * s + 1, W), T.dd[:, o + W:o + 2 * W], A.max, [XU, "dU%d" % s], ["vU%d" % s])
+
+        def mid(w, s):
+            o, up = 2 * s * W, w >= 8
+            m = 2 * W if up else W
+            for nm in (("f",) if up else ("f", "w")):
+                for par in range(2):
+                    scan(T["f" + nm][:, o + par:o + m:2], T.rst[:, par:m:2], T.vv[:, o + par:o + m:2], 0.0, A.max, A.min,
+                         ["rst", "vL%d" % s] + (["vU%d" % s] if up else []), ["%s%d%d" % (nm, s, par)])
+
+        def ends(w, s):
+            if w >= 8:
+                for u in range(2):
+                    o = (2 * s + u) * W
+                    cp(T.fw[:, o + 32:o + 102], T.ff[:, o + 32:o + 102], ["f%d0" % s, "f%d1" % s], ["w%d%d" % (s, u), "w%d%d" % (s, 1 - u)] if u == 0 else ["wu%d" % s])
+
+        def flags(w, s):
+            o = 2 * s * W
+            for u in range(2 if w >= 8 else 1):
+                c = slice(o + u * W, o + (u + 1) * W)
+                tt(zl(s, 2 * u), T.fw[:, c].indirect(L(LM, 7)), T.ff[:, c], A.is_lt,
+                   ["f%d0" % s, "f%d1" % s, "LM"] + (["wu%d" % s] if u else ["w%d0" % s, "w%d1" % s]), ["t%dl%d" % (s, 2 * u)])
+
+        def tail(w, s):
+            nm = "t%d" % s
+            qz(nm, 0, 130, T["tt%d" % s][:], ["t%dl%d" % (s, t) for t in range(4)], ["q" + nm])
+            mm(2 * s, "s", 128, nm, 0, 128, True, False, ["qs1", "q" + nm])
+            mm(2 * s, "s", 256, nm, 2, 128, False, True, ["qs1", "q" + nm])
+            if w == SW - 1:
+                mm(2 * s + 1, "s", 512, nm, 2, 128, True, True, ["qs1", "q" + nm])
+            elif w >= 7:
+                mm(2 * s + 1, "s", 128, nm, 0, 128, True, False, ["qs1", "q" + nm])
+                mm(2 * s + 1, "s", 384, nm, 2, 128, False, True, ["qs1", "q" + nm])
+
+        def aside(w):
+            b = w % 4
+            k = "#%d" % (4 + b)
+            if w < 4:
+                act(T.gt[:, b:4 * C:4], bank(4 + b, C), F.Copy, [k], ["gt%d" % b], scale=1 / 32)
+                decode_mm(XN, b, "q" + XN)
+            elif w < 8:
+                act(T.dn[:, b * C:(b + 1) * C], bank(4 + b, C), F.Copy, [k], ["dn%d" % b], scale=1 / 32)
+                if w == 5:
+                    qz("g", 0, C, T.gt[:], ["gt%d" % i for i in range(4)], ["qg"])
+                if w == 6:
+                    decode_mm("g", 0, "qg")
+                    decode_mm("g", 1, "qg")
+                if w == 7:
+                    decode_mm("g", 2, "qg")
+            else:
+                if w == 8:
+                    decode_mm("g", 3, "qg")
+                act(T.dp[:, b * C:(b + 1) * C], bank(4 + b, C), F.Copy, [k], ["dp%d" % b], scale=1 / 32)
+
+        def extras(w):
+            if w < 4:
+                qz("e", 128 * w, 128 * w + 128, T.et[:, 3 - w:515 - w], ["et"], ["qe%d" % w])
+                decode_mm(XP, w, "q" + XP)
+            if w == 2:
+                ms(T.fw[:, W:W + 32], 0.0, ["wu0"])
+                ms(T.fw[:, W + 102:2 * W], 0.0, ["wu0"])
+            if w == 3:
+                ms(T.fw[:, 3 * W:3 * W + 32], 0.0, ["wu1"])
+                ms(T.fw[:, 3 * W + 102:4 * W], 0.0, ["wu1"])
+            if w == 4:
+                tt(T.oa[:, 0:2 * W], T.tc[:], T.td[:], A.add, ["tc", "td"], ["oa"])
+            if w == 6:
+                tt(T.dl[:], T.oa[:, 2:2 * W + 2], T.oa[:, 0:2 * W], A.subtract, ["oa", "oax"], ["dl"])
+            if 2 <= w < 7:
+                late_lists(w - 2)
+            if 3 <= w < 8:
+                seat_of_place(w - 3)
+
+        head(0, 0)
+        mid(0, 0)
+        for w in range(SW):
+            head(w, 1)
+            ends(w, 0)
+            if w >= 8:
+                mid(w, 1)
+                flags(w, 0)
+                ends(w, 1)
+            else:
+                flags(w, 0)
+                mid(w, 1)
+            tail(w, 0)
+            flags(w, 1)
+            if r == 0:
+                extras(w)
+            tail(w, 1)
+            if w + 1 < SW:
+                aside(w)
+                head(w + 1, 0)
+                mid(w + 1, 0)
+
+        sl = lambda nm, s: T[nm][:, s * W:(s + 1) * W]
+        for s in range(2):
+            ts(sl("rr", s), bank(2 * s, W), -1 / B, A.mult, ["#%d" % (2 * s)], ["rr%d" % s], 1.0, A.add)
+            act(sl("ep", s), bank(2 * s + 1, W), F.Identity, ["#%d" % (2 * s + 1), "cf11"], ["ep%d" % s], scale=-1.0, bias=col(11))
+            if s == 0:
+                tt(sl("pr", 0), zl(0, 0), sl("dl", 0), A.mult, ["t0l0", "dl"], ["prL0"])
+        aside(SW - 1)
+        for par in range(2):
+            scan(T.ro[:, par:2 * W:2], T.rr[:, par:2 * W:2], T.mw[:, par:2 * W:2], 0.0, A.add, A.mult, ["rr0", "rr1", "mw0", "mw1"], ["ro%d" % par])
+        tt(sl("pr", 2), zl(1, 0), sl("dl", 1), A.mult, ["t1l0", "dl"], ["prL1"])
+        tt(T.g2[:], T.ep[:].indirect(L(LE, 14)), T.ro[:], A.is_gt, ["ep0", "ep1", "LE", "ro0", "ro1"], ["g2"])
+        for s in range(2):
+            tt(sl("gu", s), sl("g2", s), zl(s, 2), A.add, ["g2", "t%dl2" % s], ["gu%d" % s])
+        for s in range(2):
+            tt(sl("pr", 2 * s + 1), sl("gu", s), sl("dl", s), A.mult, ["gu%d" % s, "dl"], ["prU%d" % s])
+        for s in range(2):
+            o = 2 * s * W
+            for par in range(2):
+                scan(T.hs[:, o + par:o + 2 * W:2], T.mw[:, par:2 * W:2], T.pr[:, o + par:o + 2 * W:2], 0.0, A.mult, A.add,
+                     ["mw0", "mw1", "prL%d" % s, "prU%d" % s], ["hs%d%d" % (s, par)])
+        cp(T[HW][:], T.hs[:].indirect(L(LH, 2)), ["hs00", "hs01", "hs10", "hs11", "LH"], [HW])
+        send([(nxt, T[HW][:, 0:24], T[HP][:], "ah%d" % r)], [HW])
+        arrive(HP, "ah%d" % r, 8)
+        bk = lambda h, b: (4 + b, b)[h]
+        for h in range(2):
+            for b in range(4):
+                mm(bk(h, b), "e", 128 * b, X, H * h, H, True, False, ["qe%d" % b] + KX)
+        cp(T.wr[:].indirect(T[HW][:, 0:24]), T.ons[:], ["ons", HW], ["wr"])
+        act(T.hr[:], T.iof[:].indirect(T[HP][:]), F.Copy, ["iof", HP], ["hr"])
+        if r + 1 < R:
+            for s in range(2):
+                ms(zl(s, 2), 0.0, ["t%dl2" % s])
+        else:
+            qz("v", 0, 128, T.vt[:], ["vt"], ["qv"])
+            dma("s", T.ol[:], T.wr[0:128:16, :], "out_s", ["wr"], ())
+        tt(T.y2[:], T.wr[:], T.cap[:], A.min, ["wr", "cap"], ["y2"])
+        scan(T.f2[:], T.rho[:], T.y2[:], -BIG, A.min, A.max, ["rho", "y2"], ["f2"])
+        cp(T.wl[:], T.f2[:, 15:C:16], ["f2"], ["wl"])
+        for h in range(2):
+            for b in range(4):
+                act(T.vg[:, b * C + H * h:b * C + H * h + H], T.dn[:, b * C:(b + 1) * C].indirect(T.wl[:, 12 * h:12 * h + 12]), F.Copy,
+                    ["dn%d" % b, "wl"], ["vg%d%d" % (h, b)])
+        tt(T.y1[:], T.hr[:].indirect(T.sp[:]), T.cap[:], A.min, ["hr", "sp", "cap"], ["y1"])
+        scan(T.fs[:], T.rho[:], T.y1[:], -BIG, A.min, A.max, ["rho", "y1"], ["fs"])
+        cp(T.hl[:], T.fs[:, 15:C:16], ["fs"], ["hl"])
+        XO = "x%d" % (r + 1)
+
+        def z_half(h, bs):
+            for b in bs:
+                tt(T.zt[:, 4 * H * h + b:4 * H * (h + 1):4], T.dp[:, b * C:(b + 1) * C].indirect(T.hl[:, 12 * h:12 * h + 12]),
+                   T.vg[:, b * C + H * h:b * C + H * h + H], A.max, ["dp%d" % b, "hl", "vg%d%d" % (h, b)], ["zt%d%d" % (h, b)])
+
+        def w_half(h):
+            qz("z", H * h, H * h + H, T.zt[:, 4 * H * h:4 * H * (h + 1)], ["zt%d%d" % (h, b) for b in range(4)], ["qz%d" % h])
+            for b in range(4):
+                mm(bk(h, b), "w", 128 * b, "z", H * h, H, False, True, ["qw", "sw", "qz%d" % h])
+            for b in range(4):
+                out, k = T.xn[:, 4 * H * h + b:4 * H * (h + 1):4], "#%d" % bk(h, b)
+                if h == 0 or b % 2:
+                    act(out, bank(bk(h, b), H), F.Copy, [k], ["xn%d%d" % (h, b)], scale=0.03125)
+
+        def x_half(h):
+            qz(XO, H * h, H * h + H, T.xn[:, 4 * H * h:4 * H * (h + 1)], ["xn%d%d" % (h, b) for b in range(4)], ["q%s%d" % (XO, h)])
+
+        z_half(0, range(4))
+        z_half(1, [0])
+        w_half(0)
+        z_half(1, [1, 2, 3])
+        w_half(1)
+        x_half(0)
+        for b in (0, 2):
+            ts(T.xn[:, 4 * H + b:8 * H:4], bank(b, H), 0.03125, A.mult, ["#%d" % b], ["xn1%d" % b])
+        x_half(1)
+
+    for h in range(2):
+        mm(4 + h, "v", 0, "x2", H * h, H, True, True, ["qv", "qx2%d" % h])
+    dma("s", T.oc[:], T.qx2[:].bitcast(dt.uint8), "out_s", ["qx20", "qx21"], ())
+    act(T.yo[:, 0:H], bank(4, H), F.Copy, ["#4"], ["yo0"])
+    cp(T.yo[:, H:C], bank(5, H), ["#5"], ["yo1"])
+    dma("a", T.y[:], T.yo[:], "out_a", ["yo0", "yo1"], ())
+    for k in range(4):
+        dma("a" if k % 2 else "s", T.osc[4 * k:4 * k + 4, :], T.sx2[32 * k:32 * k + 4, :], "out_a" if k % 2 else "out_s", ["qx20", "qx21"], ())
+
+    chan = lambda i: ops[i][3] if ops[i][3] else "e" + ops[i][0]
+    known = {e: {} for e in ENG}
+    snap, waits, needed = {}, {}, set()
+    for i, (eng, fn, deps, sem, cnt) in enumerate(ops):
+        if eng == "x":
+            snap[i] = {}
+            continue
+        kn, w = known[eng], []
+        for d in sorted(deps, reverse=True):
+            if kn.get(chan(d), -1) >= d:
+                continue
+            w.append(d)
+            needed.add(d)
+            kn[chan(d)] = d
+            for c, val in snap[d].items():
+                if kn.get(c, -1) < val:
+                    kn[c] = val
+        waits[i], snap[i] = w, dict(kn)
+    total, value = {}, {}
+    for i, (eng, fn, deps, sem, cnt) in enumerate(ops):
+        c = chan(i)
+        if eng == "x":
+            total[c] = value[i] = cnt
+            continue
+        for d in waits[i]:
+            Q[eng].wait_ge(T.sem[chan(d)], value[d])
+        ins = fn()
+        if sem == "-":
+            continue
+        if sem or i in needed:
+            k = cnt or 1
+            ins.then_inc(T.sem[c], k)
+            total[c] = value[i] = total.get(c, 0) + k
+    total["sent"] = sent[0]
+    for c in sorted(total, key=lambda c: c.startswith("out")):
+        g.wait_ge(T.sem[c], total[c])

@@ -14,7 +14,7 @@ BIG = 2.0 ** 90
 TN = [384, 320, 256, 192, 128, 128]
 TO = [0, 384, 704, 960, 1152, 1280]
 KS = (23, 22, 21)
-LU, LM, LE, LA0, LA1, LBL, LBU, LSW, LH, LO0, LO1 = 0, 16, 142, 32, 46, 60, 74, 88, 112, 114, 128
+LU, LM, LE, LA0, LA1, LBL, LBU, LSW, LH, LO0, LO1 = 0, 16, 24, 32, 46, 60, 74, 88, 112, 114, 128
 
 Q4, U8, F32, BF, I32, U16 = "float8_e4m3fn_x4", "uint8", "float32", "bfloat16", "int32", "uint16"
 SCRATCH = {"ps": ("psum", [128, 4096], F32)}
@@ -152,6 +152,41 @@ def rank_program(g, core, T, topo):
     col = lambda i: T.cf[:, i:i + 1]
     lane_of = lambda k, t: T.st[:, 512 * k + t:512 * (k + 1):4]
     tf = lambda i, k=14: T.tf[:, 16 * i:16 * i + k]
+    hc = lambda h: slice(H * h, H * h + H)
+
+    def own_mask(y, h, src, rd):
+        tt(T[y][:, hc(h)], src, T.cap[:, hc(h)], A.min, rd + ["cap"], [y + "h%d" % h])
+
+    def own_scan(y, f, h):
+        scan(T[f][:, hc(h)], T.rho[:, hc(h)], T[y][:, hc(h)], -BIG, A.min, A.max, ["rho", y + "h%d" % h], [f + "h%d" % h])
+
+    def own(y, f, src, rd, between=None):
+        for h in range(2):
+            own_mask(y, h, src(h), rd)
+        if between:
+            between()
+        for h in range(2):
+            own_scan(y, f, h)
+
+    def as_list(out, f, key):
+        for h in range(2):
+            cp(T[out][:, 12 * h:12 * h + 12], T[f][:, H * h + 15:H * h + H:16], [f + "h%d" % h], [key + "h%d" % h])
+
+    both = lambda k: [k + "h0", k + "h1"]
+
+    lane = lambda k, m: T.ct[:, 4 * TO[(24 - k) // 4] + (24 - k) % 4:4 * (TO[(24 - k) // 4] + m):4]
+    key = lambda k: "ct%d" % (24 - k)
+
+    def cmp(k):
+        b = 0 if k >= 12 else 5
+        ts(lane(k, 16 * k), bank(b, 16 * k), T.fs[:, 16 * k + 15:16 * k + 16], A.is_lt, ["#%d" % b, "fsh%d" % (k // 12)], [key(k)])
+        act(T.junk[:, 8 * k * (k - 1):8 * k * (k + 1)], lane(k, 16 * k), F.Copy, [key(k)], ["rs%d" % k], accum_out=T.rsum[:, k:k + 1])
+
+    def tile(q):
+        qz("c", TO[q], TO[q] + TN[q], T.ct[:, 4 * TO[q]:4 * (TO[q] + TN[q])], ["ct%d" % (4 * q + i) for i in range(4)], ["qc%d" % q])
+
+    def half_scores(x):
+        mm(5, "us", 0, x, 0, H, True, True, ["qus", "sus", "q%s0" % x])
 
     dma("s", T.xt[:, 0:768], T.x[:, 0:768], "dx", (), ["xt0"])
     dma("a", T.ut[:], T.u[:], "du", (), ["ut"])
@@ -173,7 +208,7 @@ def rank_program(g, core, T, topo):
     cp(L(LU, 16), T.ti[:, 0:16], ["ti0"], ["LU"])
     cp(T.cf[:, 0:9], T.ci[:, 0:9], ["ci%d" % i for i in range(9)], ["cf"])
     ts(T.mu[:], T.ii[:], 0.0, A.is_gt, ["ii"], ["mu"])
-    ts(T.y2[:], T.ii[:], col(1), A.is_equal, ["ii", "cf"], ["y2"], 2 * BIG, A.mult)
+    ts(T.y2[:], T.ii[:], col(1), A.is_equal, ["ii", "cf"], both("y2"), 2 * BIG, A.mult)
     ts(T.b16[:], T.jm[:], col(2), A.is_equal, ["jm", "cf"], ["b16"])
     ms(T.rsum[:, 0:1], 0.0, ["rs0"])
     ts(T.c0[:], T.c0[:], col(1), A.subtract, ["c0", "cf"], ["c0"])
@@ -184,15 +219,18 @@ def rank_program(g, core, T, topo):
     ms(T.tt0[:], 0.0, ["t0l0", "t0l1", "t0l2", "t0l3"])
     ms(T.tt1[:], 0.0, ["t1l0", "t1l1", "t1l2", "t1l3"])
     act(T.rho[:], T.mu[:], F.Identity, ["mu"], ["rho"], scale=2 * BIG, bias=-BIG)
-    act(T.cap[:], T.y2[:], F.Identity, ["y2"], ["cap"], bias=-BIG)
-    for t in range(4):
-        act(lane_of(0, t), T.b16[:], F.Copy, ["b16"], ["st0%d" % t])
+    act(T.cap[:], T.y2[:], F.Identity, both("y2"), ["cap"], bias=-BIG)
     qz("u", 0, 128, T.ut[:], ["ut"], ["qu"])
+    qz("x0", 0, H, T.xt[:, 0:768], ["xt0"], ["qx00"])
     cp(T.qus[:].bitcast(dt.uint32), T.qu[:].bitcast(dt.uint32).indirect(L(LU, 16)), ["qu", "LU"], ["qus"])
     act(T.sus[:], T.su[:].indirect(L(LU, 16)), F.Copy, ["qu", "LU"], ["sus"])
-    qz("x0", 0, C, T.xt[:], ["xt0", "xt1"], ["qx0"])
+    for t in range(4):
+        act(lane_of(0, t), T.b16[:], F.Copy, ["b16"], ["st0%d" % t])
+    half_scores("x0")
+    qz("x0", H, C, T.xt[:, 768:1536], ["xt1"], ["qx01"])
     for k, t in ((1, 1), (1, 3), (2, 1), (2, 3), (3, 1), (3, 3), (4, 0), (4, 1), (4, 3)):
         act(lane_of(k, t), T.b16[:], F.Copy, ["b16"], ["st%d%d" % (k, t)], scale=0.0)
+    own_mask("y1", 0, bank(5, H), ["#5"])
     qz("s", 0, 128, T.st[:, 0:512], ["st0%d" % t for t in range(4)], ["qs0"])
 
     def constants_g():
@@ -219,41 +257,46 @@ def rank_program(g, core, T, topo):
         ts(tf(0), tf(0), col(1), A.add, ["tf0", "cf"], ["tf0"])
         ts(T.cf[:, 13:14], col(5), 32.0, A.mult, ["cf"], ["cf13"])
         ts(T.cf[:, 10:11], col(4), -1.0, A.mult, ["cf"], ["cf10"], 1.0, A.add)
+        ts(T.kx[:, 0:34], T.lr[:], 1, A.arith_shift_right, ["lr"], ["kx0"], 1, A.bitwise_and)
+        ts(T.kx[:, 36:70], T.lr[:], 2, A.arith_shift_right, ["lr"], ["kx1"], 1, A.bitwise_and)
         ts(tf(10), tf(0), 112.0, A.is_ge, ["tf0"], ["tf10"], -112.0, A.mult)
         ts(tf(2), tf(0), 112.0, A.is_ge, ["tf0"], ["tf2"], 192.0, A.mult)
+        ts(T.kx[:, 72:106], T.lr[:], 3, A.arith_shift_right, ["lr"], ["kx2"], 1, A.bitwise_and)
         ms(T.aS[:, C:416], 2 * B, ["aSx"])
+        ms(T.oS[:, C:416], 0.0, ["oSx"])
         tt(tf(1), tf(10), tf(0), A.add, ["tf10", "tf0"], ["tf1"])
         ts(tf(2), tf(2), col(13), A.add, ["tf2", "cf13"], ["tf2"])
-        ms(T.oS[:, C:416], 0.0, ["oSx"])
+        for b in range(3):
+            ts(T.ky[:, 36 * b:36 * b + 34], T.kx[:, 36 * b:36 * b + 34], col(5 + b), A.not_equal, ["kx%d" % b, "cf"], ["ky%d" % b], B * 2 ** b, A.mult)
         ts(tf(3), tf(1), 34.0, A.is_ge, ["tf1"], ["tf3"])
         ts(tf(4), tf(1), 68.0, A.is_ge, ["tf1"], ["tf4"])
-        ts(T.kx[:, 0:34], T.lr[:], 1, A.arith_shift_right, ["lr"], ["kx0"], 1, A.bitwise_and)
+        ms(T.oa[:, 2 * W:240], 0.0, ["oax"])
+        tt(T.ky[:, 0:34], T.ky[:, 0:34], T.ky[:, 36:70], A.add, ["ky0", "ky1"], ["ky0"])
+        qz("e", 0, 128, T.et[:, 3:515], ["et"], ["qe0"])
         tt(tf(3), tf(3), tf(4), A.add, ["tf3", "tf4"], ["tf3"])
-        ts(T.kx[:, 36:70], T.lr[:], 2, A.arith_shift_right, ["lr"], ["kx1"], 1, A.bitwise_and)
+        qz("s", 128, 384, T.st[:, 512:1536], ["st%d%d" % (k, t) for k in (1, 2) for t in range(4)], ["qs1"])
         ts(tf(4), tf(3), 34.0, A.mult, ["tf3", "cf"], ["tf4"], col(5), A.add)
         ts(tf(5), tf(3), 64.0, A.mult, ["tf3"], ["tf5"])
-        ts(T.kx[:, 72:106], T.lr[:], 3, A.arith_shift_right, ["lr"], ["kx2"], 1, A.bitwise_and)
+        tt(T.ky[:, 0:34], T.ky[:, 0:34], T.ky[:, 72:106], A.add, ["ky0", "ky2"], ["ky0"])
+        qz("e", 128, 256, T.et[:, 2:514], ["et"], ["qe1"])
         tt(tf(6), tf(1), tf(4), A.subtract, ["tf1", "tf4"], ["tf6"])
         tt(tf(5), tf(5), tf(2), A.add, ["tf5", "tf2"], ["tf5"])
-        for b in range(2):
-            ts(T.ky[:, 36 * b:36 * b + 34], T.kx[:, 36 * b:36 * b + 34], col(5 + b), A.not_equal, ["kx%d" % b, "cf"], ["ky%d" % b], B * 2 ** b, A.mult)
+        ts(L(LM, 7), tf(4, 7), 32.0, A.add, ["tf4"], ["LM"])
+        cp(L(LE, 7), tf(4, 7), ["tf4"], ["LE"])
         ts(tf(1), tf(6), 0.0, A.is_equal, ["tf6"], ["tf1"], 384.0, A.mult)
         ts(tf(2), tf(6), 0.5, A.mult, ["tf6"], ["tf2"], -1.0, A.add)
         ts(tf(3), tf(6), 18.0, A.is_ge, ["tf6"], ["tf3"], 8.0, A.mult)
-        ts(T.ky[:, 72:106], T.kx[:, 72:106], col(7), A.not_equal, ["kx2", "cf"], ["ky2"], B * 4, A.mult)
-        tt(tf(2), tf(2), tf(5), A.add, ["tf2", "tf5"], ["tf2"])
-        tt(T.ky[:, 0:34], T.ky[:, 0:34], T.ky[:, 36:70], A.add, ["ky0", "ky1"], ["ky0"])
         ts(L(LBL, 14), tf(5), 15.0, A.add, ["tf5"], ["LB"])
-        tt(tf(2), tf(2), tf(1), A.max, ["tf2", "tf1"], ["tf2"])
-        tt(T.ky[:, 0:34], T.ky[:, 0:34], T.ky[:, 72:106], A.add, ["ky0", "ky2"], ["ky0"])
         ts(L(LBU, 14), tf(5), 31.0, A.add, ["tf5"], ["LB2"])
+        tt(tf(2), tf(2), tf(5), A.add, ["tf2", "tf5"], ["tf2"])
+        qz("e", 256, 384, T.et[:, 1:513], ["et"], ["qe2"])
+        tt(tf(2), tf(2), tf(1), A.max, ["tf2", "tf1"], ["tf2"])
+        qz("e", 384, 512, T.et[:, 0:512], ["et"], ["qe3"])
         tt(tf(3), tf(3), tf(2), A.add, ["tf3", "tf2"], ["tf3"])
         cp(L(LO0, 14), tf(2), ["tf2"], ["LO0"])
         ts(L(LO1, 14), tf(2), 16.0, A.add, ["tf2"], ["LO1"])
         cp(L(LA0, 14), tf(3), ["tf3"], ["LA0"])
         ts(L(LA1, 14), tf(3), 8.0, A.add, ["tf3"], ["LA1"])
-        ts(L(LM, 7), tf(4, 7), 32.0, A.add, ["tf4"], ["LM"])
-        qz("s", 128, 640, T.st[:, 512:2560], ["st%d%d" % (k, t) for k in range(1, 5) for t in range(4)], ["qs1"])
 
     def late_lists(step):
         if step == 0:
@@ -264,10 +307,8 @@ def rank_program(g, core, T, topo):
             ts(T.ti[:, 18:20], T.ti[:, 16:18], 2, A.arith_shift_right, ["ti1"], ["ti2"])
         elif step == 2:
             ts(T.tf[:, 116:118], T.ti[:, 18:20], 34.0, A.mult, ["ti2", "cf14"], ["tf7b"], col(14), A.add)
-            tt(tf(10), tf(4), tf(10), A.subtract, ["tf4", "tf10"], ["tf10"])
         elif step == 3:
             tt(tf(7, 2), tf(7, 2), T.tf[:, 116:118], A.add, ["tf7", "tf7b"], ["tf7"])
-            cp(L(LE, 14), tf(10), ["tf10"], ["LE"])
         elif step == 4:
             ts(L(LH, 2), tf(7, 2), 32.0, A.add, ["tf7"], ["LH"], 447.0, A.min)
             ts(T.cf[:, 11:12], col(8), 1.0, A.add, ["cf"], ["cf11"])
@@ -285,12 +326,12 @@ def rank_program(g, core, T, topo):
         else:
             cp(T.sp[:], T.t2[:], ["t2"], ["sp"])
 
-    def decode_mm(src, b, key):
-        mm(4 + b, "e", 128 * b, src, 0, C, True, True, ["qe%d" % b, key])
+    def decode_mm(src, b, k):
+        mm(4 + b, "e", 128 * b, src, 0, C, True, True, ["qe%d" % b, k])
 
     for r in range(R):
         X, XN, XP = "x%d" % r, "n%d" % r, "p%d" % r
-        KX = ["q%s0" % X, "q%s1" % X] if r else ["qx0"]
+        KX = ["q%s0" % X, "q%s1" % X]
         mm(0, "us", 0, X, 0, C, True, True, ["qus", "sus"] + KX)
         mm(1, "us", 0, X, 0, C, True, True, ["qus", "sus"] + KX)
         mm(2, "us", 128, X, 0, C, True, True, ["qus", "sus"] + KX)
@@ -301,95 +342,82 @@ def rank_program(g, core, T, topo):
         arrive("q" + XP, "ap%d" % r, 16)
         if r == 0:
             constants_g()
-        tt(T.y1[:], bank(0, C), T.cap[:], A.min, ["#0", "cap"], ["y1"])
-        act(T.ma[:], bank(2, C), F.Copy, ["#2"], ["ma"], scale=DS)
-        scan(T.fs[:], T.rho[:], T.y1[:], -BIG, A.min, A.max, ["rho", "y1"], ["fs"])
-        lane = lambda k, m: T.ct[:, 4 * TO[(24 - k) // 4] + (24 - k) % 4:4 * (TO[(24 - k) // 4] + m):4]
-        key = lambda k: "ct%d" % (24 - k)
+        own_scan("y1", "fs", 0)
+        for k in (11, 10, 9, 8):
+            cmp(k)
+        own_mask("y1", 1, T.ps[:, hc(1)], ["#0"])
+        for k in (7, 6, 5):
+            cmp(k)
+        own_scan("y1", "fs", 1)
+        for k in (4, 3, 2, 1):
+            cmp(k)
         for i, k in enumerate(KS):
-            act(T.sgn[:, C * i:C * i + 16 * k], bank(1, 16 * k), F.Sign, ["#1", "fs"], ["sg%d" % i], scale=-1.0, bias=T.fs[:, 16 * k + 15:16 * k + 16])
+            act(T.sgn[:, C * i:C * i + 16 * k], bank(1, 16 * k), F.Sign, ["#1", "fsh1"], ["sg%d" % i], scale=-1.0, bias=T.fs[:, 16 * k + 15:16 * k + 16])
         for i, k in enumerate(KS):
             act(lane(k, 16 * k), T.sgn[:, C * i:C * i + 16 * k], F.Relu, ["sg%d" % i], [key(k), "rs%d" % k], accum_out=T.rsum[:, k:k + 1])
-
-        def cmp(k):
-            ts(lane(k, 16 * k), bank(0, 16 * k), T.fs[:, 16 * k + 15:16 * k + 16], A.is_lt, ["#0", "fs"], [key(k)])
-            act(T.junk[:, 8 * k * (k - 1):8 * k * (k + 1)], lane(k, 16 * k), F.Copy, [key(k)], ["rs%d" % k], accum_out=T.rsum[:, k:k + 1])
-
-        def tile(q):
-            qz("c", TO[q], TO[q] + TN[q], T.ct[:, 4 * TO[q]:4 * (TO[q] + TN[q])], ["ct%d" % (4 * q + i) for i in range(4)], ["qc%d" % q])
-
-        for k in range(20, 12, -1):
+        for k in range(20, 11, -1):
             cmp(k)
-        tt(lane(24, C), T.fs[:], bank(0, C), A.is_ge, ["#0", "fs"], [key(24)])
-        tile(1)
-        for k in range(12, 8, -1):
-            cmp(k)
-        tile(2)
-        tile(0)
-        for k in range(8, 0, -1):
-            cmp(k)
-        tile(3)
-        tile(4)
-        tile(5)
+        tt(lane(24, C), T.fs[:], bank(0, C), A.is_ge, ["#0"] + both("fs"), [key(24)])
+        for q in (1, 0, 2, 3, 4, 5):
+            tile(q)
         for q in range(6):
             mm(4, "s", 0, "c", TO[q], TN[q], q == 0, q == 5, ["qs0", "qc%d" % q])
         mm(3, "us", 128, XN, 0, C, True, True, ["qus", "sus", "q" + XN])
         scan(T.seg[:], T.mu[:], lane(24, C), 0.0, A.mult, A.add, ["mu", key(24)], ["seg"])
-        tt(T.y2[:], bank(4, C), T.cap[:], A.min, ["#4", "cap"], ["y2"])
-        tt(T.t1[:], T.c0[:], T.seg[:, 15:C:16], A.subtract, ["c0", "seg"], ["t1"])
-        scan(T.f2[:], T.rho[:], T.y2[:], -BIG, A.min, A.max, ["rho", "y2"], ["f2"])
+        act(T.ma[:], bank(2, C), F.Copy, ["#2"], ["ma"], scale=DS)
+        own("y2", "f2", lambda h: T.ps[:, 2048 + H * h:2048 + H * h + H], ["#4"],
+            between=lambda: tt(T.t1[:], T.c0[:], T.seg[:, 15:C:16], A.subtract, ["c0", "seg"], ["t1"]))
         tt(T.t1[:], T.t1[:], T.rsum[:], A.subtract, ["t1"] + ["rs%d" % k for k in range(24)], ["t1"])
-        tt(T.pi[:], T.t1[:], T.f2[:, 15:C:16], A.add, ["t1", "f2"], ["pi"])
+        tt(T.pi[:], T.t1[:], T.f2[:, 15:C:16], A.add, ["t1"] + both("f2"), ["pi"])
         OW, ON, HW, HP = "ow%d" % r, "on%d" % r, "hw%d" % r, "hp%d" % r
         cp(T.pl[:], T.pi[:], ["pi"], ["pl"])
+        seat_of_place(0)
         if r == 0:
             constants_a()
             dma("s", T.qw[:].bitcast(dt.uint8), T.wc[:], "dw", ["pl"], ["qw"])
             dma("s", T.sw[:], T.ws[:], "dw2", (), ["sw"])
             dma("s", T.vt[:], T.v[:], "dv", (), ["vt"])
         cp(T.oS[:, 0:C].indirect(T.pl[:]), T.iof[:], ["iof", "pl"], ["oS"])
-        tt(T.y1[:], T.oS[:, 0:C].indirect(L(LSW, 24)), T.cap[:], A.min, ["oS", "LSW", "cap"], ["y1"])
-        scan(T.fs[:], T.rho[:], T.y1[:], -BIG, A.min, A.max, ["rho", "y1"], ["fs"])
-        cp(T[OW][:], T.fs[:, 15:C:16], ["fs"], [OW])
-        send([(prv, T[OW][:], T[ON][:], "al%d" % r)], [OW])
+        seat_of_place(1)
+        own("y1", "fs", lambda h: T.oS[:, 0:C].indirect(L(LSW + 12 * h, 12)), ["oS", "LSW"])
+        as_list(OW, "fs", OW)
+        send([(prv, T[OW][:], T[ON][:], "al%d" % r)], both(OW))
         arrive(ON, "al%d" % r, 8)
         if r:
             act(T.tc[:], T.oS[:].indirect(L(LO0, 14)), F.Identity, ["oS", "oSx", "LO0", "cf10"], ["tc"], scale=col(10))
             act(T.td[:], T.oS[:].indirect(L(LO1, 14)), F.Identity, ["oS", "oSx", "LO1", "cf"], ["td"], scale=col(4))
-        act(T.aS[:, 0:C], T.ma[:].indirect(T[OW][:]), F.Copy, ["ma", OW], ["aS"])
+        act(T.aS[:, 0:C], T.ma[:].indirect(T[OW][:]), F.Copy, ["ma"] + both(OW), ["aS"])
+        seat_of_place(2)
         if r == 0:
             lists_v()
             act(T.mb[:], bank(3, C), F.Copy, ["#3"], ["mb"], scale=DS)
-        else:
-            seat_of_place(0)
-            tt(T.oa[:, 0:2 * W], T.tc[:], T.td[:], A.add, ["tc", "td"], ["oa"])
-            seat_of_place(1)
-        act(T.ta[:], T.aS[:].indirect(L(LA0, 14)), F.Identity, ["aS", "aSx", "LA0", "cf10"], ["ta"], scale=col(10))
-        act(T.tb[:], T.aS[:].indirect(L(LA1, 14)), F.Identity, ["aS", "aSx", "LA1", "cf"], ["tb"], scale=col(4))
-        if r == 0:
             for q in range(4):
                 m = min(34, W - 34 * q)
                 act(T.kb[:, 34 * q:34 * q + m], T.ky[:, 0:m], F.Copy, ["ky0"], ["kb%d" % q])
-            act(T.kb1[:], T.kb[:], F.Identity, ["kb0", "kb1", "kb2", "kb3"], ["kbm"], bias=-B)
-            ms(T.oa[:, 2 * W:240], 0.0, ["oax"])
         else:
+            tt(T.oa[:, 0:2 * W], T.tc[:], T.td[:], A.add, ["tc", "td"], ["oa"])
             act(T.mb[:], bank(3, C), F.Copy, ["#3"], ["mb"], scale=DS)
+        act(T.ta[:], T.aS[:].indirect(L(LA0, 14)), F.Identity, ["aS", "aSx", "LA0", "cf10"], ["ta"], scale=col(10))
+        act(T.tb[:], T.aS[:].indirect(L(LA1, 14)), F.Identity, ["aS", "aSx", "LA1", "cf"], ["tb"], scale=col(4))
+        seat_of_place(3)
+        if r == 0:
+            act(T.kb1[:], T.kb[:], F.Identity, ["kb0", "kb1", "kb2", "kb3"], ["kbm"], bias=-B)
+        else:
             tt(T.dl[:], T.oa[:, 2:2 * W + 2], T.oa[:, 0:2 * W], A.subtract, ["oa", "oax"], ["dl"])
-            for i in (2, 3, 4):
-                seat_of_place(i)
+            seat_of_place(4)
             tt(T.aa[:], T.ta[:], T.tb[:], A.add, ["ta", "tb"], ["aa"])
-            for b in range(4):
-                decode_mm(XP, b, "q" + XP)
-        tt(T.y2[:], T.mb[:].indirect(T[ON][:]), T.cap[:], A.min, ["mb", ON, "cap"], ["y2"])
+        for b in range(4):
+            decode_mm(XP, b, "q" + XP)
+        own("y2", "f2", lambda h: T.mb[:].indirect(T[ON][:, 12 * h:12 * h + 12]), ["mb", ON])
         if r == 0:
             tt(T.aa[:], T.ta[:], T.tb[:], A.add, ["ta", "tb"], ["aa"])
-        scan(T.f2[:], T.rho[:], T.y2[:], -BIG, A.min, A.max, ["rho", "y2"], ["f2"])
-        tt(T.ee[:, 0:2 * W], T.f2[:].indirect(L(LBL, 14)), T.aa[:], A.subtract, ["f2", "LB", "aa"], ["eeL"])
-        tt(T.ee[:, 2 * W:4 * W], T.f2[:].indirect(L(LBU, 14)), T.aa[:], A.subtract, ["f2", "LB2", "aa"], ["eeU"])
+        tt(T.ee[:, 0:2 * W], T.f2[:].indirect(L(LBL, 14)), T.aa[:], A.subtract, both("f2") + ["LB", "aa"], ["eeL"])
+        tt(T.ee[:, 2 * W:4 * W], T.f2[:].indirect(L(LBU, 14)), T.aa[:], A.subtract, both("f2") + ["LB2", "aa"], ["eeU"])
         for u, nm in ((0, "L"), (1, "U")):
             for s in range(2):
                 act(T.dd[:, (2 * s + u) * W:(2 * s + u + 1) * W], T.ee[:, (2 * u + s) * W:(2 * u + s + 1) * W], F.Abs, ["ee" + nm], ["d%s%d" % (nm, s)])
         if r == 0:
+            seat_of_place(4)
             act(T.tc[:], T.oS[:].indirect(L(LO0, 14)), F.Identity, ["oS", "oSx", "LO0", "cf10"], ["tc"], scale=col(10))
             act(T.td[:], T.oS[:].indirect(L(LO1, 14)), F.Identity, ["oS", "oSx", "LO1", "cf"], ["td"], scale=col(4))
         act(T.ons[:], T.iof[:].indirect(T[ON][:]), F.Copy, ["iof", ON], ["ons"])
@@ -398,47 +426,43 @@ def rank_program(g, core, T, topo):
             return T["tt%d" % s][:, 8 + t:8 + 4 * W:4]
 
         def head(w, s):
-            o, up = 2 * s * W, w >= 8
+            o = 2 * s * W
             vL, dL = T.vv[:, o:o + W], T.dd[:, o:o + W]
-            XL, XU = "#%d" % (2 * s), "#%d" % (2 * s + 1)
+            XL = "#%d" % (2 * s)
             if w == 0:
-                tt(vL, dL, T.kb[:], A.max, ["dL%d" % s, "kb0", "kb1", "kb2", "kb3"], ["vL%d" % s])
+                tt(vL, dL, T.kb[:], A.max, ["dL%d" % s, "kb0", "kb1", "kb2", "kb3"], ["v0%d" % s])
             elif w == 1:
                 y = T.yy[:, s * W:(s + 1) * W]
                 tt(y, bank(2 * s, W), T.kb1[:], A.add, [XL, "kbm"], ["yy%d" % s])
                 act(zl(s, 1), y, F.Identity, ["yy%d" % s], ["t%dl1" % s], scale=1 / B, bias=-1.0)
-                tt(vL, y, dL, A.max, ["yy%d" % s, "dL%d" % s], ["vL%d" % s])
             else:
-                tt(vL, bank(2 * s, W), dL, A.max, [XL, "dL%d" % s], ["vL%d" % s])
+                tt(vL, bank(2 * s, W), dL, A.max, [XL, "dL%d" % s], ["v0%d" % s])
                 if w == SW - 1:
                     act(zl(s, 1), dL, F.Copy, ["dL%d" % s], ["t%dl1" % s], scale=0.0)
                 else:
                     act(zl(s, 1), bank(2 * s, W), F.Identity, [XL], ["t%dl1" % s], scale=1 / B, bias=-1.0)
                     if w >= 7:
                         act(zl(s, 3), bank(2 * s, W), F.Identity, [XL], ["t%dl3" % s], scale=1 / B, bias=7.0)
-                if up:
-                    tt(T.vv[:, o + W:o + 2 * W], bank(2 * s + 1, W), T.dd[:, o + W:o + 2 * W], A.max, [XU, "dU%d" % s], ["vU%d" % s])
-
-        def mid(w, s):
-            o, up = 2 * s * W, w >= 8
-            m = 2 * W if up else W
-            for nm in (("f",) if up else ("f", "w")):
-                for par in range(2):
-                    scan(T["f" + nm][:, o + par:o + m:2], T.rst[:, par:m:2], T.vv[:, o + par:o + m:2], 0.0, A.max, A.min,
-                         ["rst", "vL%d" % s] + (["vU%d" % s] if up else []), ["%s%d%d" % (nm, s, par)])
-
-        def ends(w, s):
             if w >= 8:
-                for u in range(2):
-                    o = (2 * s + u) * W
-                    cp(T.fw[:, o + 32:o + 102], T.ff[:, o + 32:o + 102], ["f%d0" % s, "f%d1" % s], ["w%d%d" % (s, u), "w%d%d" % (s, 1 - u)] if u == 0 else ["wu%d" % s])
+                tt(T.vv[:, o + W:o + 2 * W], bank(2 * s + 1, W), T.dd[:, o + W:o + 2 * W], A.max, ["#%d" % (2 * s + 1), "dU%d" % s], ["v1%d" % s])
 
-        def flags(w, s):
-            o = 2 * s * W
-            for u in range(2 if w >= 8 else 1):
-                c = slice(o + u * W, o + (u + 1) * W)
+        def body(w, s, fill=None):
+            if w == 1:
+                o = 2 * s * W
+                tt(T.vv[:, o:o + W], T.yy[:, s * W:(s + 1) * W], T.dd[:, o:o + W], A.max, ["yy%d" % s, "dL%d" % s], ["v0%d" % s])
+            us = range(2 if w >= 8 else 1)
+            for u in us:
+                o = (2 * s + u) * W
+                for nm in ("f", "w"):
+                    for par in range(2):
+                        scan(T["f" + nm][:, o + par:o + W:2], T.rst[:, par:W:2], T.vv[:, o + par:o + W:2], 0.0, A.max, A.min,
+                             ["rst", "v%d%d" % (u, s)], ["%s%d%d%d" % (nm, u, s, par)])
+            if fill:
+                fill()
+            for u in us:
+                c = slice((2 * s + u) * W, (2 * s + u + 1) * W)
                 tt(zl(s, 2 * u), T.fw[:, c].indirect(L(LM, 7)), T.ff[:, c], A.is_lt,
-                   ["f%d0" % s, "f%d1" % s, "LM"] + (["wu%d" % s] if u else ["w%d0" % s, "w%d1" % s]), ["t%dl%d" % (s, 2 * u)])
+                   ["%s%d%d%d" % (nm, u, s, par) for nm in "fw" for par in range(2)] + ["LM"], ["t%dl%d" % (s, 2 * u)])
 
         def tail(w, s):
             nm = "t%d" % s
@@ -446,10 +470,10 @@ def rank_program(g, core, T, topo):
             mm(2 * s, "s", 128, nm, 0, 128, True, False, ["qs1", "q" + nm])
             mm(2 * s, "s", 256, nm, 2, 128, False, True, ["qs1", "q" + nm])
             if w == SW - 1:
-                mm(2 * s + 1, "s", 512, nm, 2, 128, True, True, ["qs1", "q" + nm])
+                mm(2 * s + 1, "s", 512, nm, 2, 128, True, True, ["qs2", "q" + nm])
             elif w >= 7:
                 mm(2 * s + 1, "s", 128, nm, 0, 128, True, False, ["qs1", "q" + nm])
-                mm(2 * s + 1, "s", 384, nm, 2, 128, False, True, ["qs1", "q" + nm])
+                mm(2 * s + 1, "s", 384, nm, 2, 128, False, True, ["qs2", "q" + nm])
 
         def aside(w):
             b = w % 4
@@ -459,8 +483,6 @@ def rank_program(g, core, T, topo):
                 decode_mm(XN, b, "q" + XN)
             elif w < 8:
                 act(T.dn[:, b * C:(b + 1) * C], bank(4 + b, C), F.Copy, [k], ["dn%d" % b], scale=1 / 32)
-                if w == 5:
-                    qz("g", 0, C, T.gt[:], ["gt%d" % i for i in range(4)], ["qg"])
                 if w == 6:
                     decode_mm("g", 0, "qg")
                     decode_mm("g", 1, "qg")
@@ -471,67 +493,68 @@ def rank_program(g, core, T, topo):
                     decode_mm("g", 3, "qg")
                 act(T.dp[:, b * C:(b + 1) * C], bank(4 + b, C), F.Copy, [k], ["dp%d" % b], scale=1 / 32)
 
-        def extras(w):
-            if w < 4:
-                qz("e", 128 * w, 128 * w + 128, T.et[:, 3 - w:515 - w], ["et"], ["qe%d" % w])
-                decode_mm(XP, w, "q" + XP)
+        def extras(w, s):
+            if w == 5:
+                qz("g", H * s, H * s + H, T.gt[:, 4 * H * s:4 * H * (s + 1)], ["gt%d" % i for i in range(4)] + ["qg"], ["qg"])
+            if r:
+                return
             if w == 2:
-                ms(T.fw[:, W:W + 32], 0.0, ["wu0"])
-                ms(T.fw[:, W + 102:2 * W], 0.0, ["wu0"])
+                qz("s", 384 + 128 * s, 512 + 128 * s, T.st[:, 1536 + 512 * s:2048 + 512 * s], ["st%d%d" % (3 + s, t) for t in range(4)] + ["qs2"], ["qs2"])
             if w == 3:
-                ms(T.fw[:, 3 * W:3 * W + 32], 0.0, ["wu1"])
-                ms(T.fw[:, 3 * W + 102:4 * W], 0.0, ["wu1"])
+                c = slice(s * W, (s + 1) * W)
+                tt(T.oa[:, c], T.tc[:, c], T.td[:, c], A.add, ["tc", "td", "oa"], ["oa"])
             if w == 4:
-                tt(T.oa[:, 0:2 * W], T.tc[:], T.td[:], A.add, ["tc", "td"], ["oa"])
-            if w == 6:
-                tt(T.dl[:], T.oa[:, 2:2 * W + 2], T.oa[:, 0:2 * W], A.subtract, ["oa", "oax"], ["dl"])
-            if 2 <= w < 7:
-                late_lists(w - 2)
-            if 3 <= w < 8:
-                seat_of_place(w - 3)
+                tt(T.dl[:, s * W:(s + 1) * W], T.oa[:, s * W + 2:(s + 1) * W + 2], T.oa[:, s * W:(s + 1) * W], A.subtract, ["oa", "oax", "dl"], ["dl"])
+            if w == 0 and s:
+                late_lists(0)
+            if w in (6, 7):
+                late_lists(2 * (w - 6) + 1 + s)
 
-        head(0, 0)
-        mid(0, 0)
         for w in range(SW):
+            head(w, 0)
+            if w:
+                tail(w - 1, 1)
+                aside(w - 1)
+            body(w, 0, lambda: extras(w, 0))
             head(w, 1)
-            ends(w, 0)
-            if w >= 8:
-                mid(w, 1)
-                flags(w, 0)
-                ends(w, 1)
-            else:
-                flags(w, 0)
-                mid(w, 1)
             tail(w, 0)
-            flags(w, 1)
-            if r == 0:
-                extras(w)
-            tail(w, 1)
-            if w + 1 < SW:
-                aside(w)
-                head(w + 1, 0)
-                mid(w + 1, 0)
+            body(w, 1, lambda: extras(w, 1))
 
         sl = lambda nm, s: T[nm][:, s * W:(s + 1) * W]
-        for s in range(2):
-            ts(sl("rr", s), bank(2 * s, W), -1 / B, A.mult, ["#%d" % (2 * s)], ["rr%d" % s], 1.0, A.add)
-            act(sl("ep", s), bank(2 * s + 1, W), F.Identity, ["#%d" % (2 * s + 1), "cf11"], ["ep%d" % s], scale=-1.0, bias=col(11))
-            if s == 0:
-                tt(sl("pr", 0), zl(0, 0), sl("dl", 0), A.mult, ["t0l0", "dl"], ["prL0"])
+
+        def fin(step, s):
+            if step == 0:
+                ts(sl("rr", s), bank(2 * s, W), -1 / B, A.mult, ["#%d" % (2 * s)], ["rr%d" % s], 1.0, A.add)
+                act(sl("ep", s), bank(2 * s + 1, W), F.Identity, ["#%d" % (2 * s + 1), "cf11"], ["ep%d" % s], scale=-1.0, bias=col(11))
+            elif step == 1:
+                for par in range(2):
+                    c = slice(s * W + par, (s + 1) * W, 2)
+                    scan(T.ro[:, c], T.rr[:, c], T.mw[:, par:W:2], 0.0, A.add, A.mult, ["rr%d" % s, "mw0"], ["ro%d%d" % (s, par)])
+            elif step == 2:
+                tt(sl("g2", s), sl("ep", s).indirect(L(LE, 7)), sl("ro", s), A.is_gt, ["ep%d" % s, "LE", "ro%d0" % s, "ro%d1" % s], ["g2%d" % s])
+            elif step == 3:
+                tt(sl("gu", s), sl("g2", s), zl(s, 2), A.add, ["g2%d" % s, "t%dl2" % s], ["gu%d" % s])
+            elif step == 4:
+                tt(sl("pr", 2 * s + 1), sl("gu", s), sl("dl", s), A.mult, ["gu%d" % s, "dl"], ["prU%d" % s])
+            elif step == 5:
+                o = 2 * s * W
+                for par in range(2):
+                    scan(T.hs[:, o + par:o + 2 * W:2], T.mw[:, par:2 * W:2], T.pr[:, o + par:o + 2 * W:2], 0.0, A.mult, A.add,
+                         ["mw0", "mw1", "prL%d" % s, "prU%d" % s], ["hs%d%d" % (s, par)])
+            else:
+                tt(sl("pr", 2 * s), zl(s, 0), sl("dl", s), A.mult, ["t%dl0" % s, "dl"], ["prL%d" % s])
+
+        fin(0, 0)
+        tail(SW - 1, 1)
         aside(SW - 1)
-        for par in range(2):
-            scan(T.ro[:, par:2 * W:2], T.rr[:, par:2 * W:2], T.mw[:, par:2 * W:2], 0.0, A.add, A.mult, ["rr0", "rr1", "mw0", "mw1"], ["ro%d" % par])
-        tt(sl("pr", 2), zl(1, 0), sl("dl", 1), A.mult, ["t1l0", "dl"], ["prL1"])
-        tt(T.g2[:], T.ep[:].indirect(L(LE, 14)), T.ro[:], A.is_gt, ["ep0", "ep1", "LE", "ro0", "ro1"], ["g2"])
-        for s in range(2):
-            tt(sl("gu", s), sl("g2", s), zl(s, 2), A.add, ["g2", "t%dl2" % s], ["gu%d" % s])
-        for s in range(2):
-            tt(sl("pr", 2 * s + 1), sl("gu", s), sl("dl", s), A.mult, ["gu%d" % s, "dl"], ["prU%d" % s])
-        for s in range(2):
-            o = 2 * s * W
-            for par in range(2):
-                scan(T.hs[:, o + par:o + 2 * W:2], T.mw[:, par:2 * W:2], T.pr[:, o + par:o + 2 * W:2], 0.0, A.mult, A.add,
-                     ["mw0", "mw1", "prL%d" % s, "prU%d" % s], ["hs%d%d" % (s, par)])
+        for step, s in ((1, 0), (6, 0), (2, 0), (0, 1), (3, 0), (1, 1), (6, 1), (2, 1), (4, 0), (3, 1), (5, 0), (4, 1)):
+            fin(step, s)
+        if r + 1 < R:
+            for s in range(2):
+                ms(zl(s, 2), 0.0, ["t%dl2" % s])
+        else:
+            qz("v", 0, 128, T.vt[:], ["vt"], ["qv"])
+        fin(5, 1)
         cp(T[HW][:], T.hs[:].indirect(L(LH, 2)), ["hs00", "hs01", "hs10", "hs11", "LH"], [HW])
         send([(nxt, T[HW][:, 0:24], T[HP][:], "ah%d" % r)], [HW])
         arrive(HP, "ah%d" % r, 8)
@@ -541,28 +564,22 @@ def rank_program(g, core, T, topo):
                 mm(bk(h, b), "e", 128 * b, X, H * h, H, True, False, ["qe%d" % b] + KX)
         cp(T.wr[:].indirect(T[HW][:, 0:24]), T.ons[:], ["ons", HW], ["wr"])
         act(T.hr[:], T.iof[:].indirect(T[HP][:]), F.Copy, ["iof", HP], ["hr"])
-        if r + 1 < R:
-            for s in range(2):
-                ms(zl(s, 2), 0.0, ["t%dl2" % s])
-        else:
-            qz("v", 0, 128, T.vt[:], ["vt"], ["qv"])
+        if r + 1 == R:
             dma("s", T.ol[:], T.wr[0:128:16, :], "out_s", ["wr"], ())
-        tt(T.y2[:], T.wr[:], T.cap[:], A.min, ["wr", "cap"], ["y2"])
-        scan(T.f2[:], T.rho[:], T.y2[:], -BIG, A.min, A.max, ["rho", "y2"], ["f2"])
-        cp(T.wl[:], T.f2[:, 15:C:16], ["f2"], ["wl"])
+        own("y2", "f2", lambda h: T.wr[:, hc(h)], ["wr"])
+        as_list("wl", "f2", "wl")
         for h in range(2):
             for b in range(4):
                 act(T.vg[:, b * C + H * h:b * C + H * h + H], T.dn[:, b * C:(b + 1) * C].indirect(T.wl[:, 12 * h:12 * h + 12]), F.Copy,
-                    ["dn%d" % b, "wl"], ["vg%d%d" % (h, b)])
-        tt(T.y1[:], T.hr[:].indirect(T.sp[:]), T.cap[:], A.min, ["hr", "sp", "cap"], ["y1"])
-        scan(T.fs[:], T.rho[:], T.y1[:], -BIG, A.min, A.max, ["rho", "y1"], ["fs"])
-        cp(T.hl[:], T.fs[:, 15:C:16], ["fs"], ["hl"])
+                    ["dn%d" % b, "wlh%d" % h], ["vg%d%d" % (h, b)])
+        own("y1", "fs", lambda h: T.hr[:].indirect(T.sp[:, 12 * h:12 * h + 12]), ["hr", "sp"])
+        as_list("hl", "fs", "hl")
         XO = "x%d" % (r + 1)
 
         def z_half(h, bs):
             for b in bs:
                 tt(T.zt[:, 4 * H * h + b:4 * H * (h + 1):4], T.dp[:, b * C:(b + 1) * C].indirect(T.hl[:, 12 * h:12 * h + 12]),
-                   T.vg[:, b * C + H * h:b * C + H * h + H], A.max, ["dp%d" % b, "hl", "vg%d%d" % (h, b)], ["zt%d%d" % (h, b)])
+                   T.vg[:, b * C + H * h:b * C + H * h + H], A.max, ["dp%d" % b, "hlh%d" % h, "vg%d%d" % (h, b)], ["zt%d%d" % (h, b)])
 
         def w_half(h):
             qz("z", H * h, H * h + H, T.zt[:, 4 * H * h:4 * H * (h + 1)], ["zt%d%d" % (h, b) for b in range(4)], ["qz%d" % h])
@@ -582,18 +599,23 @@ def rank_program(g, core, T, topo):
         z_half(1, [1, 2, 3])
         w_half(1)
         x_half(0)
+        if r + 1 < R:
+            half_scores(XO)
+        else:
+            mm(4, "v", 0, "x2", 0, H, True, True, ["qv", "qx20"])
         for b in (0, 2):
             ts(T.xn[:, 4 * H + b:8 * H:4], bank(b, H), 0.03125, A.mult, ["#%d" % b], ["xn1%d" % b])
+        if r + 1 < R:
+            own_mask("y1", 0, bank(5, H), ["#5"])
         x_half(1)
 
-    for h in range(2):
-        mm(4 + h, "v", 0, "x2", H * h, H, True, True, ["qv", "qx2%d" % h])
-    dma("s", T.oc[:], T.qx2[:].bitcast(dt.uint8), "out_s", ["qx20", "qx21"], ())
+    mm(5, "v", 0, "x2", H, H, True, True, ["qv", "qx21"])
     act(T.yo[:, 0:H], bank(4, H), F.Copy, ["#4"], ["yo0"])
+    dma("s", T.oc[:], T.qx2[:].bitcast(dt.uint8), "out_s", ["qx20", "qx21"], ())
     cp(T.yo[:, H:C], bank(5, H), ["#5"], ["yo1"])
-    dma("a", T.y[:], T.yo[:], "out_a", ["yo0", "yo1"], ())
     for k in range(4):
         dma("a" if k % 2 else "s", T.osc[4 * k:4 * k + 4, :], T.sx2[32 * k:32 * k + 4, :], "out_a" if k % 2 else "out_s", ["qx20", "qx21"], ())
+    dma("a", T.y[:], T.yo[:], "out_a", ["yo0", "yo1"], ())
 
     chan = lambda i: ops[i][3] if ops[i][3] else "e" + ops[i][0]
     known = {e: {} for e in ENG}

@@ -8,13 +8,16 @@ H = 192
 R = 2
 SW = 12
 W = 112
+WU = 102
 B = 2.0 ** 30
 DS = 2.0 ** -42
 BIG = 2.0 ** 90
+K = 1024.0
 TN = [384, 320, 256, 192, 128, 128]
 TO = [0, 384, 704, 960, 1152, 1280]
 KS = (23, 22, 21)
-LU, LM, LE, LA0, LA1, LBL, LBU, LSW, LH, LO0, LO1 = 0, 16, 24, 32, 46, 60, 74, 88, 112, 114, 128
+NV = 3
+LU, LP, LSW, LA0, LA1, LBL, LBU, LE, LH = 0, 16, 40, 64, 72, 80, 88, 96, 104
 
 Q4, U8, F32, BF, I32, U16 = "float8_e4m3fn_x4", "uint8", "float32", "bfloat16", "int32", "uint16"
 SCRATCH = {"ps": ("psum", [128, 4096], F32)}
@@ -25,29 +28,37 @@ def _sb(name, n, d):
 
 
 for _n, _w in (("qu", 128), ("qus", 256), ("qv", 128), ("qw", 512), ("qx0", C), ("qx1", C), ("qx2", C), ("qn0", C), ("qn1", C),
-               ("qp0", C), ("qp1", C), ("qg", C), ("qz", C), ("qc", 1408), ("qt0", 130), ("qt1", 130), ("qe", 512), ("qs", 640)):
+               ("qp0", C), ("qp1", C), ("qg", C), ("qz", C), ("qc", 1408), ("qt0", 130), ("qt1", 130), ("qe", 512), ("qs", 768)):
     _sb(_n, _w, Q4)
     _sb("s" + _n[1:], _w, U8)
 for _n, _w in (("xt", 4 * C), ("ut", 512), ("vt", 512), ("xn", 4 * C), ("gt", 4 * C), ("zt", 4 * C), ("ct", 4 * 1408), ("tt0", 520), ("tt1", 520),
-               ("et", 516), ("st", 2560), ("dn", 4 * C), ("dp", 4 * C), ("vg", 4 * C), ("sgn", 3 * C), ("junk", 3360)):
+               ("et", 516), ("st", 3072), ("dn", 4 * C), ("dp", 4 * C), ("vg", 4 * C), ("sgn", 4 * C), ("junk", 3360), ("mu", C), ("seg", C)):
     _sb(_n, _w, BF)
-for _n, _w in (("iof", C), ("cap", C), ("rho", C), ("mu", C), ("c0", 24), ("cf", 16), ("jm", 128), ("b16", 128), ("b8", 128), ("kb", W), ("kb1", W),
-               ("ky", 144), ("slot", 136), ("rst", 2 * W), ("mw", 2 * W), ("tf", 192), ("y1", C), ("fs", C), ("seg", C), ("rsum", 24), ("t1", 24),
-               ("t2", 24), ("y2", C), ("f2", C), ("ma", C), ("mb", C), ("aS", 416), ("oS", 416), ("ons", C), ("ta", 2 * W), ("tb", 2 * W),
-               ("tc", 2 * W), ("td", 2 * W), ("aa", 2 * W), ("oa", 240), ("dl", 2 * W), ("ee", 4 * W), ("dd", 4 * W), ("vv", 4 * W), ("ff", 4 * W),
-               ("fw", 4 * W), ("yy", 2 * W), ("rr", 2 * W), ("ro", 2 * W), ("ep", 2 * W), ("g2", 2 * W), ("gu", 2 * W), ("pr", 4 * W), ("hs", 4 * W),
-               ("wr", C), ("hr", C), ("yo", C)):
+for _n, _w in (("iof", C), ("cap", C), ("rho", C), ("cs", C), ("c0", 24), ("cf", 16), ("c16", 64), ("jm", 128), ("b16", 128), ("b8", 128),
+               ("kb", W), ("kb1", W), ("kx", 96), ("ky", 144), ("slot", 136), ("rst", 2 * W), ("mw", 2 * W), ("cb", 272), ("rows", C), ("rowo", C),
+               ("tf", 32), ("y1", C), ("fs", C), ("rsum", 24), ("t1", 24), ("y2", C), ("f2", C), ("ma", C), ("mb", C), ("aS", 416), ("oS", C),
+               ("ons", C), ("opr", C), ("opn", C), ("ta", 2 * W), ("tb", 2 * W), ("aa", 2 * W), ("ee", 4 * W), ("dd", 4 * W), ("vv", 4 * W), ("ff", 4 * W),
+               ("yy", 2 * W), ("rr", 2 * W), ("ro", 2 * W), ("ep", 2 * W), ("g2", 2 * W), ("gu", 2 * W), ("hs", 4 * W),
+               ("wr", C), ("wj", C), ("hr", C), ("yo", C)):
     _sb(_n, _w, F32)
-for _n, _w in (("ii", C), ("ci", 16), ("lr", 34), ("kx", 108), ("ti", 64), ("pi", 24), ("pj", 72)):
+for _n, _w in (("ci", 16), ("ti", 16), ("pi", 24), ("pj", 96)):
     _sb(_n, _w, I32)
-for _n, _w in (("lst", 160), ("pl", 24), ("ow0", 24), ("ow1", 24), ("on0", 24), ("on1", 24), ("hw0", 32), ("hw1", 32), ("hp0", 24), ("hp1", 24),
-               ("sp", 24), ("wl", 24), ("hl", 24)):
+for _n, _w in (("lst", 136), ("pl", 24), ("ow0", 24), ("ow1", 24), ("on0", 24), ("on1", 24), ("op0", 24), ("op1", 24), ("hw0", 32), ("hw1", 32),
+               ("hp0", 24), ("hp1", 24), ("sp", 24), ("wl", 24), ("hl", 24)):
     _sb(_n, _w, U16)
 
 ENG = ("v", "a", "t", "g", "s")
 DMAS = ["dx", "dx2", "du", "dv", "dw", "dw2", "out_s", "out_a"]
-ARR = ["an0", "an1", "ap0", "ap1", "al0", "al1", "ah0", "ah1"]
+ARR = ["an0", "an1", "ap0", "ap1", "al0", "al1", "ao0", "ao1", "ah0", "ah1"]
 SEMAPHORES = ["ev", "ea", "et", "eg", "sent"] + DMAS + ARR
+
+
+def v(name, a=0, b=None, step=1):
+    return (name, a, SCRATCH[name][1][1] if b is None else b, step, None)
+
+
+def at(win, offs):
+    return win[:4] + (offs,)
 
 
 def rank_program(g, core, T, topo):
@@ -59,79 +70,90 @@ def rank_program(g, core, T, topo):
     Q = {"v": g.vector, "a": g.scalar, "t": g.tensor, "g": g, "s": g.sync}
     V, S, P = g.vector, g.scalar, g.tensor
 
-    ops, last_w, readers, sent = [], {}, {}, [0]
+    ops, seen, sent = [], {}, [0]
+
+    def ap(x, cast=None):
+        if not isinstance(x, tuple):
+            return x
+        r = T[x[0]][:, x[1]:x[2]:x[3]] if x[3] > 1 else T[x[0]][:, x[1]:x[2]]
+        if cast:
+            r = r.bitcast(cast)
+        return r.indirect(ap(x[4])) if x[4] else r
+
+    def bits(x):
+        if x[0] == "ps":
+            return sum(1 << b for b in range(x[1] // 512, (x[2] - 1) // 512 + 1))
+        return sum(1 << c for c in range(x[1], x[2], x[3]))
 
     def add(eng, fn, rd=(), wr=(), sem=None, cnt=None):
-        deps = set()
-        for k in rd:
-            if k in last_w:
-                deps.add(last_w[k])
-            if k[0] == "#":
-                deps.update(i for i in readers.get(k, ()) if ops[i][0] != eng)
-        for k in wr:
-            if k in last_w:
-                deps.add(last_w[k])
-            deps.update(readers.get(k, ()))
+        me, deps = len(ops), set()
+        rd = [x for x in rd if isinstance(x, tuple)]
+        rd += [x[4] for x in rd + list(wr) if x[4]]
+        for x in rd:
+            m = bits(x)
+            deps.update(i for i, k, w in seen.get(x[0], ()) if k & m and (w or (x[0] == "ps" and ops[i][0] != eng)))
+        for x in wr:
+            m = bits(x)
+            deps.update(i for i, k, w in seen.get(x[0], ()) if k & m)
         if eng == "t":
             deps = {i for i in deps if ops[i][0] != "t"}
-        me = len(ops)
         ops.append((eng, fn, deps, sem, cnt))
-        for k in rd:
-            readers.setdefault(k, []).append(me)
-        for k in wr:
-            last_w[k] = me
-            readers[k] = []
-        return me
+        for x in wr:
+            m = bits(x)
+            seen[x[0]] = [(i, k & ~m, w) for i, k, w in seen.get(x[0], ()) if k & ~m] + [(me, m, True)]
+        for x in rd:
+            seen.setdefault(x[0], []).append((me, bits(x), False))
 
-    def arrive(key, sem, cnt):
-        last_w[key] = len(ops)
-        ops.append(("x", None, set(), sem, cnt))
+    def arrive(views, sem, cnt):
+        add("x", None, (), views, sem, cnt)
 
-    def tt(out, a, b, op, rd, wr):
-        add("v", lambda: V.tensor_tensor(out, a, b, op), rd, wr)
+    def tt(out, a, b, op):
+        add("v", lambda: V.tensor_tensor(ap(out), ap(a), ap(b), op), [a, b], [out])
 
-    def ts(out, a, s1, op0, rd, wr, s2=None, op1=None):
+    def ts(out, a, s1, op0, s2=None, op1=None):
         if op1 is None:
-            add("v", lambda: V.tensor_scalar(out, a, s1, None, op0), rd, wr)
+            add("v", lambda: V.tensor_scalar(ap(out), ap(a), ap(s1), None, op0), [a, s1], [out])
         else:
-            add("v", lambda: V.tensor_scalar(out, a, s1, s2, op0, op1), rd, wr)
+            add("v", lambda: V.tensor_scalar(ap(out), ap(a), ap(s1), ap(s2), op0, op1), [a, s1, s2], [out])
 
-    def cp(out, a, rd, wr):
-        add("v", lambda: V.tensor_copy(out, a), rd, wr)
+    def cp(out, a, cast=None):
+        add("v", lambda: V.tensor_copy(ap(out, cast), ap(a, cast)), [a], [out])
 
-    def scan(out, d0, d1, init, op0, op1, rd, wr):
-        add("v", lambda: V.tensor_tensor_scan(out, d0, d1, init, op0, op1), rd, wr)
+    def scan(out, d0, d1, init, op0, op1):
+        add("v", lambda: V.tensor_tensor_scan(ap(out), ap(d0), ap(d1), init, op0, op1), [d0, d1], [out])
 
-    def ms(ap, c, wr):
-        add("v", lambda: V.memset(ap, c), (), wr)
+    def ms(out, c):
+        add("v", lambda: V.memset(ap(out), c), (), [out])
 
-    def act(out, a, f, rd, wr, **kw):
-        add("a", lambda: S.activation(out, a, f, **kw), rd, wr)
+    def act(out, a, f=F.Copy, **kw):
+        acc = [kw["accum_out"]] if "accum_out" in kw else []
+        add("a", lambda: S.activation(ap(out), ap(a), f, **{k: ap(x) for k, x in kw.items()}), [a, kw.get("bias"), kw.get("scale")], [out] + acc)
 
-    def qz(name, c0, c1, src, rd, wr):
-        add("v", lambda: V.quantize_mx(T["q" + name][:, c0:c1], T["s" + name][:, c0:c1], src), rd, wr)
+    def qz(name, c0, c1, src):
+        q, s = v("q" + name, c0, c1), v("s" + name, c0, c1)
+        add("v", lambda: V.quantize_mx(ap(q), ap(s), ap(src)), [src], [q, s])
 
-    def mm(bk, st, s0, mv, m0, m, start, stop, rd):
-        add("t", lambda: P.matmul_mx(T.ps[:, 512 * bk:512 * bk + m], T["q" + st][:, s0:s0 + 128], T["s" + st][:, s0:s0 + 128],
-                                     T["q" + mv][:, m0:m0 + m], T["s" + mv][:, m0:m0 + m], start, stop), rd, ["#%d" % bk])
+    def bank(b, m, a=0):
+        return v("ps", 512 * b + a, 512 * b + m)
 
-    def iota(out, pat, base, cm, wr, fl=False):
-        if fl:
-            add("g", lambda: g.iota(out, pat, base, cm, allow_small_or_imprecise_dtypes=True), (), wr)
+    def mm(bk, st, s0, mv, m0, m, start=True, stop=True):
+        x = [v("q" + st, s0, s0 + 128), v("s" + st, s0, s0 + 128), v("q" + mv, m0, m0 + m), v("s" + mv, m0, m0 + m)]
+        add("t", lambda: P.matmul_mx(ap(bank(bk, m)), ap(x[0]), ap(x[1]), ap(x[2]), ap(x[3]), start, stop), x, [bank(bk, m)])
+
+    def iota(out, pat, base, cm=0):
+        if SCRATCH[out[0]][2] == I32:
+            add("g", lambda: g.iota(ap(out), pat, base, cm), (), [out])
         else:
-            add("g", lambda: g.iota(out, pat, base, cm), (), wr)
+            add("g", lambda: g.iota(ap(out), pat, base, cm, allow_small_or_imprecise_dtypes=True), (), [out])
 
-    def sel(out, a, pat, op, fill, base, cm, rd, wr):
-        add("g", lambda: g.affine_select(out, a, pat, op, fill, base, cm), rd, wr)
+    def sel(out, a, pat, op, fill, base, cm):
+        add("g", lambda: g.affine_select(ap(out), ap(a), pat, op, fill, base, cm), [a], [out])
 
-    def dma(eng, out, a, sem, rd, wr):
+    def dma(eng, out, a, sem, rd=(), wr=()):
         add(eng, lambda: Q[eng].dma_start(out, a), rd, wr, sem, 16)
 
-    def bank(b, m):
-        return T.ps[:, 512 * b:512 * b + m]
-
     def L(c, k):
-        return T.lst[:, c:c + k]
+        return v("lst", c, c + k)
 
     first, second = sorted((prv, nxt), key=lambda d: len(topo.engines(core, d)))
     e1 = topo.engines(core, first)[:8]
@@ -139,459 +161,442 @@ def rank_program(g, core, T, topo):
     mask = {first: sum(1 << e for e in e1), second: sum(1 << e for e in e2)}
     assert len(e1) == 8 and len(e2) == 8
 
-    def send(items, rd):
+    def send(items, cast=None):
         def fn():
             tr = []
             for dst, src, land, sem in items:
                 rid, pid, _se = topo.addr(dst)
-                tr.append(RemoteDMATransfer(dst_ids=[DstId(rid=rid, pnc=pid)], dma_engine_mask=mask[dst], remote_sem=T.sem[sem], src=src, dst=land))
+                tr.append(RemoteDMATransfer(dst_ids=[DstId(rid=rid, pnc=pid)], dma_engine_mask=mask[dst], remote_sem=T.sem[sem],
+                                            src=ap(src, cast), dst=ap(land, cast)))
             g.remote_dma_fused(tr, local_sem=T.sem.sent)
-        add("g", fn, rd, (), "-")
+        add("g", fn, [x[1] for x in items], (), "-")
         sent[0] += 8 * len(items)
 
-    col = lambda i: T.cf[:, i:i + 1]
-    lane_of = lambda k, t: T.st[:, 512 * k + t:512 * (k + 1):4]
-    tf = lambda i, k=14: T.tf[:, 16 * i:16 * i + k]
-    hc = lambda h: slice(H * h, H * h + H)
+    col = lambda i: v("cf", i, i + 1)
+    lane_of = lambda k, t: v("st", 512 * k + t, 512 * (k + 1), 4)
+    half = lambda nm, h: v(nm, H * h, H * h + H)
+    lhalf = lambda nm, h: v(nm, 12 * h, 12 * h + 12)
+    ends = lambda nm, h: v(nm, H * h + 15, H * h + H, 16)
 
-    def own_mask(y, h, src, rd):
-        tt(T[y][:, hc(h)], src, T.cap[:, hc(h)], A.min, rd + ["cap"], [y + "h%d" % h])
+    def own_mask(y, h, src):
+        tt(half(y, h), src, half("cap", h), A.min)
 
     def own_scan(y, f, h):
-        scan(T[f][:, hc(h)], T.rho[:, hc(h)], T[y][:, hc(h)], -BIG, A.min, A.max, ["rho", y + "h%d" % h], [f + "h%d" % h])
+        scan(half(f, h), half("rho", h), half(y, h), -BIG, A.min, A.max)
 
-    def own(y, f, src, rd, between=None):
-        for h in range(2):
-            own_mask(y, h, src(h), rd)
-        if between:
-            between()
-        for h in range(2):
-            own_scan(y, f, h)
+    def own_whole(f, h, src):
+        scan(half(f, h), src, half("cs", h), K, A.min, A.add)
 
-    def as_list(out, f, key):
-        for h in range(2):
-            cp(T[out][:, 12 * h:12 * h + 12], T[f][:, H * h + 15:H * h + H:16], [f + "h%d" % h], [key + "h%d" % h])
+    def as_list(out, f, h):
+        ts(lhalf(out, h), ends(f, h), -K, A.add)
 
-    both = lambda k: [k + "h0", k + "h1"]
-
-    lane = lambda k, m: T.ct[:, 4 * TO[(24 - k) // 4] + (24 - k) % 4:4 * (TO[(24 - k) // 4] + m):4]
-    key = lambda k: "ct%d" % (24 - k)
+    lane = lambda k, m: v("ct", 4 * TO[(24 - k) // 4] + (24 - k) % 4, 4 * (TO[(24 - k) // 4] + m), 4)
+    mine = lambda k: v("fs", 16 * k + 15, 16 * k + 16)
 
     def cmp(k):
-        b = 0 if k >= 12 else 5
-        ts(lane(k, 16 * k), bank(b, 16 * k), T.fs[:, 16 * k + 15:16 * k + 16], A.is_lt, ["#%d" % b, "fsh%d" % (k // 12)], [key(k)])
-        act(T.junk[:, 8 * k * (k - 1):8 * k * (k + 1)], lane(k, 16 * k), F.Copy, [key(k)], ["rs%d" % k], accum_out=T.rsum[:, k:k + 1])
+        ts(lane(k, 16 * k), bank(0 if k >= 12 else 5, 16 * k), mine(k), A.is_lt)
+        act(v("junk", 8 * k * (k - 1), 8 * k * (k + 1)), lane(k, 16 * k), accum_out=v("rsum", k, k + 1))
 
     def tile(q):
-        qz("c", TO[q], TO[q] + TN[q], T.ct[:, 4 * TO[q]:4 * (TO[q] + TN[q])], ["ct%d" % (4 * q + i) for i in range(4)], ["qc%d" % q])
+        qz("c", TO[q], TO[q] + TN[q], v("ct", 4 * TO[q], 4 * (TO[q] + TN[q])))
 
-    def half_scores(x):
-        mm(5, "us", 0, x, 0, H, True, True, ["qus", "sus", "q%s0" % x])
+    dma("s", T.xt[:, 0:768], T.x[:, 0:768], "dx", (), [v("xt", 0, 768)])
+    dma("a", T.ut[:], T.u[:], "du", (), [v("ut")])
+    dma("a", T.xt[:, 768:1536], T.x[:, 768:1536], "dx2", (), [v("xt", 768, 1536)])
 
-    dma("s", T.xt[:, 0:768], T.x[:, 0:768], "dx", (), ["xt0"])
-    dma("a", T.ut[:], T.u[:], "du", (), ["ut"])
-    dma("a", T.xt[:, 768:1536], T.x[:, 768:1536], "dx2", (), ["xt1"])
-
-    iota(T.ci[:, 0:1], [[0, 1]], 0, 1, ["ci0"])
-    iota(T.ti[:, 0:16], [[1, 2], [16, 8]], 0, 0, ["ti0"])
-    iota(T.ii[:], [[0, 24], [1, 16]], 0, 0, ["ii"])
-    iota(T.jm[:], [[1, 8], [0, 16]], 0, 0, ["jm"], True)
-    iota(T.c0[:], [[16, 24]], 15, 0, ["c0"], True)
-    iota(T.tf[:, 128:152], [[32, 12], [8, 2]], 0, 0, ["tfs"], True)
-    iota(T.tf[:, 0:14], [[16, 14]], 0, 0, ["tf0"], True)
-    iota(T.iof[:], [[1, C]], 0, 0, ["iof"], True)
+    iota(v("ci", 0, 1), [[0, 1]], 0, 1)
+    iota(v("ti"), [[1, 2], [16, 8]], 0)
+    iota(v("c16", 0, 16), [[1, 16]], 0)
+    iota(v("jm"), [[1, 8], [0, 16]], 0)
+    iota(v("c0"), [[16, 24]], 15 - int(K))
+    iota(v("tf", 0, 24), [[32, 12], [8, 2]], 0)
+    iota(v("iof"), [[1, C]], 0)
+    ms(v("mu"), 1.0)
+    ms(v("c16", 48, 64), 0.0)
+    for i, (sh, an) in enumerate(((0, 15), (4, 7), (3, 1), (0, 1), (1, 1), (2, 1), (0, 7))):
+        ts(v("ci", i + 1, i + 2), v("ci", 0, 1), sh, A.arith_shift_right, an, A.bitwise_and)
+    ms(v("mu", 0, C, 16), 0.0)
+    ms(v("c16", 63, 64), 2 * K)
+    cp(v("cf", 0, 8), v("ci", 0, 8))
+    cp(L(LU, 16), v("ti"))
+    act(v("rho"), v("mu"), F.Identity, scale=2 * BIG, bias=-BIG)
+    ts(v("c16", 16, 32), v("c16", 0, 16), col(1), A.is_equal)
+    ts(v("c16", 32, 48), v("c16", 0, 16), col(1), A.is_lt)
+    ts(L(LP, 24), v("c0"), 0.0, A.mult, col(1), A.add)
+    ts(v("b16"), v("jm"), col(2), A.is_equal)
+    tt(v("c16", 32, 48), v("c16", 32, 48), v("c16", 16, 32), A.subtract)
+    act(v("cap"), at(v("c16", 16, 32), L(LP, 24)), F.Identity, scale=2 * BIG, bias=-BIG)
     for q in range(6):
         lo = TN[q] - (112 if q == 5 else 48)
-        ms(T.ct[:, 4 * (TO[q] + lo):4 * (TO[q] + TN[q])], 0.0, ["ct%d" % (4 * q + i) for i in range(4)])
-    for i, (sh, an) in enumerate(((0, 15), (4, 7), (3, 15), (3, 1), (0, 1), (1, 1), (2, 1), (0, 7))):
-        ts(T.ci[:, i + 1:i + 2], T.ci[:, 0:1], sh, A.arith_shift_right, ["ci0"], ["ci%d" % (i + 1)], an, A.bitwise_and)
-    cp(L(LU, 16), T.ti[:, 0:16], ["ti0"], ["LU"])
-    cp(T.cf[:, 0:9], T.ci[:, 0:9], ["ci%d" % i for i in range(9)], ["cf"])
-    ts(T.mu[:], T.ii[:], 0.0, A.is_gt, ["ii"], ["mu"])
-    ts(T.y2[:], T.ii[:], col(1), A.is_equal, ["ii", "cf"], both("y2"), 2 * BIG, A.mult)
-    ts(T.b16[:], T.jm[:], col(2), A.is_equal, ["jm", "cf"], ["b16"])
-    ms(T.rsum[:, 0:1], 0.0, ["rs0"])
-    ts(T.c0[:], T.c0[:], col(1), A.subtract, ["c0", "cf"], ["c0"])
-    ts(T.cf[:, 12:13], col(4), 8.0, A.mult, ["cf"], ["cf12"], col(1), A.add)
-    ms(T.et[:], 0.0, ["et"])
-    ms(T.b8[:], 0.0, ["b8"])
-    ts(L(LSW, 24), T.tf[:, 128:152], col(12), A.add, ["tfs", "cf12"], ["LSW"])
-    ms(T.tt0[:], 0.0, ["t0l0", "t0l1", "t0l2", "t0l3"])
-    ms(T.tt1[:], 0.0, ["t1l0", "t1l1", "t1l2", "t1l3"])
-    act(T.rho[:], T.mu[:], F.Identity, ["mu"], ["rho"], scale=2 * BIG, bias=-BIG)
-    act(T.cap[:], T.y2[:], F.Identity, both("y2"), ["cap"], bias=-BIG)
-    qz("u", 0, 128, T.ut[:], ["ut"], ["qu"])
-    qz("x0", 0, H, T.xt[:, 0:768], ["xt0"], ["qx00"])
-    cp(T.qus[:].bitcast(dt.uint32), T.qu[:].bitcast(dt.uint32).indirect(L(LU, 16)), ["qu", "LU"], ["qus"])
-    act(T.sus[:], T.su[:].indirect(L(LU, 16)), F.Copy, ["qu", "LU"], ["sus"])
+        ms(v("ct", 4 * (TO[q] + lo), 4 * (TO[q] + TN[q])), 0.0)
+    ts(v("c16", 32, 48), v("c16", 32, 48), K, A.mult)
+    ms(v("rsum", 0, 1), 0.0)
+    ts(v("c0"), v("c0"), col(1), A.subtract)
+    ts(col(8), col(3), 8.0, A.mult, col(1), A.add)
+    tt(v("c16", 32, 48), v("c16", 32, 48), v("c16", 48, 64), A.add)
     for t in range(4):
-        act(lane_of(0, t), T.b16[:], F.Copy, ["b16"], ["st0%d" % t])
-    half_scores("x0")
-    qz("x0", H, C, T.xt[:, 768:1536], ["xt1"], ["qx01"])
-    for k, t in ((1, 1), (1, 3), (2, 1), (2, 3), (3, 1), (3, 3), (4, 0), (4, 1), (4, 3)):
-        act(lane_of(k, t), T.b16[:], F.Copy, ["b16"], ["st%d%d" % (k, t)], scale=0.0)
-    own_mask("y1", 0, bank(5, H), ["#5"])
-    qz("s", 0, 128, T.st[:, 0:512], ["st0%d" % t for t in range(4)], ["qs0"])
+        act(lane_of(0, t), v("b16"))
+    ms(v("et"), 0.0)
+    ms(v("b8"), 0.0)
+    ts(L(LSW, 24), v("tf", 0, 24), col(8), A.add)
+    qz("u", 0, 128, v("ut"))
+    qz("x0", 0, H, v("xt", 0, 768))
+    cp(v("qus", 0, 128), at(v("qu"), L(LU, 8)), dt.uint32)
+    act(v("sus", 0, 128), at(v("su"), L(LU, 8)))
+    mm(5, "us", 0, "x0", 0, H)
+    qz("x0", H, C, v("xt", 768, 1536))
+    cp(v("qus", 128, 256), at(v("qu"), L(LU + 8, 8)), dt.uint32)
+    act(v("sus", 128, 256), at(v("su"), L(LU + 8, 8)))
+    act(v("cs"), at(v("c16", 32, 48), L(LP, 24)))
+    own_mask("y1", 0, bank(5, H))
+    qz("s", 0, 128, v("st", 0, 512))
 
     def constants_g():
-        iota(T.lr[:], [[1, 17], [0, 2]], -1, 0, ["lr"])
-        iota(T.slot[:], [[0, 4], [1, 17], [0, 2]], 0, 0, ["slot"], True)
         eye = [[-1, 128]]
-        sel(T.b8[:], T.b8[:], [[8, 16], [0, 8]], A.is_gt, 1.0, 0, -1, ["b8"], ["b8"])
-        sel(T.b8[:], T.b8[:], [[8, 16], [0, 8]], A.is_ge, 0.0, 7, -1, ["b8"], ["b8"])
-        sel(lane_of(2, 1), lane_of(2, 1), eye, A.not_equal, B, 0, 1, ["st21"], ["st21"])
-        sel(lane_of(3, 3), lane_of(3, 3), eye, A.not_equal, B, 0, 1, ["st33"], ["st33"])
-        sel(T.et[:, 3:515:4], T.et[:, 3:515:4], eye, A.not_equal, 32.0, 0, 1, ["et"], ["et"])
-        sel(T.jm[:], T.b8[:], [[1, 128]], A.is_ge, 0.0, 0, -1, ["b8"], ["jm"])
-        sel(lane_of(4, 2), T.jm[:], eye, A.not_equal, 16.0, 0, 1, ["jm"], ["st42"])
+        iota(v("slot"), [[0, 4], [1, 17], [0, 2]], 0)
+        sel(v("b8"), v("b8"), [[8, 16], [0, 8]], A.is_gt, 1.0, 0, -1)
+        sel(v("b8"), v("b8"), [[8, 16], [0, 8]], A.is_ge, 0.0, 7, -1)
+        sel(v("et", 3, 515, 4), v("et", 3, 515, 4), eye, A.not_equal, 32.0, 0, 1)
+        sel(v("jm"), v("b8"), [[1, 128]], A.is_ge, 0.0, 0, -1)
+        iota(v("rows", 0, W), [[0, W]], H)
+        for q in range(3):
+            iota(v("rows", 34 * q + 2, 34 * q + 34), [[16, 2], [1, 8], [32, 2]], 64 * q)
+        iota(v("rows", W, W + WU), [[64, 3], [0, 17], [32, 2]], 15)
+        iota(v("rows", W + WU, 2 * W), [[0, W - WU]], 15)
+        iota(v("rows", 2 * W, 2 * W + WU), [[34, 3], [0, 17], [1, 2]], 0)
+        iota(v("rows", 2 * W + WU, 3 * W), [[0, W - WU]], 0)
+        for s in range(2):
+            iota(v("rows", 3 * W + 12 * s, 3 * W + 12 + 12 * s), [[34, 3], [1, 2], [W, 2]], 2 * W * s + 32)
+            iota(v("cb", 136 * s, 136 * s + 136), [[64, 4], [0, 17], [32, 2]], 192 * s - 1)
+        iota(v("rows", 3 * W + 24, 3 * W + 32), [[0, 8]], 32)
+        sel(v("cb"), v("cb"), [[0, 8], [1, 17], [0, 2]], A.is_equal, -K, 0, 0)
+        for b, pat in enumerate(([[0, 4], [1, 2], [0, 4]], [[0, 2], [1, 2], [0, 8]], [[1, 2], [0, 16]])):
+            iota(v("kx", 32 * b, 32 * b + 32), pat, 0)
+
+    def constants_g2():
+        eye = [[-1, 128]]
+        sel(lane_of(3, 1), lane_of(3, 1), eye, A.not_equal, B, 0, 1)
+        sel(lane_of(4, 3), lane_of(4, 3), eye, A.not_equal, B, 0, 1)
+        sel(lane_of(5, 2), v("jm"), eye, A.not_equal, 16.0, 0, 1)
 
     def constants_a():
-        for k, sg in ((1, B), (2, -B), (3, -B)):
-            for t in (0, 2):
-                act(lane_of(k, t), T.b8[:], F.Copy, ["b8"], ["st%d%d" % (k, t)], scale=sg)
-        for h in range(2):
-            act(T.mw[:, h * W:(h + 1) * W], T.slot[:, 0:W], F.Sign, ["slot"], ["mw%d" % h])
-        act(T.rst[:], T.mw[:], F.Identity, ["mw0", "mw1"], ["rst"], scale=-B, bias=B)
+        for k, t in ((3, 1), (4, 3), (1, 1), (1, 2), (1, 3), (2, 1), (2, 3), (3, 3), (4, 1), (5, 0), (5, 1), (5, 3)):
+            act(lane_of(k, t), v("b16"), scale=0.0)
+        for k, t, sg in ((1, 0, -B), (2, 0, -B), (2, 2, -B), (3, 0, B), (3, 2, B), (4, 0, B), (4, 2, B)):
+            act(lane_of(k, t), v("b8"), scale=sg)
 
     def lists_v():
-        ts(tf(0), tf(0), col(1), A.add, ["tf0", "cf"], ["tf0"])
-        ts(T.cf[:, 13:14], col(5), 32.0, A.mult, ["cf"], ["cf13"])
-        ts(T.cf[:, 10:11], col(4), -1.0, A.mult, ["cf"], ["cf10"], 1.0, A.add)
-        ts(T.kx[:, 0:34], T.lr[:], 1, A.arith_shift_right, ["lr"], ["kx0"], 1, A.bitwise_and)
-        ts(T.kx[:, 36:70], T.lr[:], 2, A.arith_shift_right, ["lr"], ["kx1"], 1, A.bitwise_and)
-        ts(tf(10), tf(0), 112.0, A.is_ge, ["tf0"], ["tf10"], -112.0, A.mult)
-        ts(tf(2), tf(0), 112.0, A.is_ge, ["tf0"], ["tf2"], 192.0, A.mult)
-        ts(T.kx[:, 72:106], T.lr[:], 3, A.arith_shift_right, ["lr"], ["kx2"], 1, A.bitwise_and)
-        ms(T.aS[:, C:416], 2 * B, ["aSx"])
-        ms(T.oS[:, C:416], 0.0, ["oSx"])
-        tt(tf(1), tf(10), tf(0), A.add, ["tf10", "tf0"], ["tf1"])
-        ts(tf(2), tf(2), col(13), A.add, ["tf2", "cf13"], ["tf2"])
+        m = 3 * W + 32
+        scan(v("rowo", 0, m), v("rows", 0, m), v("cs", 0, m), K, A.min, A.add)
+        ts(col(9), col(3), -1.0, A.mult, 1.0, A.add)
+        for s in range(2):
+            ms(v("aS", 208 * s + H, 208 * s + 208), 2 * B)
+        for c, a, k, d in ((LA0, 0, 7, 0), (LA1, 0, 7, 8), (LBL, W, 7, 0), (LBU, W, 7, 16), (LE, 2 * W, 7, 0), (LH, 3 * W, 2, 0)):
+            ts(L(c, k), v("rowo", a + 15, a + 16 * k, 16), d - K, A.add)
+        ms(v("ky", 0, 2), 0.0)
         for b in range(3):
-            ts(T.ky[:, 36 * b:36 * b + 34], T.kx[:, 36 * b:36 * b + 34], col(5 + b), A.not_equal, ["kx%d" % b, "cf"], ["ky%d" % b], B * 2 ** b, A.mult)
-        ts(tf(3), tf(1), 34.0, A.is_ge, ["tf1"], ["tf3"])
-        ts(tf(4), tf(1), 68.0, A.is_ge, ["tf1"], ["tf4"])
-        ms(T.oa[:, 2 * W:240], 0.0, ["oax"])
-        tt(T.ky[:, 0:34], T.ky[:, 0:34], T.ky[:, 36:70], A.add, ["ky0", "ky1"], ["ky0"])
-        qz("e", 0, 128, T.et[:, 3:515], ["et"], ["qe0"])
-        tt(tf(3), tf(3), tf(4), A.add, ["tf3", "tf4"], ["tf3"])
-        qz("s", 128, 384, T.st[:, 512:1536], ["st%d%d" % (k, t) for k in (1, 2) for t in range(4)], ["qs1"])
-        ts(tf(4), tf(3), 34.0, A.mult, ["tf3", "cf"], ["tf4"], col(5), A.add)
-        ts(tf(5), tf(3), 64.0, A.mult, ["tf3"], ["tf5"])
-        tt(T.ky[:, 0:34], T.ky[:, 0:34], T.ky[:, 72:106], A.add, ["ky0", "ky2"], ["ky0"])
-        qz("e", 128, 256, T.et[:, 2:514], ["et"], ["qe1"])
-        tt(tf(6), tf(1), tf(4), A.subtract, ["tf1", "tf4"], ["tf6"])
-        tt(tf(5), tf(5), tf(2), A.add, ["tf5", "tf2"], ["tf5"])
-        ts(L(LM, 7), tf(4, 7), 32.0, A.add, ["tf4"], ["LM"])
-        cp(L(LE, 7), tf(4, 7), ["tf4"], ["LE"])
-        ts(tf(1), tf(6), 0.0, A.is_equal, ["tf6"], ["tf1"], 384.0, A.mult)
-        ts(tf(2), tf(6), 0.5, A.mult, ["tf6"], ["tf2"], -1.0, A.add)
-        ts(tf(3), tf(6), 18.0, A.is_ge, ["tf6"], ["tf3"], 8.0, A.mult)
-        ts(L(LBL, 14), tf(5), 15.0, A.add, ["tf5"], ["LB"])
-        ts(L(LBU, 14), tf(5), 31.0, A.add, ["tf5"], ["LB2"])
-        tt(tf(2), tf(2), tf(5), A.add, ["tf2", "tf5"], ["tf2"])
-        qz("e", 256, 384, T.et[:, 1:513], ["et"], ["qe2"])
-        tt(tf(2), tf(2), tf(1), A.max, ["tf2", "tf1"], ["tf2"])
-        qz("e", 384, 512, T.et[:, 0:512], ["et"], ["qe3"])
-        tt(tf(3), tf(3), tf(2), A.add, ["tf3", "tf2"], ["tf3"])
-        cp(L(LO0, 14), tf(2), ["tf2"], ["LO0"])
-        ts(L(LO1, 14), tf(2), 16.0, A.add, ["tf2"], ["LO1"])
-        cp(L(LA0, 14), tf(3), ["tf3"], ["LA0"])
-        ts(L(LA1, 14), tf(3), 8.0, A.add, ["tf3"], ["LA1"])
-
-    def late_lists(step):
-        if step == 0:
-            ts(tf(7, 2), tf(0, 2), 12.0, A.is_ge, ["tf0"], ["tf7"], 122.0, A.mult)
-            cp(T.ti[:, 16:18], tf(0, 2), ["tf0"], ["ti1"])
-        elif step == 1:
-            ts(T.cf[:, 14:15], col(5), 112.0, A.mult, ["cf"], ["cf14"], col(6), A.add)
-            ts(T.ti[:, 18:20], T.ti[:, 16:18], 2, A.arith_shift_right, ["ti1"], ["ti2"])
-        elif step == 2:
-            ts(T.tf[:, 116:118], T.ti[:, 18:20], 34.0, A.mult, ["ti2", "cf14"], ["tf7b"], col(14), A.add)
-        elif step == 3:
-            tt(tf(7, 2), tf(7, 2), T.tf[:, 116:118], A.add, ["tf7", "tf7b"], ["tf7"])
-        elif step == 4:
-            ts(L(LH, 2), tf(7, 2), 32.0, A.add, ["tf7"], ["LH"], 447.0, A.min)
-            ts(T.cf[:, 11:12], col(8), 1.0, A.add, ["cf"], ["cf11"])
+            ts(v("ky", 36 * b + 2, 36 * b + 34), v("kx", 32 * b, 32 * b + 32), col(4 + b), A.not_equal, B * 2 ** b, A.mult)
+        qz("e", 0, 128, v("et", 3, 515))
+        tt(v("ky", 2, 34), v("ky", 2, 34), v("ky", 38, 70), A.add)
+        qz("e", 128, 256, v("et", 2, 514))
+        tt(v("ky", 2, 34), v("ky", 2, 34), v("ky", 74, 106), A.add)
+        qz("e", 256, 384, v("et", 1, 513))
+        qz("e", 384, 512, v("et", 0, 512))
+        ms(v("tt0"), 0.0)
+        ms(v("tt1"), 0.0)
 
     def seat_of_place(step):
         if step == 0:
-            ts(T.pj[:, 0:24], T.pi[:], 3, A.arith_shift_right, ["pi"], ["pj0"], 1, A.bitwise_and)
-            ts(T.pj[:, 24:48], T.pi[:], 4, A.arith_shift_right, ["pi"], ["pj1"], 1, A.bitwise_and)
+            ts(v("pj", 0, 24), v("pi"), 0, A.arith_shift_right, 8, A.bitwise_and)
+            ts(v("pj", 24, 48), v("pi"), 1, A.arith_shift_right, 8, A.bitwise_and)
         elif step == 1:
-            tt(T.pj[:, 48:72], T.pj[:, 0:24], T.pj[:, 24:48], A.subtract, ["pj0", "pj1"], ["pj2"])
+            tt(v("pj", 48, 72), v("pj", 0, 24), v("pi"), A.add)
         elif step == 2:
-            ts(T.t2[:], T.pj[:, 48:72], 8.0, A.mult, ["pj2"], ["t2"])
-        elif step == 3:
-            tt(T.t2[:], T.t2[:], T.pi[:], A.add, ["t2", "pi"], ["t2"])
+            tt(v("pj", 72, 96), v("pj", 48, 72), v("pj", 24, 48), A.subtract)
         else:
-            cp(T.sp[:], T.t2[:], ["t2"], ["sp"])
+            cp(v("sp"), v("pj", 72, 96))
 
-    def decode_mm(src, b, k):
-        mm(4 + b, "e", 128 * b, src, 0, C, True, True, ["qe%d" % b, k])
+    def decode_mm(src, b):
+        mm(4 + b, "e", 128 * b, src, 0, C)
 
     for r in range(R):
         X, XN, XP = "x%d" % r, "n%d" % r, "p%d" % r
-        KX = ["q%s0" % X, "q%s1" % X]
-        mm(0, "us", 0, X, 0, C, True, True, ["qus", "sus"] + KX)
-        mm(1, "us", 0, X, 0, C, True, True, ["qus", "sus"] + KX)
-        mm(2, "us", 128, X, 0, C, True, True, ["qus", "sus"] + KX)
-        u8 = lambda nm: T[nm][:].bitcast(dt.uint8)
-        send([(prv, u8("q" + X), u8("q" + XN), "an%d" % r), (nxt, u8("q" + X), u8("q" + XP), "ap%d" % r)], KX)
-        send([(prv, T["s" + X][:], T["s" + XN][:], "an%d" % r), (nxt, T["s" + X][:], T["s" + XP][:], "ap%d" % r)], KX)
-        arrive("q" + XN, "an%d" % r, 16)
-        arrive("q" + XP, "ap%d" % r, 16)
+        OW, ON, OP, HW, HP = "ow%d" % r, "on%d" % r, "op%d" % r, "hw%d" % r, "hp%d" % r
+        mm(0, "us", 0, X, 0, C)
+        mm(1, "us", 0, X, 0, C)
+        mm(2, "us", 128, X, 0, C)
+        send([(prv, v("q" + X), v("q" + XN), "an%d" % r), (nxt, v("q" + X), v("q" + XP), "ap%d" % r)], dt.uint8)
+        send([(prv, v("s" + X), v("s" + XN), "an%d" % r), (nxt, v("s" + X), v("s" + XP), "ap%d" % r)])
+        arrive([v("q" + XN), v("s" + XN)], "an%d" % r, 16)
+        arrive([v("q" + XP), v("s" + XP)], "ap%d" % r, 16)
         if r == 0:
             constants_g()
         own_scan("y1", "fs", 0)
         for k in (11, 10, 9, 8):
             cmp(k)
-        own_mask("y1", 1, T.ps[:, hc(1)], ["#0"])
+        own_mask("y1", 1, bank(0, C, H))
         for k in (7, 6, 5):
             cmp(k)
         own_scan("y1", "fs", 1)
         for k in (4, 3, 2, 1):
             cmp(k)
         for i, k in enumerate(KS):
-            act(T.sgn[:, C * i:C * i + 16 * k], bank(1, 16 * k), F.Sign, ["#1", "fsh1"], ["sg%d" % i], scale=-1.0, bias=T.fs[:, 16 * k + 15:16 * k + 16])
+            act(v("sgn", C * i, C * i + 16 * k), bank(1, 16 * k), F.Sign, scale=-1.0, bias=mine(k))
         for i, k in enumerate(KS):
-            act(lane(k, 16 * k), T.sgn[:, C * i:C * i + 16 * k], F.Relu, ["sg%d" % i], [key(k), "rs%d" % k], accum_out=T.rsum[:, k:k + 1])
-        for k in range(20, 11, -1):
+            act(lane(k, 16 * k), v("sgn", C * i, C * i + 16 * k), F.Relu, accum_out=v("rsum", k, k + 1))
+        tile(5)
+        tile(4)
+        tt(lane(24, C), v("fs"), bank(0, C), A.is_ge)
+        for k in range(12, 24 - len(KS)):
             cmp(k)
-        tt(lane(24, C), T.fs[:], bank(0, C), A.is_ge, ["#0"] + both("fs"), [key(24)])
-        for q in (1, 0, 2, 3, 4, 5):
-            tile(q)
-        for q in range(6):
-            mm(4, "s", 0, "c", TO[q], TN[q], q == 0, q == 5, ["qs0", "qc%d" % q])
-        mm(3, "us", 128, XN, 0, C, True, True, ["qus", "sus", "q" + XN])
-        scan(T.seg[:], T.mu[:], lane(24, C), 0.0, A.mult, A.add, ["mu", key(24)], ["seg"])
-        act(T.ma[:], bank(2, C), F.Copy, ["#2"], ["ma"], scale=DS)
-        own("y2", "f2", lambda h: T.ps[:, 2048 + H * h:2048 + H * h + H], ["#4"],
-            between=lambda: tt(T.t1[:], T.c0[:], T.seg[:, 15:C:16], A.subtract, ["c0", "seg"], ["t1"]))
-        tt(T.t1[:], T.t1[:], T.rsum[:], A.subtract, ["t1"] + ["rs%d" % k for k in range(24)], ["t1"])
-        tt(T.pi[:], T.t1[:], T.f2[:, 15:C:16], A.add, ["t1"] + both("f2"), ["pi"])
-        OW, ON, HW, HP = "ow%d" % r, "on%d" % r, "hw%d" % r, "hp%d" % r
-        cp(T.pl[:], T.pi[:], ["pi"], ["pl"])
+            if k in (12, 16, 20):
+                tile((24 - k) // 4)
+            if k == 17:
+                tile(0)
+            if k == 13:
+                scan(v("seg"), v("mu"), lane(24, C), 0.0, A.mult, A.add)
+            if k == 14:
+                tt(v("t1"), v("c0"), v("seg", 15, C, 16), A.subtract)
+        mm(4, "s", 0, "c", TO[0], TN[0], True, False)
+        for q in (5, 4, 3, 2, 1):
+            mm(4, "s", 0, "c", TO[q], TN[q], False, q == 1)
+        mm(3, "us", 128, XN, 0, C)
+        act(v("ma"), bank(2, C), scale=DS)
+        for h in range(2):
+            own_whole("f2", h, bank(4, H * h + H, H * h))
+        tt(v("t1"), v("t1"), v("rsum"), A.subtract)
+        tt(v("pi"), v("t1"), v("f2", 15, C, 16), A.add)
+        cp(v("pl"), v("pi"))
         seat_of_place(0)
         if r == 0:
             constants_a()
-            dma("s", T.qw[:].bitcast(dt.uint8), T.wc[:], "dw", ["pl"], ["qw"])
-            dma("s", T.sw[:], T.ws[:], "dw2", (), ["sw"])
-            dma("s", T.vt[:], T.v[:], "dv", (), ["vt"])
-        cp(T.oS[:, 0:C].indirect(T.pl[:]), T.iof[:], ["iof", "pl"], ["oS"])
+            constants_g2()
+            dma("s", T.qw[:].bitcast(dt.uint8), T.wc[:], "dw", [v("pl")], [v("qw")])
+            dma("s", T.sw[:], T.ws[:], "dw2", (), [v("sw")])
+            dma("s", T.vt[:], T.v[:], "dv", (), [v("vt")])
+        cp(at(v("oS"), v("pl")), v("iof"))
         seat_of_place(1)
-        own("y1", "fs", lambda h: T.oS[:, 0:C].indirect(L(LSW + 12 * h, 12)), ["oS", "LSW"])
-        as_list(OW, "fs", OW)
-        send([(prv, T[OW][:], T[ON][:], "al%d" % r)], both(OW))
-        arrive(ON, "al%d" % r, 8)
-        if r:
-            act(T.tc[:], T.oS[:].indirect(L(LO0, 14)), F.Identity, ["oS", "oSx", "LO0", "cf10"], ["tc"], scale=col(10))
-            act(T.td[:], T.oS[:].indirect(L(LO1, 14)), F.Identity, ["oS", "oSx", "LO1", "cf"], ["td"], scale=col(4))
-        act(T.aS[:, 0:C], T.ma[:].indirect(T[OW][:]), F.Copy, ["ma"] + both(OW), ["aS"])
+        cp(half("y1", 0), at(v("oS"), L(LSW, 12)))
+        act(half("y1", 1), at(v("oS"), L(LSW + 12, 12)))
         seat_of_place(2)
-        if r == 0:
-            lists_v()
-            act(T.mb[:], bank(3, C), F.Copy, ["#3"], ["mb"], scale=DS)
-            for q in range(4):
-                m = min(34, W - 34 * q)
-                act(T.kb[:, 34 * q:34 * q + m], T.ky[:, 0:m], F.Copy, ["ky0"], ["kb%d" % q])
-        else:
-            tt(T.oa[:, 0:2 * W], T.tc[:], T.td[:], A.add, ["tc", "td"], ["oa"])
-            act(T.mb[:], bank(3, C), F.Copy, ["#3"], ["mb"], scale=DS)
-        act(T.ta[:], T.aS[:].indirect(L(LA0, 14)), F.Identity, ["aS", "aSx", "LA0", "cf10"], ["ta"], scale=col(10))
-        act(T.tb[:], T.aS[:].indirect(L(LA1, 14)), F.Identity, ["aS", "aSx", "LA1", "cf"], ["tb"], scale=col(4))
+        for h in range(2):
+            own_whole("fs", h, half("y1", h))
+        for h in range(2):
+            as_list(OW, "fs", h)
+        send([(prv, v(OW), v(ON), "al%d" % r), (nxt, v(OW), v(OP), "ao%d" % r)])
+        arrive([v(ON)], "al%d" % r, 8)
+        arrive([v(OP)], "ao%d" % r, 8)
+        sl = lambda nm, s, m=WU: v(nm, s * W, s * W + m)
+        for s in range(2):
+            act(v("aS", 208 * s, 208 * s + H), at(v("ma"), lhalf(OW, s)))
         seat_of_place(3)
         if r == 0:
-            act(T.kb1[:], T.kb[:], F.Identity, ["kb0", "kb1", "kb2", "kb3"], ["kbm"], bias=-B)
-        else:
-            tt(T.dl[:], T.oa[:, 2:2 * W + 2], T.oa[:, 0:2 * W], A.subtract, ["oa", "oax"], ["dl"])
-            seat_of_place(4)
-            tt(T.aa[:], T.ta[:], T.tb[:], A.add, ["ta", "tb"], ["aa"])
+            lists_v()
+            for h in range(2):
+                act(v("mw", h * W, (h + 1) * W), v("slot", 0, W), F.Sign)
+        for s in range(2):
+            win = v("aS", 208 * s, 208 * s + 208)
+            act(sl("ta", s, W), at(win, L(LA0, 7)), F.Identity, scale=col(9))
+            act(sl("tb", s, W), at(win, L(LA1, 7)), F.Identity, scale=col(3))
+        act(v("mb"), bank(3, C), scale=DS)
         for b in range(4):
-            decode_mm(XP, b, "q" + XP)
-        own("y2", "f2", lambda h: T.mb[:].indirect(T[ON][:, 12 * h:12 * h + 12]), ["mb", ON])
+            decode_mm(XP, b)
         if r == 0:
-            tt(T.aa[:], T.ta[:], T.tb[:], A.add, ["ta", "tb"], ["aa"])
-        tt(T.ee[:, 0:2 * W], T.f2[:].indirect(L(LBL, 14)), T.aa[:], A.subtract, both("f2") + ["LB", "aa"], ["eeL"])
-        tt(T.ee[:, 2 * W:4 * W], T.f2[:].indirect(L(LBU, 14)), T.aa[:], A.subtract, both("f2") + ["LB2", "aa"], ["eeU"])
-        for u, nm in ((0, "L"), (1, "U")):
-            for s in range(2):
-                act(T.dd[:, (2 * s + u) * W:(2 * s + u + 1) * W], T.ee[:, (2 * u + s) * W:(2 * u + s + 1) * W], F.Abs, ["ee" + nm], ["d%s%d" % (nm, s)])
-        if r == 0:
-            seat_of_place(4)
-            act(T.tc[:], T.oS[:].indirect(L(LO0, 14)), F.Identity, ["oS", "oSx", "LO0", "cf10"], ["tc"], scale=col(10))
-            act(T.td[:], T.oS[:].indirect(L(LO1, 14)), F.Identity, ["oS", "oSx", "LO1", "cf"], ["td"], scale=col(4))
-        act(T.ons[:], T.iof[:].indirect(T[ON][:]), F.Copy, ["iof", ON], ["ons"])
+            for q in range(3):
+                act(v("kb", 34 * q, 34 * q + 34), v("ky", 0, 34))
+            act(v("rst"), v("mw"), F.Identity, scale=-B, bias=B)
+            act(v("kb1", 0, WU), v("kb", 0, WU), F.Identity, bias=-B)
+            qz("s", 256, 512, v("st", 1024, 2048))
+        tt(v("aa"), v("ta"), v("tb"), A.add)
+        later = []
+        for b in range(4):
+            act(v("gt", b, 4 * C, 4), bank(4 + b, C), scale=1 / 32)
+            later.append((XN, b))
+        for h in range(2):
+            own_mask("y2", h, at(v("mb"), lhalf(ON, h)))
+        for s in range(2):
+            own_scan("y2", "f2", s)
+        for s in range(2):
+            tt(sl("ee", s, W), at(half("f2", s), L(LBL, 7)), sl("aa", s, W), A.subtract)
+            act(sl("dd", 2 * s), sl("ee", s), F.Abs)
 
-        def zl(s, t):
-            return T["tt%d" % s][:, 8 + t:8 + 4 * W:4]
+        def zl(s, t, a=0, b=WU, step=1):
+            return v("tt%d" % s, 8 + 4 * a + t, 8 + 4 * b, 4 * step)
 
         def head(w, s):
-            o = 2 * s * W
-            vL, dL = T.vv[:, o:o + W], T.dd[:, o:o + W]
-            XL = "#%d" % (2 * s)
+            vL, dL, xL = sl("vv", 2 * s), sl("dd", 2 * s), bank(2 * s, WU)
             if w == 0:
-                tt(vL, dL, T.kb[:], A.max, ["dL%d" % s, "kb0", "kb1", "kb2", "kb3"], ["v0%d" % s])
+                tt(vL, dL, v("kb", 0, WU), A.max)
             elif w == 1:
-                y = T.yy[:, s * W:(s + 1) * W]
-                tt(y, bank(2 * s, W), T.kb1[:], A.add, [XL, "kbm"], ["yy%d" % s])
-                act(zl(s, 1), y, F.Identity, ["yy%d" % s], ["t%dl1" % s], scale=1 / B, bias=-1.0)
+                tt(sl("yy", s), xL, v("kb1", 0, WU), A.add)
+                act(zl(s, 1), sl("yy", s), F.Identity, scale=1 / B, bias=-1.0)
             else:
-                tt(vL, bank(2 * s, W), dL, A.max, [XL, "dL%d" % s], ["v0%d" % s])
+                tt(vL, xL, dL, A.max)
                 if w == SW - 1:
-                    act(zl(s, 1), dL, F.Copy, ["dL%d" % s], ["t%dl1" % s], scale=0.0)
+                    act(zl(s, 1), dL, scale=0.0)
                 else:
-                    act(zl(s, 1), bank(2 * s, W), F.Identity, [XL], ["t%dl1" % s], scale=1 / B, bias=-1.0)
-                    if w >= 7:
-                        act(zl(s, 3), bank(2 * s, W), F.Identity, [XL], ["t%dl3" % s], scale=1 / B, bias=7.0)
-            if w >= 8:
-                tt(T.vv[:, o + W:o + 2 * W], bank(2 * s + 1, W), T.dd[:, o + W:o + 2 * W], A.max, ["#%d" % (2 * s + 1), "dU%d" % s], ["v1%d" % s])
+                    act(zl(s, 1), xL, F.Identity, scale=1 / B, bias=-1.0)
+                    if w == 8:
+                        act(zl(s, 2), xL, F.Relu, scale=-1 / B, bias=-7.0)
+                    if w >= 8:
+                        act(zl(s, 3), xL, F.Identity, scale=1 / B, bias=7.0)
+            if w >= 9:
+                tt(sl("vv", 2 * s + 1), bank(2 * s + 1, WU), sl("dd", 2 * s + 1), A.max)
 
-        def body(w, s, fill=None):
+        def body(w, s):
             if w == 1:
-                o = 2 * s * W
-                tt(T.vv[:, o:o + W], T.yy[:, s * W:(s + 1) * W], T.dd[:, o:o + W], A.max, ["yy%d" % s, "dL%d" % s], ["v0%d" % s])
-            us = range(2 if w >= 8 else 1)
-            for u in us:
-                o = (2 * s + u) * W
-                for nm in ("f", "w"):
-                    for par in range(2):
-                        scan(T["f" + nm][:, o + par:o + W:2], T.rst[:, par:W:2], T.vv[:, o + par:o + W:2], 0.0, A.max, A.min,
-                             ["rst", "v%d%d" % (u, s)], ["%s%d%d%d" % (nm, u, s, par)])
-            if fill:
-                fill()
-            for u in us:
-                c = slice((2 * s + u) * W, (2 * s + u + 1) * W)
-                tt(zl(s, 2 * u), T.fw[:, c].indirect(L(LM, 7)), T.ff[:, c], A.is_lt,
-                   ["%s%d%d%d" % (nm, u, s, par) for nm in "fw" for par in range(2)] + ["LM"], ["t%dl%d" % (s, 2 * u)])
+                tt(sl("vv", 2 * s), sl("yy", s), sl("dd", 2 * s), A.max)
+            o, m = 2 * s * W, (W + WU if w >= 9 else WU)
+            for par in range(2):
+                scan(v("ff", o + par, o + m, 2), v("rst", par, m, 2), v("vv", o + par, o + m, 2), 0.0, A.max, A.min)
+            for u in range(2 if w >= 9 else 1):
+                for i, (par, q) in enumerate([(par, q) for par in range(2) for q in range(3)]):
+                    a = o + u * W + 34 * q + par
+                    out, x, last = zl(s, 2 * u, 34 * q + par, 34 * q + 34, 2), v("ff", a, a + 33, 2), v("ff", a + 32, a + 33)
+                    if i < NV:
+                        ts(out, x, last, A.is_gt, -1.0, A.mult)
+                    else:
+                        act(out, x, F.Sign, scale=-1.0, bias=last)
 
         def tail(w, s):
             nm = "t%d" % s
-            qz(nm, 0, 130, T["tt%d" % s][:], ["t%dl%d" % (s, t) for t in range(4)], ["q" + nm])
-            mm(2 * s, "s", 128, nm, 0, 128, True, False, ["qs1", "q" + nm])
-            mm(2 * s, "s", 256, nm, 2, 128, False, True, ["qs1", "q" + nm])
+            before = 128 if w <= 8 else 256
+            qz(nm, 0, 130, v("tt%d" % s))
+            mm(2 * s, "s", before, nm, 0, 128, True, False)
+            mm(2 * s, "s", 384, nm, 2, 128, False, True)
             if w == SW - 1:
-                mm(2 * s + 1, "s", 512, nm, 2, 128, True, True, ["qs2", "q" + nm])
-            elif w >= 7:
-                mm(2 * s + 1, "s", 128, nm, 0, 128, True, False, ["qs1", "q" + nm])
-                mm(2 * s + 1, "s", 384, nm, 2, 128, False, True, ["qs2", "q" + nm])
+                mm(2 * s + 1, "s", 640, nm, 2, 128)
+            elif w >= 8:
+                mm(2 * s + 1, "s", before, nm, 0, 128, True, False)
+                mm(2 * s + 1, "s", 512, nm, 2, 128, False, True)
 
-        def aside(w):
-            b = w % 4
-            k = "#%d" % (4 + b)
-            if w < 4:
-                act(T.gt[:, b:4 * C:4], bank(4 + b, C), F.Copy, [k], ["gt%d" % b], scale=1 / 32)
-                decode_mm(XN, b, "q" + XN)
-            elif w < 8:
-                act(T.dn[:, b * C:(b + 1) * C], bank(4 + b, C), F.Copy, [k], ["dn%d" % b], scale=1 / 32)
-                if w == 6:
-                    decode_mm("g", 0, "qg")
-                    decode_mm("g", 1, "qg")
-                if w == 7:
-                    decode_mm("g", 2, "qg")
-            else:
-                if w == 8:
-                    decode_mm("g", 3, "qg")
-                act(T.dp[:, b * C:(b + 1) * C], bank(4 + b, C), F.Copy, [k], ["dp%d" % b], scale=1 / 32)
+        def unpack(dst, b, h, then=None):
+            def fn():
+                act(v(dst, b * C + H * h, b * C + H * h + H), bank(4 + b, H * h + H, H * h), scale=1 / 32)
+                if then and h:
+                    later.append((then, b))
+            return fn
+
+        def rows_of(out, win, lst, h):
+            return lambda: act(half(out, h), at(v(win), lst))
+
+        aside = [rows_of("opr", "iof", lhalf(OP, h), h) for h in range(2)] + [rows_of("opn", "opr", L(LSW + 12 * h, 12), h) for h in range(2)]
+        aside += [unpack("dn", b, h, "g") for b in range(4) for h in range(2)]
+        aside += [lambda: [act(sl("dd", 2 * s + 1), sl("ee", 2 + s), F.Abs) for s in range(2)]]
+        aside += [rows_of("ons", "iof", lhalf(ON, h), h) for h in range(2)]
+        aside += [unpack("dp", b, h) for b in range(4) for h in range(2)]
 
         def extras(w, s):
-            if w == 5:
-                qz("g", H * s, H * s + H, T.gt[:, 4 * H * s:4 * H * (s + 1)], ["gt%d" % i for i in range(4)] + ["qg"], ["qg"])
-            if r:
-                return
+            if w == 0:
+                qz("g", H * s, H * s + H, v("gt", 4 * H * s, 4 * H * (s + 1)))
             if w == 2:
-                qz("s", 384 + 128 * s, 512 + 128 * s, T.st[:, 1536 + 512 * s:2048 + 512 * s], ["st%d%d" % (3 + s, t) for t in range(4)] + ["qs2"], ["qs2"])
-            if w == 3:
-                c = slice(s * W, (s + 1) * W)
-                tt(T.oa[:, c], T.tc[:, c], T.td[:, c], A.add, ["tc", "td", "oa"], ["oa"])
-            if w == 4:
-                tt(T.dl[:, s * W:(s + 1) * W], T.oa[:, s * W + 2:(s + 1) * W + 2], T.oa[:, s * W:(s + 1) * W], A.subtract, ["oa", "oax", "dl"], ["dl"])
-            if w == 0 and s:
-                late_lists(0)
-            if w in (6, 7):
-                late_lists(2 * (w - 6) + 1 + s)
+                tt(sl("ee", 2 + s, W), at(half("f2", s), L(LBU, 7)), sl("aa", s, W), A.subtract)
+            if r == 0 and w == 0:
+                if s == 0:
+                    qz("s", 128, 256, v("st", 512, 1024))
+                else:
+                    ms(v("vv", WU, W), 0.0)
+                    ms(v("vv", 2 * W + WU, 3 * W), 0.0)
+            if r == 0 and w == 3:
+                qz("s", 512 + 128 * s, 640 + 128 * s, v("st", 2048 + 512 * s, 2560 + 512 * s))
+            if r == 0 and w == 4:
+                ms(v("ro", s * W + WU, (s + 1) * W), 0.0)
+                if s:
+                    ts(col(10), col(7), 1.0, A.add)
+                else:
+                    ts(col(11), col(3), 16.0, A.mult)
 
         for w in range(SW):
-            head(w, 0)
-            if w:
-                tail(w - 1, 1)
-                aside(w - 1)
-            body(w, 0, lambda: extras(w, 0))
-            head(w, 1)
-            tail(w, 0)
-            body(w, 1, lambda: extras(w, 1))
-
-        sl = lambda nm, s: T[nm][:, s * W:(s + 1) * W]
+            for s in range(2):
+                head(w, s)
+                if w + s:
+                    tail(w - 1 + s, 1 - s)
+                while later:
+                    decode_mm(*later.pop(0))
+                body(w, s)
+                extras(w, s)
+                if aside:
+                    aside.pop(0)()
+        assert not aside
 
         def fin(step, s):
             if step == 0:
-                ts(sl("rr", s), bank(2 * s, W), -1 / B, A.mult, ["#%d" % (2 * s)], ["rr%d" % s], 1.0, A.add)
-                act(sl("ep", s), bank(2 * s + 1, W), F.Identity, ["#%d" % (2 * s + 1), "cf11"], ["ep%d" % s], scale=-1.0, bias=col(11))
+                act(sl("rr", s), bank(2 * s, WU), F.Identity, scale=-1 / B, bias=1.0)
+                act(sl("ep", s), bank(2 * s + 1, WU), F.Identity, bias=col(10))
             elif step == 1:
                 for par in range(2):
-                    c = slice(s * W + par, (s + 1) * W, 2)
-                    scan(T.ro[:, c], T.rr[:, c], T.mw[:, par:W:2], 0.0, A.add, A.mult, ["rr%d" % s, "mw0"], ["ro%d%d" % (s, par)])
+                    c = lambda nm: v(nm, s * W + par, s * W + WU, 2)
+                    scan(c("ro"), c("rr"), v("mw", par, WU, 2), 0.0, A.add, A.mult)
             elif step == 2:
-                tt(sl("g2", s), sl("ep", s).indirect(L(LE, 7)), sl("ro", s), A.is_gt, ["ep%d" % s, "LE", "ro%d0" % s, "ro%d1" % s], ["g2%d" % s])
+                tt(sl("g2", s, W), at(sl("ep", s), L(LE, 7)), sl("ro", s, W), A.is_gt)
             elif step == 3:
-                tt(sl("gu", s), sl("g2", s), zl(s, 2), A.add, ["g2%d" % s, "t%dl2" % s], ["gu%d" % s])
-            elif step == 4:
-                tt(sl("pr", 2 * s + 1), sl("gu", s), sl("dl", s), A.mult, ["gu%d" % s, "dl"], ["prU%d" % s])
-            elif step == 5:
-                o = 2 * s * W
-                for par in range(2):
-                    scan(T.hs[:, o + par:o + 2 * W:2], T.mw[:, par:2 * W:2], T.pr[:, o + par:o + 2 * W:2], 0.0, A.mult, A.add,
-                         ["mw0", "mw1", "prL%d" % s, "prU%d" % s], ["hs%d%d" % (s, par)])
+                tt(sl("gu", s), sl("g2", s), zl(s, 2), A.subtract)
             else:
-                tt(sl("pr", 2 * s), zl(s, 0), sl("dl", s), A.mult, ["t%dl0" % s, "dl"], ["prL%d" % s])
+                u = step - 4
+                for par in range(2):
+                    o = (2 * s + u) * W
+                    flags = v("gu", s * W + par, s * W + WU, 2) if u else zl(s, 0, par, WU, 2)
+                    scan(v("hs", o + par, o + WU, 2), v("cb", 136 * s + par, 136 * s + WU, 2), flags, -K, A.max, A.add if u else A.subtract)
 
         fin(0, 0)
         tail(SW - 1, 1)
-        aside(SW - 1)
-        for step, s in ((1, 0), (6, 0), (2, 0), (0, 1), (3, 0), (1, 1), (6, 1), (2, 1), (4, 0), (3, 1), (5, 0), (4, 1)):
+        fin(0, 1)
+        for step, s in ((4, 0), (1, 0), (4, 1), (2, 0), (1, 1), (3, 0), (2, 1), (5, 0), (3, 1)):
             fin(step, s)
         if r + 1 < R:
-            for s in range(2):
-                ms(zl(s, 2), 0.0, ["t%dl2" % s])
-        else:
-            qz("v", 0, 128, T.vt[:], ["vt"], ["qv"])
+            ms(zl(0, 2), 0.0)
         fin(5, 1)
-        cp(T[HW][:], T.hs[:].indirect(L(LH, 2)), ["hs00", "hs01", "hs10", "hs11", "LH"], [HW])
-        send([(nxt, T[HW][:, 0:24], T[HP][:], "ah%d" % r)], [HW])
-        arrive(HP, "ah%d" % r, 8)
+        if r + 1 < R:
+            ms(zl(1, 2), 0.0)
+        ts(v(HW), at(v("hs"), L(LH, 2)), col(11), A.add)
+        send([(nxt, v(HW, 0, 24), v(HP), "ah%d" % r)])
+        arrive([v(HP)], "ah%d" % r, 8)
         bk = lambda h, b: (4 + b, b)[h]
         for h in range(2):
             for b in range(4):
-                mm(bk(h, b), "e", 128 * b, X, H * h, H, True, False, ["qe%d" % b] + KX)
-        cp(T.wr[:].indirect(T[HW][:, 0:24]), T.ons[:], ["ons", HW], ["wr"])
-        act(T.hr[:], T.iof[:].indirect(T[HP][:]), F.Copy, ["iof", HP], ["hr"])
+                mm(bk(h, b), "e", 128 * b, X, H * h, H, True, False)
+        cp(at(v("wr"), v(HW, 0, 24)), v("ons"))
         if r + 1 == R:
-            dma("s", T.ol[:], T.wr[0:128:16, :], "out_s", ["wr"], ())
-        own("y2", "f2", lambda h: T.wr[:, hc(h)], ["wr"])
-        as_list("wl", "f2", "wl")
+            qz("v", 0, 128, v("vt"))
+        cp(half("wj", 0), at(v("wr"), lhalf("pl", 0)))
+        act(half("wj", 1), at(v("wr"), lhalf("pl", 1)))
+        if r + 1 == R:
+            dma("s", T.ol[:], T.wj[0:128:16, :], "out_s", [v("wj")])
+        for h in range(2):
+            own_whole("f2", h, half("wj", h))
+        for h in range(2):
+            as_list("wl", "f2", h)
+        act(half("hr", 1), at(v("opn"), lhalf(HP, 1)))
+        cp(half("hr", 0), at(v("opn"), lhalf(HP, 0)))
         for h in range(2):
             for b in range(4):
-                act(T.vg[:, b * C + H * h:b * C + H * h + H], T.dn[:, b * C:(b + 1) * C].indirect(T.wl[:, 12 * h:12 * h + 12]), F.Copy,
-                    ["dn%d" % b, "wlh%d" % h], ["vg%d%d" % (h, b)])
-        own("y1", "fs", lambda h: T.hr[:].indirect(T.sp[:, 12 * h:12 * h + 12]), ["hr", "sp"])
-        as_list("hl", "fs", "hl")
+                act(v("vg", b * C + H * h, b * C + H * h + H), at(v("dn", b * C, (b + 1) * C), lhalf("wl", h)))
+        for h in range(2):
+            cp(half("y1", h), at(v("hr"), lhalf("sp", h)))
+        for h in range(2):
+            own_whole("fs", h, half("y1", h))
+        for h in range(2):
+            as_list("hl", "fs", h)
         XO = "x%d" % (r + 1)
 
         def z_half(h, bs):
             for b in bs:
-                tt(T.zt[:, 4 * H * h + b:4 * H * (h + 1):4], T.dp[:, b * C:(b + 1) * C].indirect(T.hl[:, 12 * h:12 * h + 12]),
-                   T.vg[:, b * C + H * h:b * C + H * h + H], A.max, ["dp%d" % b, "hlh%d" % h, "vg%d%d" % (h, b)], ["zt%d%d" % (h, b)])
+                tt(v("zt", 4 * H * h + b, 4 * H * (h + 1), 4), at(v("dp", b * C, (b + 1) * C), lhalf("hl", h)), v("vg", b * C + H * h, b * C + H * h + H), A.max)
 
         def w_half(h):
-            qz("z", H * h, H * h + H, T.zt[:, 4 * H * h:4 * H * (h + 1)], ["zt%d%d" % (h, b) for b in range(4)], ["qz%d" % h])
+            qz("z", H * h, H * h + H, v("zt", 4 * H * h, 4 * H * (h + 1)))
             for b in range(4):
-                mm(bk(h, b), "w", 128 * b, "z", H * h, H, False, True, ["qw", "sw", "qz%d" % h])
+                mm(bk(h, b), "w", 128 * b, "z", H * h, H, False, True)
             for b in range(4):
-                out, k = T.xn[:, 4 * H * h + b:4 * H * (h + 1):4], "#%d" % bk(h, b)
                 if h == 0 or b % 2:
-                    act(out, bank(bk(h, b), H), F.Copy, [k], ["xn%d%d" % (h, b)], scale=0.03125)
+                    act(v("xn", 4 * H * h + b, 4 * H * (h + 1), 4), bank(bk(h, b), H), scale=0.03125)
 
         def x_half(h):
-            qz(XO, H * h, H * h + H, T.xn[:, 4 * H * h:4 * H * (h + 1)], ["xn%d%d" % (h, b) for b in range(4)], ["q%s%d" % (XO, h)])
+            qz(XO, H * h, H * h + H, v("xn", 4 * H * h, 4 * H * (h + 1)))
+
+        def store(h):
+            c = slice(H * h, H * h + H)
+            dma("s", T.oc[:, 4 * H * h:4 * H * (h + 1)], T.qx2[:, c].bitcast(dt.uint8), "out_s", [half("qx2", h)])
 
         z_half(0, range(4))
         z_half(1, [0])
@@ -600,22 +605,24 @@ def rank_program(g, core, T, topo):
         w_half(1)
         x_half(0)
         if r + 1 < R:
-            half_scores(XO)
+            mm(5, "us", 0, XO, 0, H)
         else:
-            mm(4, "v", 0, "x2", 0, H, True, True, ["qv", "qx20"])
+            mm(4, "v", 0, "x2", 0, H)
+            store(0)
         for b in (0, 2):
-            ts(T.xn[:, 4 * H + b:8 * H:4], bank(b, H), 0.03125, A.mult, ["#%d" % b], ["xn1%d" % b])
+            ts(v("xn", 4 * H + b, 8 * H, 4), bank(b, H), 0.03125, A.mult)
         if r + 1 < R:
-            own_mask("y1", 0, bank(5, H), ["#5"])
+            own_mask("y1", 0, bank(5, H))
         x_half(1)
 
-    mm(5, "v", 0, "x2", H, H, True, True, ["qv", "qx21"])
-    act(T.yo[:, 0:H], bank(4, H), F.Copy, ["#4"], ["yo0"])
-    dma("s", T.oc[:], T.qx2[:].bitcast(dt.uint8), "out_s", ["qx20", "qx21"], ())
-    cp(T.yo[:, H:C], bank(5, H), ["#5"], ["yo1"])
+    mm(5, "v", 0, "x2", H, H)
+    act(half("yo", 0), bank(4, H))
+    dma("a", T.y[:, 0:H], T.yo[:, 0:H], "out_a", [half("yo", 0)])
+    store(1)
+    cp(half("yo", 1), bank(5, H))
     for k in range(4):
-        dma("a" if k % 2 else "s", T.osc[4 * k:4 * k + 4, :], T.sx2[32 * k:32 * k + 4, :], "out_a" if k % 2 else "out_s", ["qx20", "qx21"], ())
-    dma("a", T.y[:], T.yo[:], "out_a", ["yo0", "yo1"], ())
+        dma("a" if k % 2 else "s", T.osc[4 * k:4 * k + 4, :], T.sx2[32 * k:32 * k + 4, :], "out_a" if k % 2 else "out_s", [v("sx2")])
+    dma("a", T.y[:, H:C], T.yo[:, H:C], "out_a", [half("yo", 1)])
 
     chan = lambda i: ops[i][3] if ops[i][3] else "e" + ops[i][0]
     known = {e: {} for e in ENG}

@@ -16,8 +16,15 @@ K = 1024.0
 TN = [384, 320, 256, 192, 128, 128]
 TO = [0, 384, 704, 960, 1152, 1280]
 KS = (23, 22, 21)
+LAST = ((0, 256), (256, C))
+FIRST = ((0, H), (H, C))
+EARLY = (11, 10, 9, 8, 7, 6, 5)
+XV = (0, 2)
 NV = 3
-LU, LP, LSW, LA0, LA1, LBL, LBU, LE, LH = 0, 16, 40, 64, 72, 80, 88, 96, 104
+CYCLE, PE_CYCLE, GATHER, SCATTER, WAKE, DMA_LAG, LIST_LAG, TILE_LAG = 0.0009, 0.0006, 1.7, 3.8, 0.19, 3.0, 2.2, 8.0
+SLIP = 0.1
+LEAD = (0.8, 0.7, 0.0, 1.0)
+LU, LP, LSW, LEO, LEI, LES, LE, LH = 0, 16, 40, 64, 88, 112, 136, 144
 
 Q4, U8, F32, BF, I32, U16 = "float8_e4m3fn_x4", "uint8", "float32", "bfloat16", "int32", "uint16"
 SCRATCH = {"ps": ("psum", [128, 4096], F32)}
@@ -28,28 +35,28 @@ def _sb(name, n, d):
 
 
 for _n, _w in (("qu", 128), ("qus", 256), ("qv", 128), ("qw", 512), ("qx0", C), ("qx1", C), ("qx2", C), ("qn0", C), ("qn1", C),
-               ("qp0", C), ("qp1", C), ("qg", C), ("qz", C), ("qc", 1408), ("qt0", 130), ("qt1", 130), ("qe", 512), ("qs", 768)):
+               ("qp0", C), ("qp1", C), ("qg", C), ("qz", C), ("qc", 1408), ("qt0", 130), ("qt1", 130), ("qe", 512), ("qs", 1024)):
     _sb(_n, _w, Q4)
     _sb("s" + _n[1:], _w, U8)
 for _n, _w in (("xt", 4 * C), ("ut", 512), ("vt", 512), ("xn", 4 * C), ("gt", 4 * C), ("zt", 4 * C), ("ct", 4 * 1408), ("tt0", 520), ("tt1", 520),
-               ("et", 516), ("st", 3072), ("dn", 4 * C), ("dp", 4 * C), ("vg", 4 * C), ("sgn", 4 * C), ("junk", 3360), ("mu", C), ("seg", C)):
+               ("et", 516), ("st", 4096), ("dn", 4 * C), ("dp", 4 * C), ("vg", 4 * C), ("sgn", 4 * C), ("junk", 3360), ("mu", C), ("seg", C)):
     _sb(_n, _w, BF)
-for _n, _w in (("iof", C), ("cap", C), ("rho", C), ("cs", C), ("c0", 24), ("cf", 16), ("c16", 64), ("jm", 128), ("b16", 128), ("b8", 128),
+for _n, _w in (("iof", C), ("cap", C), ("rho", C), ("cs", C), ("cs2", C), ("bS", C), ("c0", 24), ("cf", 16), ("c16", 64), ("jm", 128), ("b16", 128), ("b8", 128),
                ("kb", W), ("kb1", W), ("kx", 96), ("ky", 144), ("slot", 136), ("rst", 2 * W), ("mw", 2 * W), ("cb", 272), ("rows", C), ("rowo", C),
-               ("tf", 32), ("y1", C), ("fs", C), ("rsum", 24), ("t1", 24), ("y2", C), ("f2", C), ("ma", C), ("mb", C), ("aS", 416), ("oS", C),
-               ("ons", C), ("opr", C), ("opn", C), ("ta", 2 * W), ("tb", 2 * W), ("aa", 2 * W), ("ee", 4 * W), ("dd", 4 * W), ("vv", 4 * W), ("ff", 4 * W),
-               ("yy", 2 * W), ("rr", 2 * W), ("ro", 2 * W), ("ep", 2 * W), ("g2", 2 * W), ("gu", 2 * W), ("hs", 4 * W),
+               ("tf", 96), ("y1", C), ("fs", C), ("rsum", 24), ("t1", 24), ("y2", C), ("f2", C), ("fb", C), ("ma", C), ("mb", C), ("oS", C),
+               ("onr", C), ("ons", C), ("opr", C), ("opn", C), ("ta", 3 * H), ("dd", 4 * W), ("vv", 4 * W), ("ff", 4 * W),
+               ("yy", 2 * W), ("rr", 2 * W), ("ro", 2 * W), ("ep", 2 * W), ("g2", 2 * W), ("hs", 4 * W),
                ("wr", C), ("wj", C), ("hr", C), ("yo", C)):
     _sb(_n, _w, F32)
 for _n, _w in (("ci", 16), ("ti", 16), ("pi", 24), ("pj", 96)):
     _sb(_n, _w, I32)
-for _n, _w in (("lst", 136), ("pl", 24), ("ow0", 24), ("ow1", 24), ("on0", 24), ("on1", 24), ("op0", 24), ("op1", 24), ("hw0", 32), ("hw1", 32),
+for _n, _w in (("lst", 152), ("pl0", 24), ("pl1", 24), ("pn0", 24), ("pn1", 24), ("ow0", 24), ("ow1", 24), ("on0", 24), ("on1", 24), ("op0", 24), ("op1", 24), ("hw0", 32), ("hw1", 32),
                ("hp0", 24), ("hp1", 24), ("sp", 24), ("wl", 24), ("hl", 24)):
     _sb(_n, _w, U16)
 
 ENG = ("v", "a", "t", "g", "s")
 DMAS = ["dx", "dx2", "du", "dv", "dw", "dw2", "out_s", "out_a"]
-ARR = ["an0", "an1", "ap0", "ap1", "al0", "al1", "ao0", "ao1", "ah0", "ah1"]
+ARR = ["an0", "an1", "ap0", "ap1", "al0", "al1", "ao0", "ao1", "ah0", "ah1", "ak0", "ak1"]
 SEMAPHORES = ["ev", "ea", "et", "eg", "sent"] + DMAS + ARR
 
 
@@ -70,7 +77,10 @@ def rank_program(g, core, T, topo):
     Q = {"v": g.vector, "a": g.scalar, "t": g.tensor, "g": g, "s": g.sync}
     V, S, P = g.vector, g.scalar, g.tensor
 
-    ops, seen, sent = [], {}, [0]
+    ops, seen, sent, lead = [], {}, [0], {}
+
+    def ahead(t):
+        lead[len(ops) - 1] = t
 
     def ap(x, cast=None):
         if not isinstance(x, tuple):
@@ -85,8 +95,18 @@ def rank_program(g, core, T, topo):
             return sum(1 << b for b in range(x[1] // 512, (x[2] - 1) // 512 + 1))
         return sum(1 << c for c in range(x[1], x[2], x[3]))
 
-    def add(eng, fn, rd=(), wr=(), sem=None, cnt=None):
-        me, deps = len(ops), set()
+    def size(x):
+        return 16 * (x[4][2] - x[4][1]) if x[4] else len(range(x[1], x[2], x[3]))
+
+    def cost(out, ins, each=1.0, fast=True):
+        if out[4] or ins[0][4]:
+            return 0.06 + (SCATTER * size(out) if out[4] else GATHER * size(ins[0])) * CYCLE
+        if fast and all(SCRATCH[x[0]][2] in (BF, U16) for x in [out] + ins):
+            each /= 2
+        return max(64, each * size(ins[0])) * CYCLE
+
+    def add(eng, fn, rd=(), wr=(), sem=None, cnt=None, busy=0.06, lag=0.0, after=()):
+        me, deps = len(ops), set(after)
         rd = [x for x in rd if isinstance(x, tuple)]
         rd += [x[4] for x in rd + list(wr) if x[4]]
         for x in rd:
@@ -95,62 +115,66 @@ def rank_program(g, core, T, topo):
         for x in wr:
             m = bits(x)
             deps.update(i for i, k, w in seen.get(x[0], ()) if k & m)
-        if eng == "t":
-            deps = {i for i in deps if ops[i][0] != "t"}
-        ops.append((eng, fn, deps, sem, cnt))
+        ops.append((eng, fn, deps, sem, cnt, busy, lag))
         for x in wr:
             m = bits(x)
             seen[x[0]] = [(i, k & ~m, w) for i, k, w in seen.get(x[0], ()) if k & ~m] + [(me, m, True)]
         for x in rd:
             seen.setdefault(x[0], []).append((me, bits(x), False))
+        return me
 
-    def arrive(views, sem, cnt):
-        add("x", None, (), views, sem, cnt)
+    def arrive(views, sem, cnt, call, lag):
+        add("x", None, (), views, sem, cnt, 0.001, lag, [call])
 
     def tt(out, a, b, op):
-        add("v", lambda: V.tensor_tensor(ap(out), ap(a), ap(b), op), [a, b], [out])
+        add("v", lambda: V.tensor_tensor(ap(out), ap(a), ap(b), op), [a, b], [out], busy=cost(out, [a, b], 1.0 if "ps" in (a[0], b[0]) else 2.0, False))
 
     def ts(out, a, s1, op0, s2=None, op1=None):
         if op1 is None:
-            add("v", lambda: V.tensor_scalar(ap(out), ap(a), ap(s1), None, op0), [a, s1], [out])
+            add("v", lambda: V.tensor_scalar(ap(out), ap(a), ap(s1), None, op0), [a, s1], [out], busy=cost(out, [a]))
         else:
-            add("v", lambda: V.tensor_scalar(ap(out), ap(a), ap(s1), ap(s2), op0, op1), [a, s1, s2], [out])
+            add("v", lambda: V.tensor_scalar(ap(out), ap(a), ap(s1), ap(s2), op0, op1), [a, s1, s2], [out], busy=cost(out, [a]))
 
     def cp(out, a, cast=None):
-        add("v", lambda: V.tensor_copy(ap(out, cast), ap(a, cast)), [a], [out])
+        add("v", lambda: V.tensor_copy(ap(out, cast), ap(a, cast)), [a], [out], busy=cost(out, [a]))
 
     def scan(out, d0, d1, init, op0, op1):
-        add("v", lambda: V.tensor_tensor_scan(ap(out), ap(d0), ap(d1), init, op0, op1), [d0, d1], [out])
+        add("v", lambda: V.tensor_tensor_scan(ap(out), ap(d0), ap(d1), init, op0, op1), [d0, d1], [out], busy=cost(out, [d0, d1]))
 
-    def ms(out, c):
-        add("v", lambda: V.memset(ap(out), c), (), [out])
+    def ms(out, c, parts=1):
+        k = (out[2] - out[1]) // parts
+        for x in [out] if parts == 1 else [v(out[0], out[1] + k * i, out[1] + k * i + k) for i in range(parts)]:
+            add("v", lambda x=x: V.memset(ap(x), c), (), [x], busy=cost(x, [x]))
 
     def act(out, a, f=F.Copy, **kw):
         acc = [kw["accum_out"]] if "accum_out" in kw else []
-        add("a", lambda: S.activation(ap(out), ap(a), f, **{k: ap(x) for k, x in kw.items()}), [a, kw.get("bias"), kw.get("scale")], [out] + acc)
+        add("a", lambda: S.activation(ap(out), ap(a), f, **{k: ap(x) for k, x in kw.items()}), [a, kw.get("bias"), kw.get("scale")], [out] + acc,
+            busy=cost(out, [a], 1.0, False) + 0.02 * len(acc))
 
     def qz(name, c0, c1, src):
         q, s = v("q" + name, c0, c1), v("s" + name, c0, c1)
-        add("v", lambda: V.quantize_mx(ap(q), ap(s), ap(src)), [src], [q, s])
+        add("v", lambda: V.quantize_mx(ap(q), ap(s), ap(src)), [src], [q, s], busy=0.012 + 0.00022 * size(src))
 
     def bank(b, m, a=0):
         return v("ps", 512 * b + a, 512 * b + m)
 
     def mm(bk, st, s0, mv, m0, m, start=True, stop=True):
         x = [v("q" + st, s0, s0 + 128), v("s" + st, s0, s0 + 128), v("q" + mv, m0, m0 + m), v("s" + mv, m0, m0 + m)]
-        add("t", lambda: P.matmul_mx(ap(bank(bk, m)), ap(x[0]), ap(x[1]), ap(x[2]), ap(x[3]), start, stop), x, [bank(bk, m)])
+        add("t", lambda: P.matmul_mx(ap(bank(bk, m)), ap(x[0]), ap(x[1]), ap(x[2]), ap(x[3]), start, stop), x, [bank(bk, m)],
+            busy=(m + 16) * PE_CYCLE)
 
     def iota(out, pat, base, cm=0):
+        busy = 0.13 + 2 * size(out) * CYCLE
         if SCRATCH[out[0]][2] == I32:
-            add("g", lambda: g.iota(ap(out), pat, base, cm), (), [out])
+            add("g", lambda: g.iota(ap(out), pat, base, cm), (), [out], busy=busy)
         else:
-            add("g", lambda: g.iota(ap(out), pat, base, cm, allow_small_or_imprecise_dtypes=True), (), [out])
+            add("g", lambda: g.iota(ap(out), pat, base, cm, allow_small_or_imprecise_dtypes=True), (), [out], busy=busy)
 
     def sel(out, a, pat, op, fill, base, cm):
-        add("g", lambda: g.affine_select(ap(out), ap(a), pat, op, fill, base, cm), [a], [out])
+        add("g", lambda: g.affine_select(ap(out), ap(a), pat, op, fill, base, cm), [a], [out], busy=0.17 + 2 * size(out) * CYCLE)
 
-    def dma(eng, out, a, sem, rd=(), wr=()):
-        add(eng, lambda: Q[eng].dma_start(out, a), rd, wr, sem, 16)
+    def dma(eng, out, a, sem, rd=(), wr=(), more=0.0):
+        add(eng, lambda: Q[eng].dma_start(out, a), rd, wr, sem, 16, lag=DMA_LAG + more)
 
     def L(c, k):
         return v("lst", c, c + k)
@@ -161,7 +185,7 @@ def rank_program(g, core, T, topo):
     mask = {first: sum(1 << e for e in e1), second: sum(1 << e for e in e2)}
     assert len(e1) == 8 and len(e2) == 8
 
-    def send(items, cast=None):
+    def send(items, cast=None, after=()):
         def fn():
             tr = []
             for dst, src, land, sem in items:
@@ -169,13 +193,16 @@ def rank_program(g, core, T, topo):
                 tr.append(RemoteDMATransfer(dst_ids=[DstId(rid=rid, pnc=pid)], dma_engine_mask=mask[dst], remote_sem=T.sem[sem],
                                             src=ap(src, cast), dst=ap(land, cast)))
             g.remote_dma_fused(tr, local_sem=T.sem.sent)
-        add("g", fn, [x[1] for x in items], (), "-")
         sent[0] += 8 * len(items)
+        return add("g", fn, [x[1] for x in items], (), "-", busy=0.4 if sent[0] > 16 else 1.4, after=after)
 
+    PC = FIRST
     col = lambda i: v("cf", i, i + 1)
     lane_of = lambda k, t: v("st", 512 * k + t, 512 * (k + 1), 4)
     half = lambda nm, h: v(nm, H * h, H * h + H)
     lhalf = lambda nm, h: v(nm, 12 * h, 12 * h + 12)
+    piece = lambda nm, h, o=0: v(nm, o + PC[h][0], o + PC[h][1])
+    lpiece = lambda nm, h: v(nm, PC[h][0] // 16, PC[h][1] // 16)
     ends = lambda nm, h: v(nm, H * h + 15, H * h + H, 16)
 
     def own_mask(y, h, src):
@@ -193,23 +220,26 @@ def rank_program(g, core, T, topo):
     lane = lambda k, m: v("ct", 4 * TO[(24 - k) // 4] + (24 - k) % 4, 4 * (TO[(24 - k) // 4] + m), 4)
     mine = lambda k: v("fs", 16 * k + 15, 16 * k + 16)
 
-    def cmp(k):
-        ts(lane(k, 16 * k), bank(0 if k >= 12 else 5, 16 * k), mine(k), A.is_lt)
+    def cmp(k, b):
+        ts(lane(k, 16 * k), bank(b, 16 * k), mine(k), A.is_lt)
         act(v("junk", 8 * k * (k - 1), 8 * k * (k + 1)), lane(k, 16 * k), accum_out=v("rsum", k, k + 1))
 
     def tile(q):
         qz("c", TO[q], TO[q] + TN[q], v("ct", 4 * TO[q], 4 * (TO[q] + TN[q])))
 
-    dma("s", T.xt[:, 0:768], T.x[:, 0:768], "dx", (), [v("xt", 0, 768)])
+    cut = 4 * PC[0][1]
+    dma("s", T.xt[:, 0:cut], T.x[:, 0:cut], "dx", (), [v("xt", 0, cut)], 0.4)
     dma("a", T.ut[:], T.u[:], "du", (), [v("ut")])
-    dma("a", T.xt[:, 768:1536], T.x[:, 768:1536], "dx2", (), [v("xt", 768, 1536)])
+    ahead(1.0)
+    dma("a", T.xt[:, cut:4 * C], T.x[:, cut:4 * C], "dx2", (), [v("xt", cut, 4 * C)], 0.5)
 
     iota(v("ci", 0, 1), [[0, 1]], 0, 1)
     iota(v("ti"), [[1, 2], [16, 8]], 0)
     iota(v("c16", 0, 16), [[1, 16]], 0)
     iota(v("jm"), [[1, 8], [0, 16]], 0)
-    iota(v("c0"), [[16, 24]], 15 - int(K))
+    iota(v("c0"), [[16, 24]], 15)
     iota(v("tf", 0, 24), [[32, 12], [8, 2]], 0)
+    iota(v("tf", 24, 48), [[H, 2], [16, 2], [32, 6]], 0)
     iota(v("iof"), [[1, C]], 0)
     ms(v("mu"), 1.0)
     ms(v("c16", 48, 64), 0.0)
@@ -236,20 +266,25 @@ def rank_program(g, core, T, topo):
     tt(v("c16", 32, 48), v("c16", 32, 48), v("c16", 48, 64), A.add)
     for t in range(4):
         act(lane_of(0, t), v("b16"))
-    ms(v("et"), 0.0)
+    ms(v("et"), 0.0, 2)
     ms(v("b8"), 0.0)
     ts(L(LSW, 24), v("tf", 0, 24), col(8), A.add)
+    ts(L(LEO, 24), v("tf", 24, 48), col(1), A.add)
+    ts(v("c0"), v("c0"), v("c16", 47, 48), A.add)
+    ms(v("st", 512, 2560), 0.0, 8)
+    act(v("cs"), at(v("c16", 32, 48), L(LP, 24)))
     qz("u", 0, 128, v("ut"))
-    qz("x0", 0, H, v("xt", 0, 768))
+    qz("x0", 0, PC[0][1], v("xt", 0, 4 * PC[0][1]))
     cp(v("qus", 0, 128), at(v("qu"), L(LU, 8)), dt.uint32)
     act(v("sus", 0, 128), at(v("su"), L(LU, 8)))
-    mm(5, "us", 0, "x0", 0, H)
-    qz("x0", H, C, v("xt", 768, 1536))
+    mm(5, "us", 0, "x0", 0, PC[0][1])
+    qz("x0", PC[1][0], C, v("xt", 4 * PC[1][0], 4 * C))
     cp(v("qus", 128, 256), at(v("qu"), L(LU + 8, 8)), dt.uint32)
     act(v("sus", 128, 256), at(v("su"), L(LU + 8, 8)))
-    act(v("cs"), at(v("c16", 32, 48), L(LP, 24)))
-    own_mask("y1", 0, bank(5, H))
+    act(v("cs2"), v("cs"))
+    tt(piece("y1", 0), bank(5, PC[0][1]), piece("cap", 0), A.min)
     qz("s", 0, 128, v("st", 0, 512))
+    scan(piece("fs", 0), piece("rho", 0), piece("y1", 0), -BIG, A.min, A.max)
 
     def constants_g():
         eye = [[-1, 128]]
@@ -258,41 +293,43 @@ def rank_program(g, core, T, topo):
         sel(v("b8"), v("b8"), [[8, 16], [0, 8]], A.is_ge, 0.0, 7, -1)
         sel(v("et", 3, 515, 4), v("et", 3, 515, 4), eye, A.not_equal, 32.0, 0, 1)
         sel(v("jm"), v("b8"), [[1, 128]], A.is_ge, 0.0, 0, -1)
-        iota(v("rows", 0, W), [[0, W]], H)
-        for q in range(3):
-            iota(v("rows", 34 * q + 2, 34 * q + 34), [[16, 2], [1, 8], [32, 2]], 64 * q)
-        iota(v("rows", W, W + WU), [[64, 3], [0, 17], [32, 2]], 15)
-        iota(v("rows", W + WU, 2 * W), [[0, W - WU]], 15)
-        iota(v("rows", 2 * W, 2 * W + WU), [[34, 3], [0, 17], [1, 2]], 0)
-        iota(v("rows", 2 * W + WU, 3 * W), [[0, W - WU]], 0)
+        iota(v("rows", 0, WU), [[34, 3], [0, 17], [1, 2]], 0)
+        iota(v("rows", WU, W), [[0, W - WU]], 0)
         for s in range(2):
-            iota(v("rows", 3 * W + 12 * s, 3 * W + 12 + 12 * s), [[34, 3], [1, 2], [W, 2]], 2 * W * s + 32)
+            iota(v("rows", W + 12 * s, W + 12 + 12 * s), [[34, 3], [1, 2], [W, 2]], 2 * W * s + 32)
             iota(v("cb", 136 * s, 136 * s + 136), [[64, 4], [0, 17], [32, 2]], 192 * s - 1)
-        iota(v("rows", 3 * W + 24, 3 * W + 32), [[0, 8]], 32)
+        iota(v("rows", W + 24, W + 32), [[0, 8]], 32)
+        iota(v("tf", 48, 72), [[H, 2], [16, 6], [96, 2]], 0)
+        iota(v("tf", 72, 96), [[H, 2], [16, 6], [8, 2]], 0)
         sel(v("cb"), v("cb"), [[0, 8], [1, 17], [0, 2]], A.is_equal, -K, 0, 0)
         for b, pat in enumerate(([[0, 4], [1, 2], [0, 4]], [[0, 2], [1, 2], [0, 8]], [[1, 2], [0, 16]])):
             iota(v("kx", 32 * b, 32 * b + 32), pat, 0)
 
-    def constants_g2():
-        eye = [[-1, 128]]
         sel(lane_of(3, 1), lane_of(3, 1), eye, A.not_equal, B, 0, 1)
         sel(lane_of(4, 3), lane_of(4, 3), eye, A.not_equal, B, 0, 1)
-        sel(lane_of(5, 2), v("jm"), eye, A.not_equal, 16.0, 0, 1)
+        sel(lane_of(5, 2), v("jm"), eye, A.not_equal, -8.0, 0, 1)
 
-    def constants_a():
-        for k, t in ((3, 1), (4, 3), (1, 1), (1, 2), (1, 3), (2, 1), (2, 3), (3, 3), (4, 1), (5, 0), (5, 1), (5, 3)):
-            act(lane_of(k, t), v("b16"), scale=0.0)
-        for k, t, sg in ((1, 0, -B), (2, 0, -B), (2, 2, -B), (3, 0, B), (3, 2, B), (4, 0, B), (4, 2, B)):
-            act(lane_of(k, t), v("b8"), scale=sg)
+    def late_tiles():
+        fill = lambda k, t, sg: act(lane_of(k, t), v("b8"), scale=sg)
+        diag = lambda k, x: sel(lane_of(k, 2), lane_of(k, 2), [[-1, 128]], A.not_equal, x, 0, 1)
+        return [lambda: [fill(2, 0, -B), fill(2, 2, -B)], lambda: [fill(4, 0, B), fill(4, 2, B)],
+                lambda: [fill(6, 2, -1.0), diag(6, 16.0), fill(7, 2, 1.0), diag(7, -16.0)],
+                lambda: [fill(5, t, 0.0) for t in (0, 1)], lambda: [fill(5, 3, 0.0), fill(6, 0, -1.0)], lambda: [fill(6, t, 0.0) for t in (1, 3)],
+                lambda: [fill(7, 0, 1.0), fill(7, 1, 0.0)], lambda: fill(7, 3, 0.0)]
 
     def lists_v():
-        m = 3 * W + 32
+        m = W + 32
         scan(v("rowo", 0, m), v("rows", 0, m), v("cs", 0, m), K, A.min, A.add)
         ts(col(9), col(3), -1.0, A.mult, 1.0, A.add)
-        for s in range(2):
-            ms(v("aS", 208 * s + H, 208 * s + 208), 2 * B)
-        for c, a, k, d in ((LA0, 0, 7, 0), (LA1, 0, 7, 8), (LBL, W, 7, 0), (LBU, W, 7, 16), (LE, 2 * W, 7, 0), (LH, 3 * W, 2, 0)):
-            ts(L(c, k), v("rowo", a + 15, a + 16 * k, 16), d - K, A.add)
+        ts(col(12), col(7), -2.0, A.mult, -1.0, A.add)
+        ts(col(13), col(3), 96.0, A.mult, col(7), A.add)
+        ms(v("dd"), 2 * B, 4)
+        for c, a, k in ((LE, 0, 7), (LH, W, 2)):
+            ts(L(c, k), v("rowo", a + 15, a + 16 * k, 16), -K, A.add)
+        ts(L(LEI, 24), v("tf", 48, 72), col(1), A.add)
+        ts(L(LES, 24), v("tf", 72, 96), col(13), A.add)
+
+    def constants_v():
         ms(v("ky", 0, 2), 0.0)
         for b in range(3):
             ts(v("ky", 36 * b + 2, 36 * b + 34), v("kx", 32 * b, 32 * b + 32), col(4 + b), A.not_equal, B * 2 ** b, A.mult)
@@ -302,8 +339,10 @@ def rank_program(g, core, T, topo):
         tt(v("ky", 2, 34), v("ky", 2, 34), v("ky", 74, 106), A.add)
         qz("e", 256, 384, v("et", 1, 513))
         qz("e", 384, 512, v("et", 0, 512))
-        ms(v("tt0"), 0.0)
-        ms(v("tt1"), 0.0)
+        ms(v("tt0"), 0.0, 2)
+        ms(v("tt1"), 0.0, 2)
+        qz("s", 128, 256, v("st", 512, 1024))
+        qz("s", 384, 512, v("st", 1536, 2048))
 
     def seat_of_place(step):
         if step == 0:
@@ -325,100 +364,104 @@ def rank_program(g, core, T, topo):
         mm(0, "us", 0, X, 0, C)
         mm(1, "us", 0, X, 0, C)
         mm(2, "us", 128, X, 0, C)
-        send([(prv, v("q" + X), v("q" + XN), "an%d" % r), (nxt, v("q" + X), v("q" + XP), "ap%d" % r)], dt.uint8)
-        send([(prv, v("s" + X), v("s" + XN), "an%d" % r), (nxt, v("s" + X), v("s" + XP), "ap%d" % r)])
-        arrive([v("q" + XN), v("s" + XN)], "an%d" % r, 16)
-        arrive([v("q" + XP), v("s" + XP)], "ap%d" % r, 16)
+        call = send([(prv, v("q" + X), v("q" + XN), "an%d" % r), (nxt, v("q" + X), v("q" + XP), "ap%d" % r)], dt.uint8)
+        call = send([(prv, v("s" + X), v("s" + XN), "an%d" % r), (nxt, v("s" + X), v("s" + XP), "ap%d" % r)], None, [call])
+        arrive([v("q" + XN), v("s" + XN)], "an%d" % r, 16, call, TILE_LAG)
+        arrive([v("q" + XP), v("s" + XP)], "ap%d" % r, 16, call, TILE_LAG)
         if r == 0:
             constants_g()
-        own_scan("y1", "fs", 0)
-        for k in (11, 10, 9, 8):
-            cmp(k)
-        own_mask("y1", 1, bank(0, C, H))
-        for k in (7, 6, 5):
-            cmp(k)
-        own_scan("y1", "fs", 1)
-        for k in (4, 3, 2, 1):
-            cmp(k)
+        for k in EARLY[:-2]:
+            cmp(k, 5)
+        tt(piece("y1", 1), bank(0, C, PC[1][0]), piece("cap", 1), A.min)
+        cmp(EARLY[-2], 5)
+        scan(piece("fs", 1), piece("rho", 1), piece("y1", 1), -BIG, A.min, A.max)
+        cmp(EARLY[-1], 5)
         for i, k in enumerate(KS):
             act(v("sgn", C * i, C * i + 16 * k), bank(1, 16 * k), F.Sign, scale=-1.0, bias=mine(k))
         for i, k in enumerate(KS):
             act(lane(k, 16 * k), v("sgn", C * i, C * i + 16 * k), F.Relu, accum_out=v("rsum", k, k + 1))
-        tile(5)
-        tile(4)
         tt(lane(24, C), v("fs"), bank(0, C), A.is_ge)
-        for k in range(12, 24 - len(KS)):
-            cmp(k)
-            if k in (12, 16, 20):
-                tile((24 - k) // 4)
-            if k == 17:
-                tile(0)
-            if k == 13:
+        rest = [k for k in range(EARLY[0] + 1, 24) if k not in KS] + list(range(EARLY[-1] - 1, 0, -1))
+        done, order = set(EARLY), []
+        for i, k in enumerate(rest + [None]):
+            full = [q for q in range(1, 6) if q not in order and all(24 - 4 * q - t in done for t in range(4))]
+            if k:
+                cmp(k, 0)
+                done.add(k)
+            if i == 0:
                 scan(v("seg"), v("mu"), lane(24, C), 0.0, A.mult, A.add)
-            if k == 14:
+            if i == 1:
                 tt(v("t1"), v("c0"), v("seg", 15, C, 16), A.subtract)
+            if k == EARLY[-1] - 1:
+                full = [0] + full
+            for q in full:
+                tile(q)
+                order.append(q)
         mm(4, "s", 0, "c", TO[0], TN[0], True, False)
-        for q in (5, 4, 3, 2, 1):
-            mm(4, "s", 0, "c", TO[q], TN[q], False, q == 1)
+        order.remove(0)
+        for q in order:
+            mm(4, "s", 0, "c", TO[q], TN[q], False, q == order[-1])
         mm(3, "us", 128, XN, 0, C)
+        tt(v("cs2", 15, C, 16), v("t1"), v("rsum"), A.subtract)
         act(v("ma"), bank(2, C), scale=DS)
-        for h in range(2):
-            own_whole("f2", h, bank(4, H * h + H, H * h))
-        tt(v("t1"), v("t1"), v("rsum"), A.subtract)
-        tt(v("pi"), v("t1"), v("f2", 15, C, 16), A.add)
-        cp(v("pl"), v("pi"))
-        seat_of_place(0)
+        scan(v("f2"), bank(4, C), v("cs2"), K, A.min, A.add)
+        PL, PN = "pl%d" % r, "pn%d" % r
+        ts(v(PL), v("f2", 15, C, 16), -K, A.add)
+        ts(v("pi"), v("f2", 15, C, 16), -K, A.add)
+        arrive([v(PN)], "ak%d" % r, 8, send([(prv, v(PL), v(PN), "ak%d" % r)]), LIST_LAG)
         if r == 0:
-            constants_a()
-            constants_g2()
-            dma("s", T.qw[:].bitcast(dt.uint8), T.wc[:], "dw", [v("pl")], [v("qw")])
-            dma("s", T.sw[:], T.ws[:], "dw2", (), [v("sw")])
-            dma("s", T.vt[:], T.v[:], "dv", (), [v("vt")])
-        cp(at(v("oS"), v("pl")), v("iof"))
+            for k, t, sg in ((1, 0, -B), (3, 0, B), (3, 2, B)):
+                act(lane_of(k, t), v("b8"), scale=sg)
+            dma("s", T.qw[:].bitcast(dt.uint8), T.wc[:], "dw", [v(PL)], [v("qw")])
+            dma("s", T.sw[:], T.ws[:], "dw2", [v(PL)], [v("sw")])
+            dma("s", T.vt[:], T.v[:], "dv", [v(PL)], [v("vt")])
+            for h in range(2):
+                act(v("mw", h * W, (h + 1) * W), v("slot", 0, W), F.Sign)
+        cp(at(v("oS"), v(PL)), v("iof"))
+        seat_of_place(0)
+        cp(half("y1", 0), at(v("oS"), L(LEO, 12)))
+        act(half("y1", 1), at(v("oS"), L(LEO + 12, 12)))
+        act(v("mb"), bank(3, C), scale=DS)
         seat_of_place(1)
-        cp(half("y1", 0), at(v("oS"), L(LSW, 12)))
-        act(half("y1", 1), at(v("oS"), L(LSW + 12, 12)))
-        seat_of_place(2)
         for h in range(2):
             own_whole("fs", h, half("y1", h))
+        seat_of_place(2)
         for h in range(2):
             as_list(OW, "fs", h)
-        send([(prv, v(OW), v(ON), "al%d" % r), (nxt, v(OW), v(OP), "ao%d" % r)])
-        arrive([v(ON)], "al%d" % r, 8)
-        arrive([v(OP)], "ao%d" % r, 8)
+            ahead(LEAD[3])
+        call = send([(prv, v(OW), v(ON), "al%d" % r), (nxt, v(OW), v(OP), "ao%d" % r)])
+        arrive([v(ON)], "al%d" % r, 8, call, 2 * LIST_LAG)
+        arrive([v(OP)], "ao%d" % r, 8, call, 2 * LIST_LAG)
         sl = lambda nm, s, m=WU: v(nm, s * W, s * W + m)
-        for s in range(2):
-            act(v("aS", 208 * s, 208 * s + H), at(v("ma"), lhalf(OW, s)))
         seat_of_place(3)
         if r == 0:
             lists_v()
-            for h in range(2):
-                act(v("mw", h * W, (h + 1) * W), v("slot", 0, W), F.Sign)
+            constants_v()
         for s in range(2):
-            win = v("aS", 208 * s, 208 * s + 208)
-            act(sl("ta", s, W), at(win, L(LA0, 7)), F.Identity, scale=col(9))
-            act(sl("tb", s, W), at(win, L(LA1, 7)), F.Identity, scale=col(3))
-        act(v("mb"), bank(3, C), scale=DS)
+            part = lambda i: v("ta", H * i + 96 * s, H * i + 96 * s + 96)
+            act(part(1), at(v("ma"), v(OW, 12 * s, 12 * s + 6)), F.Identity, scale=col(9))
+            act(part(2), at(v("ma"), v(OW, 12 * s + 6, 12 * s + 12)), F.Identity, scale=col(3))
+            tt(part(0), part(1), part(2), A.add)
+        cp(at(v("bS"), v(PN)), v("mb"))
         for b in range(4):
             decode_mm(XP, b)
         if r == 0:
             for q in range(3):
-                act(v("kb", 34 * q, 34 * q + 34), v("ky", 0, 34))
+                act(v("kb1", 34 * q, 34 * q + 34), v("ky", 0, 34), F.Identity, bias=-B)
             act(v("rst"), v("mw"), F.Identity, scale=-B, bias=B)
-            act(v("kb1", 0, WU), v("kb", 0, WU), F.Identity, bias=-B)
-            qz("s", 256, 512, v("st", 1024, 2048))
-        tt(v("aa"), v("ta"), v("tb"), A.add)
-        later = []
-        for b in range(4):
-            act(v("gt", b, 4 * C, 4), bank(4 + b, C), scale=1 / 32)
-            later.append((XN, b))
+            act(v("kb", 0, WU), v("slot", 0, WU), F.Sign, bias=col(12))
         for h in range(2):
-            own_mask("y2", h, at(v("mb"), lhalf(ON, h)))
+            own_mask("y2", h, at(v("bS"), L(LSW + 12 * h, 12)))
+            own_scan("y2", "fb", h)
+
+        def distances(s, u):
+            for i in range(6):
+                a, k = (2 * s + u) * W + 34 * (i // 2) + i % 2, 6 * s + i
+                act(v("dd", a + 2, a + 33, 2), v("ta", 16 * k, 16 * k + 16), F.Abs, scale=-1.0, bias=v("fb", 32 * k + 16 * u + 15, 32 * k + 16 * u + 16))
+
         for s in range(2):
-            own_scan("y2", "f2", s)
-        for s in range(2):
-            tt(sl("ee", s, W), at(half("f2", s), L(LBL, 7)), sl("aa", s, W), A.subtract)
-            act(sl("dd", 2 * s), sl("ee", s), F.Abs)
+            distances(s, 0)
+        later = []
 
         def zl(s, t, a=0, b=WU, step=1):
             return v("tt%d" % s, 8 + 4 * a + t, 8 + 4 * b, 4 * step)
@@ -426,7 +469,7 @@ def rank_program(g, core, T, topo):
         def head(w, s):
             vL, dL, xL = sl("vv", 2 * s), sl("dd", 2 * s), bank(2 * s, WU)
             if w == 0:
-                tt(vL, dL, v("kb", 0, WU), A.max)
+                tt(vL, v("dd", 2 * s * W + 2, 2 * s * W + WU + 2), dL, A.is_lt)
             elif w == 1:
                 tt(sl("yy", s), xL, v("kb1", 0, WU), A.add)
                 act(zl(s, 1), sl("yy", s), F.Identity, scale=1 / B, bias=-1.0)
@@ -444,14 +487,17 @@ def rank_program(g, core, T, topo):
                 tt(sl("vv", 2 * s + 1), bank(2 * s + 1, WU), sl("dd", 2 * s + 1), A.max)
 
         def body(w, s):
+            if w == 0:
+                tt(zl(s, 0), sl("vv", 2 * s), v("kb", 0, WU), A.is_gt)
+                return
             if w == 1:
                 tt(sl("vv", 2 * s), sl("yy", s), sl("dd", 2 * s), A.max)
-            o, m = 2 * s * W, (W + WU if w >= 9 else WU)
-            for par in range(2):
-                scan(v("ff", o + par, o + m, 2), v("rst", par, m, 2), v("vv", o + par, o + m, 2), 0.0, A.max, A.min)
             for u in range(2 if w >= 9 else 1):
+                o = (2 * s + u) * W
+                for par in range(2):
+                    scan(v("ff", o + par, o + WU, 2), v("rst", par, WU, 2), v("vv", o + par, o + WU, 2), 0.0, A.max, A.min)
                 for i, (par, q) in enumerate([(par, q) for par in range(2) for q in range(3)]):
-                    a = o + u * W + 34 * q + par
+                    a = o + 34 * q + par
                     out, x, last = zl(s, 2 * u, 34 * q + par, 34 * q + 34, 2), v("ff", a, a + 33, 2), v("ff", a + 32, a + 33)
                     if i < NV:
                         ts(out, x, last, A.is_gt, -1.0, A.mult)
@@ -462,11 +508,16 @@ def rank_program(g, core, T, topo):
             nm = "t%d" % s
             before = 128 if w <= 8 else 256
             qz(nm, 0, 130, v("tt%d" % s))
-            mm(2 * s, "s", before, nm, 0, 128, True, False)
-            mm(2 * s, "s", 384, nm, 2, 128, False, True)
             if w == SW - 1:
+                mm(2 * s, "s", 768, nm, 0, 128, True, False)
+                mm(2 * s, "s", 896, nm, 2, 128, False, True)
                 mm(2 * s + 1, "s", 640, nm, 2, 128)
-            elif w >= 8:
+                return
+            mm(2 * s, "s", before if w else 384, nm, 0, 128, True, False)
+            mm(2 * s, "s", 384 if w else before, nm, 2, 128, False, True)
+            if w == SW - 2 and s == 0:
+                ahead(LEAD[0])
+            if w >= 8:
                 mm(2 * s + 1, "s", before, nm, 0, 128, True, False)
                 mm(2 * s + 1, "s", 512, nm, 2, 128, False, True)
 
@@ -480,31 +531,34 @@ def rank_program(g, core, T, topo):
         def rows_of(out, win, lst, h):
             return lambda: act(half(out, h), at(v(win), lst))
 
-        aside = [rows_of("opr", "iof", lhalf(OP, h), h) for h in range(2)] + [rows_of("opn", "opr", L(LSW + 12 * h, 12), h) for h in range(2)]
-        aside += [unpack("dn", b, h, "g") for b in range(4) for h in range(2)]
-        aside += [lambda: [act(sl("dd", 2 * s + 1), sl("ee", 2 + s), F.Abs) for s in range(2)]]
-        aside += [rows_of("ons", "iof", lhalf(ON, h), h) for h in range(2)]
-        aside += [unpack("dp", b, h) for b in range(4) for h in range(2)]
+        def whole(dst, b, then):
+            def fn():
+                act(v("gt", b, 4 * C, 4) if dst == "gt" else v(dst, b * C, b * C + C), bank(4 + b, C), scale=1 / 32)
+                later.append((then, b))
+            return fn
 
-        def extras(w, s):
-            if w == 0:
-                qz("g", H * s, H * s + H, v("gt", 4 * H * s, 4 * H * (s + 1)))
-            if w == 2:
-                tt(sl("ee", 2 + s, W), at(half("f2", s), L(LBU, 7)), sl("aa", s, W), A.subtract)
-            if r == 0 and w == 0:
-                if s == 0:
-                    qz("s", 128, 256, v("st", 512, 1024))
-                else:
-                    ms(v("vv", WU, W), 0.0)
-                    ms(v("vv", 2 * W + WU, 3 * W), 0.0)
-            if r == 0 and w == 3:
-                qz("s", 512 + 128 * s, 640 + 128 * s, v("st", 2048 + 512 * s, 2560 + 512 * s))
-            if r == 0 and w == 4:
+        aside = [whole("gt", b, XN) for b in range(4)]
+        aside += [rows_of("opr", "iof", lhalf(OP, h), h) for h in range(2)] + [rows_of("opn", "opr", L(LEI + 12 * h, 12), h) for h in range(2)]
+        aside += [whole("dn", b, "g") for b in range(4)]
+        aside += [lambda: [distances(s, 1) for s in range(2)]]
+        aside += [lambda: [rows_of("onr", "iof", lhalf(ON, h), h)() for h in range(2)], lambda: [rows_of("ons", "onr", L(LES + 12 * h, 12), h)() for h in range(2)]]
+        aside += [unpack("dp", b, h) for b in range(4) for h in range(2)]
+        tiles = late_tiles() if r == 0 else []
+
+        def extras(t):
+            if t in (4, 5, 6):
+                qz("g", 128 * (t - 4), 128 * (t - 3), v("gt", 512 * (t - 4), 512 * (t - 3)))
+            if r:
+                return
+            if 9 <= t < 14:
+                k = (4, 2, 5, 6, 7)[t - 9]
+                qz("s", 128 * k, 128 * k + 128, v("st", 512 * k, 512 * k + 512))
+            if t in (14, 15):
+                s = t - 14
                 ms(v("ro", s * W + WU, (s + 1) * W), 0.0)
-                if s:
-                    ts(col(10), col(7), 1.0, A.add)
-                else:
-                    ts(col(11), col(3), 16.0, A.mult)
+            if t == 16:
+                ts(col(10), col(7), 1.0, A.add)
+                ts(col(11), col(3), 16.0, A.mult)
 
         for w in range(SW):
             for s in range(2):
@@ -514,14 +568,16 @@ def rank_program(g, core, T, topo):
                 while later:
                     decode_mm(*later.pop(0))
                 body(w, s)
-                extras(w, s)
+                extras(2 * w + s)
                 if aside:
                     aside.pop(0)()
+                if tiles:
+                    tiles.pop(0)()
         assert not aside
 
         def fin(step, s):
             if step == 0:
-                act(sl("rr", s), bank(2 * s, WU), F.Identity, scale=-1 / B, bias=1.0)
+                act(sl("rr", s), bank(2 * s, WU), F.Identity, scale=-1.0, bias=1.0)
                 act(sl("ep", s), bank(2 * s + 1, WU), F.Identity, bias=col(10))
             elif step == 1:
                 for par in range(2):
@@ -529,37 +585,38 @@ def rank_program(g, core, T, topo):
                     scan(c("ro"), c("rr"), v("mw", par, WU, 2), 0.0, A.add, A.mult)
             elif step == 2:
                 tt(sl("g2", s, W), at(sl("ep", s), L(LE, 7)), sl("ro", s, W), A.is_gt)
-            elif step == 3:
-                tt(sl("gu", s), sl("g2", s), zl(s, 2), A.subtract)
             else:
                 u = step - 4
                 for par in range(2):
                     o = (2 * s + u) * W
-                    flags = v("gu", s * W + par, s * W + WU, 2) if u else zl(s, 0, par, WU, 2)
+                    flags = v("g2", s * W + par, s * W + WU, 2) if u else zl(s, 0, par, WU, 2)
                     scan(v("hs", o + par, o + WU, 2), v("cb", 136 * s + par, 136 * s + WU, 2), flags, -K, A.max, A.add if u else A.subtract)
+                    if s == 0:
+                        ahead(LEAD[2])
 
         fin(0, 0)
         tail(SW - 1, 1)
         fin(0, 1)
-        for step, s in ((4, 0), (1, 0), (4, 1), (2, 0), (1, 1), (3, 0), (2, 1), (5, 0), (3, 1)):
+        for step, s in ((1, 0), (4, 0), (2, 0), (4, 1), (1, 1), (5, 0), (2, 1)):
             fin(step, s)
         if r + 1 < R:
             ms(zl(0, 2), 0.0)
-        fin(5, 1)
-        if r + 1 < R:
             ms(zl(1, 2), 0.0)
+        else:
+            qz("v", 0, 128, v("vt"))
+        fin(5, 1)
         ts(v(HW), at(v("hs"), L(LH, 2)), col(11), A.add)
-        send([(nxt, v(HW, 0, 24), v(HP), "ah%d" % r)])
-        arrive([v(HP)], "ah%d" % r, 8)
+        arrive([v(HP)], "ah%d" % r, 8, send([(nxt, v(HW, 0, 24), v(HP), "ah%d" % r)]), LIST_LAG)
+        if r + 1 == R:
+            PC = LAST
         bk = lambda h, b: (4 + b, b)[h]
+        width = lambda h: PC[h][1] - PC[h][0]
         for h in range(2):
             for b in range(4):
-                mm(bk(h, b), "e", 128 * b, X, H * h, H, True, False)
+                mm(bk(h, b), "e", 128 * b, X, PC[h][0], width(h), True, False)
         cp(at(v("wr"), v(HW, 0, 24)), v("ons"))
-        if r + 1 == R:
-            qz("v", 0, 128, v("vt"))
-        cp(half("wj", 0), at(v("wr"), lhalf("pl", 0)))
-        act(half("wj", 1), at(v("wr"), lhalf("pl", 1)))
+        cp(half("wj", 0), at(v("wr"), lhalf(PL, 0)))
+        act(half("wj", 1), at(v("wr"), lhalf(PL, 1)))
         if r + 1 == R:
             dma("s", T.ol[:], T.wj[0:128:16, :], "out_s", [v("wj")])
         for h in range(2):
@@ -570,7 +627,7 @@ def rank_program(g, core, T, topo):
         cp(half("hr", 0), at(v("opn"), lhalf(HP, 0)))
         for h in range(2):
             for b in range(4):
-                act(v("vg", b * C + H * h, b * C + H * h + H), at(v("dn", b * C, (b + 1) * C), lhalf("wl", h)))
+                act(piece("vg", h, b * C), at(v("dn", b * C, (b + 1) * C), lpiece("wl", h)))
         for h in range(2):
             cp(half("y1", h), at(v("hr"), lhalf("sp", h)))
         for h in range(2):
@@ -578,25 +635,33 @@ def rank_program(g, core, T, topo):
         for h in range(2):
             as_list("hl", "fs", h)
         XO = "x%d" % (r + 1)
+        four = lambda nm, h: v(nm, 4 * PC[h][0], 4 * PC[h][1])
+        elem = lambda nm, h, b: v(nm, 4 * PC[h][0] + b, 4 * PC[h][1], 4)
 
         def z_half(h, bs):
             for b in bs:
-                tt(v("zt", 4 * H * h + b, 4 * H * (h + 1), 4), at(v("dp", b * C, (b + 1) * C), lhalf("hl", h)), v("vg", b * C + H * h, b * C + H * h + H), A.max)
+                tt(elem("zt", h, b), at(v("dp", b * C, (b + 1) * C), lpiece("hl", h)), piece("vg", h, b * C), A.max)
 
         def w_half(h):
-            qz("z", H * h, H * h + H, v("zt", 4 * H * h, 4 * H * (h + 1)))
+            qz("z", PC[h][0], PC[h][1], four("zt", h))
             for b in range(4):
-                mm(bk(h, b), "w", 128 * b, "z", H * h, H, False, True)
+                mm(bk(h, b), "w", 128 * b, "z", PC[h][0], width(h), False, True)
             for b in range(4):
-                if h == 0 or b % 2:
-                    act(v("xn", 4 * H * h + b, 4 * H * (h + 1), 4), bank(bk(h, b), H), scale=0.03125)
+                if h == 0 or b not in XV:
+                    act(elem("xn", h, b), bank(bk(h, b), width(h)), scale=0.03125)
+
+        def x_own():
+            for b in XV:
+                ts(elem("xn", 1, b), bank(bk(1, b), width(1)), 0.03125, A.mult)
 
         def x_half(h):
-            qz(XO, H * h, H * h + H, v("xn", 4 * H * h, 4 * H * (h + 1)))
+            qz(XO, PC[h][0], PC[h][1], four("xn", h))
+            if h == 0:
+                ahead(LEAD[1])
 
         def store(h):
-            c = slice(H * h, H * h + H)
-            dma("s", T.oc[:, 4 * H * h:4 * H * (h + 1)], T.qx2[:, c].bitcast(dt.uint8), "out_s", [half("qx2", h)])
+            a, b = PC[h]
+            dma("s", T.oc[:, 4 * a:4 * b], T.qx2[:, a:b].bitcast(dt.uint8), "out_s", [piece("qx2", h)])
 
         z_half(0, range(4))
         z_half(1, [0])
@@ -605,24 +670,62 @@ def rank_program(g, core, T, topo):
         w_half(1)
         x_half(0)
         if r + 1 < R:
-            mm(5, "us", 0, XO, 0, H)
+            mm(5, "us", 0, XO, 0, width(0))
+            x_own()
+            tt(piece("y1", 0), bank(5, width(0)), piece("cap", 0), A.min)
+            x_half(1)
+            scan(piece("fs", 0), piece("rho", 0), piece("y1", 0), -BIG, A.min, A.max)
         else:
-            mm(4, "v", 0, "x2", 0, H)
+            mm(4, "v", 0, "x2", 0, width(0))
             store(0)
-        for b in (0, 2):
-            ts(v("xn", 4 * H + b, 8 * H, 4), bank(b, H), 0.03125, A.mult)
-        if r + 1 < R:
-            own_mask("y1", 0, bank(5, H))
-        x_half(1)
+            x_own()
+            cp(piece("yo", 0), bank(4, width(0)))
+            dma("s", T.y[:, 0:width(0)], T.yo[:, 0:width(0)], "out_s", [piece("yo", 0)])
+            x_half(1)
 
-    mm(5, "v", 0, "x2", H, H)
-    act(half("yo", 0), bank(4, H))
-    dma("a", T.y[:, 0:H], T.yo[:, 0:H], "out_a", [half("yo", 0)])
+    mm(5, "v", 0, "x2", PC[1][0], width(1))
     store(1)
-    cp(half("yo", 1), bank(5, H))
+    cp(piece("yo", 1), bank(5, width(1)))
     for k in range(4):
         dma("a" if k % 2 else "s", T.osc[4 * k:4 * k + 4, :], T.sx2[32 * k:32 * k + 4, :], "out_a" if k % 2 else "out_s", [v("sx2")])
-    dma("a", T.y[:, H:C], T.yo[:, H:C], "out_a", [half("yo", 1)])
+    dma("a", T.y[:, PC[1][0]:C], T.yo[:, PC[1][0]:C], "out_a", [piece("yo", 1)])
+
+    free = lambda d, i: ops[d][3] == "-" or ops[d][0] == ops[i][0] == "t"
+    gap = lambda d, i: ops[d][5] + ops[d][6] + (0.0 if free(d, i) else WAKE)
+    chain = [op[5] + op[6] for op in ops]
+    for i in reversed(range(len(ops))):
+        chain[i] += lead.get(i, 0.0)
+        for d in ops[i][2]:
+            chain[d] = max(chain[d], gap(d, i) + chain[i])
+    left, users = [len(op[2]) for op in ops], [[] for op in ops]
+    for i, op in enumerate(ops):
+        for d in op[2]:
+            users[d].append(i)
+    ready, idle, order = [0.0] * len(ops), {e: 0.0 for e in ENG + ("x",)}, []
+    open_ = {e: [i for i, op in enumerate(ops) if op[0] == e and not op[2]] for e in idle}
+
+    def choice(e):
+        best, limit = None, 1e9
+        for i in sorted(open_[e], key=lambda i: (-chain[i], i)):
+            t = max(ready[i], idle[e])
+            if best is None or (t < best[0] and t + ops[i][5] <= limit + SLIP):
+                best = (t, i)
+            limit = min(limit, t)
+        return best
+
+    while len(order) < len(ops):
+        t, i = min(choice(e) for e in open_ if open_[e])
+        e = ops[i][0]
+        open_[e].remove(i)
+        idle[e] = t + ops[i][5]
+        order.append(i)
+        for u in users[i]:
+            ready[u] = max(ready[u], t + gap(i, u))
+            left[u] -= 1
+            if not left[u]:
+                open_[ops[u][0]].append(u)
+    new = {i: k for k, i in enumerate(order)}
+    ops = [ops[i][:2] + ({new[d] for d in ops[i][2] if not free(d, i)},) + ops[i][3:5] for i in order]
 
     chan = lambda i: ops[i][3] if ops[i][3] else "e" + ops[i][0]
     known = {e: {} for e in ENG}

@@ -7,23 +7,32 @@ C = 384
 H = 192
 R = 2
 SW = 12
-W = 112
-WU = 102
-B = 2.0 ** 30
-DS = 2.0 ** -42
+NS = 2
+NP = 6 // NS
+WU = 34 * NP
+W = WU + 16 - WU % 16
+B = 2.0 ** 26
+DS = 2.0 ** -46
 BIG = 2.0 ** 90
 K = 1024.0
 TN = [384, 320, 256, 192, 128, 128]
 TO = [0, 384, 704, 960, 1152, 1280]
-KS = (23, 22, 21)
-LAST = ((0, 256), (256, C))
-FIRST = ((0, H), (H, C))
-EARLY = (11, 10, 9, 8, 7, 6, 5)
+QO = (0, 4, 5, 3, 2, 1)
+KS = (23, 22, 21, 20, 19)
+KV = ((16, 15, 14, 13, 12, 11), (16, 15, 14, 13))
+FIRST = ((0, 128), (128, 256), (256, C))
+MID = ((0, H), (H, C))
+LAST = ((0, 128), (128, 256), (256, C))
 XV = (0, 2)
-NV = 3
-CYCLE, PE_CYCLE, GATHER, SCATTER, WAKE, DMA_LAG, LIST_LAG, TILE_LAG = 0.0009, 0.0006, 1.7, 3.8, 0.19, 3.0, 2.2, 8.0
+LB, UB, DB = ((0, 2), (1, 3), (4, 5, 6, 7)) if NS == 2 else ((0, 1, 2), (3, 4, 5), (6, 7, 6, 7))
+CYCLE, PE_CYCLE, GATHER, SCATTER, WAKE, DMA_LAG, LIST_LAG, TILE_LAG = 0.0009, 0.0006, 1.7, 3.8, 0.19, 3.0, 2.0, 7.6
+ACT_START = 0
+HOLD = 15.5
+LOAD = (-0.5, -0.2, 0.1, -0.4, 0.4)
 SLIP = 0.1
-LEAD = (0.8, 0.7, 0.0, 1.0)
+SOON = 4.0
+EARLY = 1.0
+LEAD = (1.0, 0.55, 1.0, 0.5, 1.0, 0.3)
 LU, LP, LSW, LEO, LEI, LES, LE, LH = 0, 16, 40, 64, 88, 112, 136, 144
 
 Q4, U8, F32, BF, I32, U16 = "float8_e4m3fn_x4", "uint8", "float32", "bfloat16", "int32", "uint16"
@@ -35,28 +44,28 @@ def _sb(name, n, d):
 
 
 for _n, _w in (("qu", 128), ("qus", 256), ("qv", 128), ("qw", 512), ("qx0", C), ("qx1", C), ("qx2", C), ("qn0", C), ("qn1", C),
-               ("qp0", C), ("qp1", C), ("qg", C), ("qz", C), ("qc", 1408), ("qt0", 130), ("qt1", 130), ("qe", 512), ("qs", 1024)):
+               ("qp0", C), ("qp1", C), ("qg", C), ("qz", C), ("qc", 1408), ("qf", 132 * NS), ("qe", 512), ("qs", 1024)):
     _sb(_n, _w, Q4)
     _sb("s" + _n[1:], _w, U8)
-for _n, _w in (("xt", 4 * C), ("ut", 512), ("vt", 512), ("xn", 4 * C), ("gt", 4 * C), ("zt", 4 * C), ("ct", 4 * 1408), ("tt0", 520), ("tt1", 520),
-               ("et", 516), ("st", 4096), ("dn", 4 * C), ("dp", 4 * C), ("vg", 4 * C), ("sgn", 4 * C), ("junk", 3360), ("mu", C), ("seg", C)):
+for _n, _w in (("xt", 4 * C), ("ut", 512), ("vt", 512), ("xn", 4 * C), ("gt", 4 * C), ("zt", 4 * C), ("ct", 4 * 1408), ("tt", 520 * NS),
+               ("et", 516), ("st", 4096), ("dn", 4 * C), ("dp", 4 * C), ("vg", 4 * C), ("copy", 4416), ("junk", 256 * 24), ("one", 256), ("mu", C), ("seg", C)):
     _sb(_n, _w, BF)
 for _n, _w in (("iof", C), ("cap", C), ("rho", C), ("cs", C), ("cs2", C), ("bS", C), ("c0", 24), ("cf", 16), ("c16", 64), ("jm", 128), ("b16", 128), ("b8", 128),
-               ("kb", W), ("kb1", W), ("kx", 96), ("ky", 144), ("slot", 136), ("rst", 2 * W), ("mw", 2 * W), ("cb", 272), ("rows", C), ("rowo", C),
-               ("tf", 96), ("y1", C), ("fs", C), ("rsum", 24), ("t1", 24), ("y2", C), ("f2", C), ("fb", C), ("ma", C), ("mb", C), ("oS", C),
-               ("onr", C), ("ons", C), ("opr", C), ("opn", C), ("ta", 3 * H), ("dd", 4 * W), ("vv", 4 * W), ("ff", 4 * W),
-               ("yy", 2 * W), ("rr", 2 * W), ("ro", 2 * W), ("ep", 2 * W), ("g2", 2 * W), ("hs", 4 * W),
+               ("kb", W), ("kb1", W), ("kx", 96), ("ky", 144), ("slot", 136), ("rst", W), ("mw", W), ("cb", NS * WU), ("rows", 320),
+               ("tf", 96), ("y1", C), ("fs", C), ("rsum", 48), ("t1", 24), ("y2", C), ("f2", C), ("fb", C), ("ma", C), ("mb", C), ("oS", C),
+               ("onr", C), ("ons", C), ("opr", C), ("opn", C), ("ta", 3 * H), ("dd", 2 * NS * W), ("vv", 2 * NS * W), ("ff", 2 * NS * W),
+               ("yy", NS * W), ("d1", NS * W), ("rr", NS * W), ("ro", NS * W), ("ep", NS * W), ("g2", NS * W), ("hs", 2 * NS * W),
                ("wr", C), ("wj", C), ("hr", C), ("yo", C)):
     _sb(_n, _w, F32)
 for _n, _w in (("ci", 16), ("ti", 16), ("pi", 24), ("pj", 96)):
     _sb(_n, _w, I32)
-for _n, _w in (("lst", 152), ("pl0", 24), ("pl1", 24), ("pn0", 24), ("pn1", 24), ("ow0", 24), ("ow1", 24), ("on0", 24), ("on1", 24), ("op0", 24), ("op1", 24), ("hw0", 32), ("hw1", 32),
-               ("hp0", 24), ("hp1", 24), ("sp", 24), ("wl", 24), ("hl", 24)):
+for _n, _w in (("lst", 152), ("pl0", 24), ("pl1", 24), ("pn0", 24), ("pn1", 24), ("ow0", 24), ("ow1", 24), ("on0", 24), ("on1", 24), ("op0", 24), ("op1", 24),
+               ("hw0", 32), ("hw1", 32), ("hp0", 32), ("hp1", 32), ("sp", 24), ("wl", 24), ("hl", 24)):
     _sb(_n, _w, U16)
 
 ENG = ("v", "a", "t", "g", "s")
-DMAS = ["dx", "dx2", "du", "dv", "dw", "dw2", "out_s", "out_a"]
-ARR = ["an0", "an1", "ap0", "ap1", "al0", "al1", "ao0", "ao1", "ah0", "ah1", "ak0", "ak1"]
+DMAS = ["dx0", "dx1", "dx2", "du", "dv", "dw", "dw2", "out_s", "out_a"]
+ARR = ["an0", "an1", "ap0", "ap1", "an0z", "an1z", "ap0z", "ap1z", "al0", "al1", "ao0", "ao1", "ah0", "ah1", "aj0", "aj1", "ak0", "ak1"]
 SEMAPHORES = ["ev", "ea", "et", "eg", "sent"] + DMAS + ARR
 
 
@@ -77,7 +86,7 @@ def rank_program(g, core, T, topo):
     Q = {"v": g.vector, "a": g.scalar, "t": g.tensor, "g": g, "s": g.sync}
     V, S, P = g.vector, g.scalar, g.tensor
 
-    ops, seen, sent, lead = [], {}, [0], {}
+    ops, seen, sent, lead, held = [], {}, [0], {}, set()
 
     def ahead(t):
         lead[len(ops) - 1] = t
@@ -149,7 +158,7 @@ def rank_program(g, core, T, topo):
     def act(out, a, f=F.Copy, **kw):
         acc = [kw["accum_out"]] if "accum_out" in kw else []
         add("a", lambda: S.activation(ap(out), ap(a), f, **{k: ap(x) for k, x in kw.items()}), [a, kw.get("bias"), kw.get("scale")], [out] + acc,
-            busy=cost(out, [a], 1.0, False) + 0.02 * len(acc))
+            busy=(cost(out, [a]) if a[4] else max(64, ACT_START + size(a)) * CYCLE) + 0.02 * len(acc))
 
     def qz(name, c0, c1, src):
         q, s = v("q" + name, c0, c1), v("s" + name, c0, c1)
@@ -194,7 +203,16 @@ def rank_program(g, core, T, topo):
                                             src=ap(src, cast), dst=ap(land, cast)))
             g.remote_dma_fused(tr, local_sem=T.sem.sent)
         sent[0] += 8 * len(items)
-        return add("g", fn, [x[1] for x in items], (), "-", busy=0.4 if sent[0] > 16 else 1.4, after=after)
+        return add("g", fn, [x[1] for x in items], (), "-", busy=0.4 if sent[0] > 8 else 1.4, after=after)
+
+    def send_state(dst, src, land, sem, cuts, after=(), more=0.0):
+        for a, b in cuts[:-1]:
+            after = [send([(dst, v("q" + src, a, b), v("q" + land, a, b), sem)], dt.uint8, after)]
+        a, b = cuts[-1]
+        call = send([(dst, v("s" + src), v("s" + land), sem)], None, after)
+        arrive([v("q" + land, 0, a), v("s" + land)], sem, 8 * len(cuts), call, TILE_LAG + more - 1.5)
+        call = send([(dst, v("q" + src, a, b), v("q" + land, a, b), sem + "z")], dt.uint8, [call])
+        arrive([v("q" + land, a, b)], sem + "z", 8, call, TILE_LAG + more - 0.4)
 
     PC = FIRST
     col = lambda i: v("cf", i, i + 1)
@@ -203,492 +221,356 @@ def rank_program(g, core, T, topo):
     lhalf = lambda nm, h: v(nm, 12 * h, 12 * h + 12)
     piece = lambda nm, h, o=0: v(nm, o + PC[h][0], o + PC[h][1])
     lpiece = lambda nm, h: v(nm, PC[h][0] // 16, PC[h][1] // 16)
-    ends = lambda nm, h: v(nm, H * h + 15, H * h + H, 16)
+    width = lambda h: PC[h][1] - PC[h][0]
+    four = lambda nm, h: v(nm, 4 * PC[h][0], 4 * PC[h][1])
+    elem = lambda nm, h, b: v(nm, 4 * PC[h][0] + b, 4 * PC[h][1], 4)
+    sl = lambda nm, s, m=WU: v(nm, s * W, s * W + m)
 
-    def own_mask(y, h, src):
-        tt(half(y, h), src, half("cap", h), A.min)
+    def own(y, f, a, b, src):
+        tt(v(y, a, b), src, v("cap", a, b), A.min)
+        scan(v(f, a, b), v("rho", a, b), v(y, a, b), -BIG, A.min, A.max)
 
-    def own_scan(y, f, h):
-        scan(half(f, h), half("rho", h), half(y, h), -BIG, A.min, A.max)
+    def as_list(out, f, row, a, b):
+        scan(v(f, a, b), v(row, a, b), v("cs", a, b), K, A.min, A.add)
+        ts(v(out, a // 16, b // 16), v(f, a + 15, b, 16), -K, A.add)
 
-    def own_whole(f, h, src):
-        scan(half(f, h), src, half("cs", h), K, A.min, A.add)
+    def picked(out, win, lst):
+        cp(half(out, 0), at(v(win), lst(0)))
+        act(half(out, 1), at(v(win), lst(1)))
 
-    def as_list(out, f, h):
-        ts(lhalf(out, h), ends(f, h), -K, A.add)
-
-    lane = lambda k, m: v("ct", 4 * TO[(24 - k) // 4] + (24 - k) % 4, 4 * (TO[(24 - k) // 4] + m), 4)
+    lane = lambda k, a, b: v("ct", 4 * (TO[(24 - k) // 4] + a) + (24 - k) % 4, 4 * (TO[(24 - k) // 4] + b), 4)
     mine = lambda k: v("fs", 16 * k + 15, 16 * k + 16)
 
-    def cmp(k, b):
-        ts(lane(k, 16 * k), bank(b, 16 * k), mine(k), A.is_lt)
-        act(v("junk", 8 * k * (k - 1), 8 * k * (k + 1)), lane(k, 16 * k), accum_out=v("rsum", k, k + 1))
-
-    def tile(q):
-        qz("c", TO[q], TO[q] + TN[q], v("ct", 4 * TO[q], 4 * (TO[q] + TN[q])))
-
-    cut = 4 * PC[0][1]
-    dma("s", T.xt[:, 0:cut], T.x[:, 0:cut], "dx", (), [v("xt", 0, cut)], 0.4)
-    dma("a", T.ut[:], T.u[:], "du", (), [v("ut")])
-    ahead(1.0)
-    dma("a", T.xt[:, cut:4 * C], T.x[:, cut:4 * C], "dx2", (), [v("xt", cut, 4 * C)], 0.5)
+    for h, (a, b) in enumerate(PC):
+        dma("ssa"[h], T.xt[:, 4 * a:4 * b], T.x[:, 4 * a:4 * b], "dx%d" % h, (), [four("xt", h)], LOAD[h])
+        ahead(2.0 - h)
+    dma("a", T.ut[:], T.u[:], "du", (), [v("ut")], LOAD[3])
+    ahead(3.0)
 
     iota(v("ci", 0, 1), [[0, 1]], 0, 1)
-    iota(v("ti"), [[1, 2], [16, 8]], 0)
-    iota(v("c16", 0, 16), [[1, 16]], 0)
-    iota(v("jm"), [[1, 8], [0, 16]], 0)
-    iota(v("c0"), [[16, 24]], 15)
-    iota(v("tf", 0, 24), [[32, 12], [8, 2]], 0)
-    iota(v("tf", 24, 48), [[H, 2], [16, 2], [32, 6]], 0)
-    iota(v("iof"), [[1, C]], 0)
-    ms(v("mu"), 1.0)
-    ms(v("c16", 48, 64), 0.0)
     for i, (sh, an) in enumerate(((0, 15), (4, 7), (3, 1), (0, 1), (1, 1), (2, 1), (0, 7))):
         ts(v("ci", i + 1, i + 2), v("ci", 0, 1), sh, A.arith_shift_right, an, A.bitwise_and)
-    ms(v("mu", 0, C, 16), 0.0)
-    ms(v("c16", 63, 64), 2 * K)
     cp(v("cf", 0, 8), v("ci", 0, 8))
-    cp(L(LU, 16), v("ti"))
+    ts(col(8), col(3), 8.0, A.mult, col(1), A.add)
+    ts(col(9), col(3), -1.0, A.mult, 1.0, A.add)
+    ts(col(10), col(7), 1.0, A.add)
+    ts(col(11), col(3), 16.0, A.mult)
+    ts(col(12), col(7), -2.0, A.mult, -1.0, A.add)
+    ts(col(13), col(3), 32.0 * NP, A.mult, col(7), A.add)
+    iota(v("iof"), [[1, C]], 0)
+    iota(v("c16", 0, 16), [[1, 16]], 0)
+    iota(v("c0"), [[16, 24]], 15)
+    ms(v("mu"), 1.0)
+    ms(v("one"), 1.0)
+    ms(v("mu", 0, C, 16), 0.0)
+    ms(v("c16", 48, 64), 0.0)
+    ms(v("c16", 63, 64), 2 * K)
     act(v("rho"), v("mu"), F.Identity, scale=2 * BIG, bias=-BIG)
     ts(v("c16", 16, 32), v("c16", 0, 16), col(1), A.is_equal)
     ts(v("c16", 32, 48), v("c16", 0, 16), col(1), A.is_lt)
     ts(L(LP, 24), v("c0"), 0.0, A.mult, col(1), A.add)
-    ts(v("b16"), v("jm"), col(2), A.is_equal)
     tt(v("c16", 32, 48), v("c16", 32, 48), v("c16", 16, 32), A.subtract)
+    ts(v("c16", 32, 48), v("c16", 32, 48), K, A.mult)
+    tt(v("c16", 32, 48), v("c16", 32, 48), v("c16", 48, 64), A.add)
     act(v("cap"), at(v("c16", 16, 32), L(LP, 24)), F.Identity, scale=2 * BIG, bias=-BIG)
+    act(v("cs"), at(v("c16", 32, 48), L(LP, 24)))
+    act(v("cs2"), v("cs"))
+    ts(v("c0"), v("c0"), col(1), A.subtract, v("c16", 47, 48), A.add)
+    ms(v("rsum"), 0.0)
+    ms(v("junk", 255, 256 * 24, 256), 0.0)
     for q in range(6):
         lo = TN[q] - (112 if q == 5 else 48)
         ms(v("ct", 4 * (TO[q] + lo), 4 * (TO[q] + TN[q])), 0.0)
-    ts(v("c16", 32, 48), v("c16", 32, 48), K, A.mult)
-    ms(v("rsum", 0, 1), 0.0)
-    ts(v("c0"), v("c0"), col(1), A.subtract)
-    ts(col(8), col(3), 8.0, A.mult, col(1), A.add)
-    tt(v("c16", 32, 48), v("c16", 32, 48), v("c16", 48, 64), A.add)
+    iota(v("ti"), [[1, 2], [16, 8]], 0)
+    cp(L(LU, 16), v("ti"))
+    for i, (c, pat, k) in enumerate(((LSW, [[8, 2], [32, 12]], 8), (LEO, [[64 * NP, NS], [16, 2], [32, 2 * NP]], 1),
+                                     (LEI, [[64 * NP, NS], [16, 2 * NP], [32 * NP, 2]], 1), (LES, [[8, 2], [64 * NP, NS], [16, 2 * NP]], 13))):
+        iota(v("tf", 24 * i, 24 * i + 24), pat, 0)
+        ts(L(c, 24), v("tf", 24 * i, 24 * i + 24), col(k), A.add)
+    iota(v("rows", 0, WU), [[34, NP], [0, 17], [1, 2]], 0)
+    iota(v("rows", WU, W), [[0, W - WU]], 0)
+    iota(v("rows", W, W + 12), [[W, NS], [34, NP], [1, 2]], 32)
+    iota(v("rows", W + 12, W + 16), [[0, 4]], 32)
+    scan(v("rows", 160, 176 + W), v("rows", 0, W + 16), v("cs", 0, W + 16), K, A.min, A.add)
+    ts(L(LE, W // 16), v("rows", 175, 160 + W, 16), -K, A.add)
+    ts(L(LH, 1), v("rows", 175 + W, 176 + W), -K, A.add)
+    iota(v("slot"), [[0, 4], [1, 17], [0, 2]], 0)
+    act(v("mw"), v("slot", 0, W), F.Sign)
+    act(v("rst"), v("mw"), F.Identity, scale=-B, bias=B)
+    act(v("kb", 0, WU), v("slot", 0, WU), F.Sign, bias=col(12))
+    iota(v("cb"), [[64, 6], [0, 17], [32, 2]], -1)
+    held.add(len(ops) - 1)
+    sel(v("cb"), v("cb"), [[0, 6], [1, 17], [0, 2]], A.is_equal, -K, 0, 0)
+    ms(v("ky", 0, 2), 0.0)
+    for b, pat in enumerate(([[0, 4], [1, 2], [0, 4]], [[0, 2], [1, 2], [0, 8]], [[1, 2], [0, 16]])):
+        iota(v("kx", 32 * b, 32 * b + 32), pat, 0)
+        ts(v("ky", 36 * b + 2, 36 * b + 34), v("kx", 32 * b, 32 * b + 32), col(4 + b), A.not_equal, B * 2 ** b, A.mult)
+    tt(v("ky", 2, 34), v("ky", 2, 34), v("ky", 38, 70), A.add)
+    tt(v("ky", 2, 34), v("ky", 2, 34), v("ky", 74, 106), A.add)
+    for q in range(NP):
+        act(v("kb1", 34 * q, 34 * q + 34), v("ky", 0, 34), F.Identity, bias=-B)
+    for s in range(2 * NS):
+        act(sl("dd", s, W), v("iof", 0, W), F.Identity, scale=0.0, bias=2 * B)
+        act(v("tt", 260 * s, 260 * s + 260), v("iof", 0, 260), scale=0.0)
+    for s in range(NS):
+        ms(v("ro", s * W + WU, (s + 1) * W), 0.0)
+    eye = [[-1, 128]]
+    iota(v("jm"), [[1, 8], [0, 16]], 0)
+    ts(v("b16"), v("jm"), col(2), A.is_equal)
     for t in range(4):
         act(lane_of(0, t), v("b16"))
-    ms(v("et"), 0.0, 2)
     ms(v("b8"), 0.0)
-    ts(L(LSW, 24), v("tf", 0, 24), col(8), A.add)
-    ts(L(LEO, 24), v("tf", 24, 48), col(1), A.add)
-    ts(v("c0"), v("c0"), v("c16", 47, 48), A.add)
-    ms(v("st", 512, 2560), 0.0, 8)
-    act(v("cs"), at(v("c16", 32, 48), L(LP, 24)))
+    sel(v("b8"), v("b8"), [[8, 16], [0, 8]], A.is_gt, 1.0, 0, -1)
+    sel(v("b8"), v("b8"), [[8, 16], [0, 8]], A.is_ge, 0.0, 7, -1)
+    sel(v("jm"), v("b8"), [[1, 128]], A.is_ge, 0.0, 0, -1)
+    for k, first_flags, second_flags in ((1, -B, 0.0), (2, -B, -B), (3, B, B), (4, B, B), (5, 0.0, None), (6, -B, -B), (7, B, B)):
+        act(lane_of(k, 0), v("b8"), scale=first_flags)
+        if second_flags is not None:
+            act(lane_of(k, 2), v("b8"), scale=second_flags)
+        act(v("st", 512 * k + 1, 512 * k + 512, 2), v("iof", 0, 256), scale=0.0)
+    for k, t, x in ((3, 1, B), (4, 3, B), (6, 2, 16 * B), (7, 2, -16 * B)):
+        sel(lane_of(k, t), lane_of(k, t), eye, A.not_equal, x, 0, 1)
+    sel(lane_of(5, 2), v("jm"), eye, A.not_equal, -8.0, 0, 1)
+    for k in range(8):
+        qz("s", 128 * k, 128 * k + 128, v("st", 512 * k, 512 * k + 512))
+    for h in range(2):
+        act(v("et", 258 * h, 258 * h + 258), v("iof", 0, 258), scale=0.0)
+    sel(v("et", 3, 515, 4), v("et", 3, 515, 4), eye, A.not_equal, 32.0, 0, 1)
+    for b in range(4):
+        qz("e", 128 * b, 128 * b + 128, v("et", 3 - b, 515 - b))
+
+    for x in (v("qe"), v("qs", 640, 768), L(LEI, 48), L(LE, 16), v("cb"), v("ro"), v("cf", 10, 12)):
+        lead.update({i: 2 * EARLY for i, k, w in seen[x[0]] if w and k & bits(x)})
+    for x in (v("tf", 48, 96), v("rows", 0, W + 16), v("jm"), v("et", 3, 515, 4)):
+        held.update(i for i, k, w in seen[x[0]] if w and k & bits(x))
+
     qz("u", 0, 128, v("ut"))
-    qz("x0", 0, PC[0][1], v("xt", 0, 4 * PC[0][1]))
-    cp(v("qus", 0, 128), at(v("qu"), L(LU, 8)), dt.uint32)
-    act(v("sus", 0, 128), at(v("su"), L(LU, 8)))
-    mm(5, "us", 0, "x0", 0, PC[0][1])
-    qz("x0", PC[1][0], C, v("xt", 4 * PC[1][0], 4 * C))
-    cp(v("qus", 128, 256), at(v("qu"), L(LU + 8, 8)), dt.uint32)
-    act(v("sus", 128, 256), at(v("su"), L(LU + 8, 8)))
-    act(v("cs2"), v("cs"))
-    tt(piece("y1", 0), bank(5, PC[0][1]), piece("cap", 0), A.min)
-    qz("s", 0, 128, v("st", 0, 512))
-    scan(piece("fs", 0), piece("rho", 0), piece("y1", 0), -BIG, A.min, A.max)
-
-    def constants_g():
-        eye = [[-1, 128]]
-        iota(v("slot"), [[0, 4], [1, 17], [0, 2]], 0)
-        sel(v("b8"), v("b8"), [[8, 16], [0, 8]], A.is_gt, 1.0, 0, -1)
-        sel(v("b8"), v("b8"), [[8, 16], [0, 8]], A.is_ge, 0.0, 7, -1)
-        sel(v("et", 3, 515, 4), v("et", 3, 515, 4), eye, A.not_equal, 32.0, 0, 1)
-        sel(v("jm"), v("b8"), [[1, 128]], A.is_ge, 0.0, 0, -1)
-        iota(v("rows", 0, WU), [[34, 3], [0, 17], [1, 2]], 0)
-        iota(v("rows", WU, W), [[0, W - WU]], 0)
-        for s in range(2):
-            iota(v("rows", W + 12 * s, W + 12 + 12 * s), [[34, 3], [1, 2], [W, 2]], 2 * W * s + 32)
-            iota(v("cb", 136 * s, 136 * s + 136), [[64, 4], [0, 17], [32, 2]], 192 * s - 1)
-        iota(v("rows", W + 24, W + 32), [[0, 8]], 32)
-        iota(v("tf", 48, 72), [[H, 2], [16, 6], [96, 2]], 0)
-        iota(v("tf", 72, 96), [[H, 2], [16, 6], [8, 2]], 0)
-        sel(v("cb"), v("cb"), [[0, 8], [1, 17], [0, 2]], A.is_equal, -K, 0, 0)
-        for b, pat in enumerate(([[0, 4], [1, 2], [0, 4]], [[0, 2], [1, 2], [0, 8]], [[1, 2], [0, 16]])):
-            iota(v("kx", 32 * b, 32 * b + 32), pat, 0)
-
-        sel(lane_of(3, 1), lane_of(3, 1), eye, A.not_equal, B, 0, 1)
-        sel(lane_of(4, 3), lane_of(4, 3), eye, A.not_equal, B, 0, 1)
-        sel(lane_of(5, 2), v("jm"), eye, A.not_equal, -8.0, 0, 1)
-
-    def late_tiles():
-        fill = lambda k, t, sg: act(lane_of(k, t), v("b8"), scale=sg)
-        diag = lambda k, x: sel(lane_of(k, 2), lane_of(k, 2), [[-1, 128]], A.not_equal, x, 0, 1)
-        return [lambda: [fill(2, 0, -B), fill(2, 2, -B)], lambda: [fill(4, 0, B), fill(4, 2, B)],
-                lambda: [fill(6, 2, -1.0), diag(6, 16.0), fill(7, 2, 1.0), diag(7, -16.0)],
-                lambda: [fill(5, t, 0.0) for t in (0, 1)], lambda: [fill(5, 3, 0.0), fill(6, 0, -1.0)], lambda: [fill(6, t, 0.0) for t in (1, 3)],
-                lambda: [fill(7, 0, 1.0), fill(7, 1, 0.0)], lambda: fill(7, 3, 0.0)]
-
-    def lists_v():
-        m = W + 32
-        scan(v("rowo", 0, m), v("rows", 0, m), v("cs", 0, m), K, A.min, A.add)
-        ts(col(9), col(3), -1.0, A.mult, 1.0, A.add)
-        ts(col(12), col(7), -2.0, A.mult, -1.0, A.add)
-        ts(col(13), col(3), 96.0, A.mult, col(7), A.add)
-        ms(v("dd"), 2 * B, 4)
-        for c, a, k in ((LE, 0, 7), (LH, W, 2)):
-            ts(L(c, k), v("rowo", a + 15, a + 16 * k, 16), -K, A.add)
-        ts(L(LEI, 24), v("tf", 48, 72), col(1), A.add)
-        ts(L(LES, 24), v("tf", 72, 96), col(13), A.add)
-
-    def constants_v():
-        ms(v("ky", 0, 2), 0.0)
-        for b in range(3):
-            ts(v("ky", 36 * b + 2, 36 * b + 34), v("kx", 32 * b, 32 * b + 32), col(4 + b), A.not_equal, B * 2 ** b, A.mult)
-        qz("e", 0, 128, v("et", 3, 515))
-        tt(v("ky", 2, 34), v("ky", 2, 34), v("ky", 38, 70), A.add)
-        qz("e", 128, 256, v("et", 2, 514))
-        tt(v("ky", 2, 34), v("ky", 2, 34), v("ky", 74, 106), A.add)
-        qz("e", 256, 384, v("et", 1, 513))
-        qz("e", 384, 512, v("et", 0, 512))
-        ms(v("tt0"), 0.0, 2)
-        ms(v("tt1"), 0.0, 2)
-        qz("s", 128, 256, v("st", 512, 1024))
-        qz("s", 384, 512, v("st", 1536, 2048))
-
-    def seat_of_place(step):
-        if step == 0:
-            ts(v("pj", 0, 24), v("pi"), 0, A.arith_shift_right, 8, A.bitwise_and)
-            ts(v("pj", 24, 48), v("pi"), 1, A.arith_shift_right, 8, A.bitwise_and)
-        elif step == 1:
-            tt(v("pj", 48, 72), v("pj", 0, 24), v("pi"), A.add)
-        elif step == 2:
-            tt(v("pj", 72, 96), v("pj", 48, 72), v("pj", 24, 48), A.subtract)
-        else:
-            cp(v("sp"), v("pj", 72, 96))
-
-    def decode_mm(src, b):
-        mm(4 + b, "e", 128 * b, src, 0, C)
+    for i in range(2):
+        cp(v("qus", 128 * i, 128 * i + 128), at(v("qu"), L(LU + 8 * i, 8)), dt.uint32)
+        ahead(0.5 - 0.5 * i)
+        act(v("sus", 128 * i, 128 * i + 128), at(v("su"), L(LU + 8 * i, 8)))
+    for h in range(len(PC)):
+        qz("x0", PC[h][0], PC[h][1], four("xt", h))
 
     for r in range(R):
-        X, XN, XP = "x%d" % r, "n%d" % r, "p%d" % r
-        OW, ON, OP, HW, HP = "ow%d" % r, "on%d" % r, "op%d" % r, "hw%d" % r, "hp%d" % r
-        mm(0, "us", 0, X, 0, C)
-        mm(1, "us", 0, X, 0, C)
-        mm(2, "us", 128, X, 0, C)
-        call = send([(prv, v("q" + X), v("q" + XN), "an%d" % r), (nxt, v("q" + X), v("q" + XP), "ap%d" % r)], dt.uint8)
-        call = send([(prv, v("s" + X), v("s" + XN), "an%d" % r), (nxt, v("s" + X), v("s" + XP), "ap%d" % r)], None, [call])
-        arrive([v("q" + XN), v("s" + XN)], "an%d" % r, 16, call, TILE_LAG)
-        arrive([v("q" + XP), v("s" + XP)], "ap%d" % r, 16, call, TILE_LAG)
-        if r == 0:
-            constants_g()
-        for k in EARLY[:-2]:
-            cmp(k, 5)
-        tt(piece("y1", 1), bank(0, C, PC[1][0]), piece("cap", 1), A.min)
-        cmp(EARLY[-2], 5)
-        scan(piece("fs", 1), piece("rho", 1), piece("y1", 1), -BIG, A.min, A.max)
-        cmp(EARLY[-1], 5)
-        for i, k in enumerate(KS):
-            act(v("sgn", C * i, C * i + 16 * k), bank(1, 16 * k), F.Sign, scale=-1.0, bias=mine(k))
-        for i, k in enumerate(KS):
-            act(lane(k, 16 * k), v("sgn", C * i, C * i + 16 * k), F.Relu, accum_out=v("rsum", k, k + 1))
-        tt(lane(24, C), v("fs"), bank(0, C), A.is_ge)
-        rest = [k for k in range(EARLY[0] + 1, 24) if k not in KS] + list(range(EARLY[-1] - 1, 0, -1))
-        done, order = set(EARLY), []
-        for i, k in enumerate(rest + [None]):
-            full = [q for q in range(1, 6) if q not in order and all(24 - 4 * q - t in done for t in range(4))]
-            if k:
-                cmp(k, 0)
-                done.add(k)
-            if i == 0:
-                scan(v("seg"), v("mu"), lane(24, C), 0.0, A.mult, A.add)
-            if i == 1:
-                tt(v("t1"), v("c0"), v("seg", 15, C, 16), A.subtract)
-            if k == EARLY[-1] - 1:
-                full = [0] + full
-            for q in full:
-                tile(q)
-                order.append(q)
-        mm(4, "s", 0, "c", TO[0], TN[0], True, False)
-        order.remove(0)
-        for q in order:
-            mm(4, "s", 0, "c", TO[q], TN[q], False, q == order[-1])
-        mm(3, "us", 128, XN, 0, C)
-        tt(v("cs2", 15, C, 16), v("t1"), v("rsum"), A.subtract)
-        act(v("ma"), bank(2, C), scale=DS)
-        scan(v("f2"), bank(4, C), v("cs2"), K, A.min, A.add)
-        PL, PN = "pl%d" % r, "pn%d" % r
+        X, XN, XP, XO = "x%d" % r, "n%d" % r, "p%d" % r, "x%d" % (r + 1)
+        PL, PN, OW, ON, OP, HW, HP = ["%s%d" % (nm, r) for nm in ("pl", "pn", "ow", "on", "op", "hw", "hp")]
+        send_state(prv, X, XN, "an%d" % r, PC, (), 0.0 if r else LOAD[4])
+        b0, b1, b2, b3, b4, b5 = range(6)
+        if r:
+            ms(v("junk", 255, 256 * 24, 256), 0.0)
+            ms(v("rsum"), 0.0)
+        mm(b5, "us", 0, X, 0, H)
+        own("y1", "fs", 0, H, bank(b5, H))
+        mm(b0, "us", 0, X, 0, C)
+        mm(b1, "us", 0, X, 0, C)
+        mm(b2, "us", 128, X, 0, C)
+        own("y1", "fs", H, C, bank(b0, C, H))
+        tt(lane(24, 0, C), v("fs"), bank(b0, C), A.is_ge)
+        scan(v("seg"), v("mu"), lane(24, 0, C), 0.0, A.mult, A.add)
+        for k in range(23, 0, -1):
+            m, spare = 16 * k, v("copy", 8 * k * (k - 1), 8 * k * (k + 1))
+            if k in KS:
+                act(spare, bank(b1, m), F.Sign, scale=-1.0, bias=mine(k))
+                act(lane(k, 0, m), spare, F.Relu, accum_out=v("rsum", k, k + 1))
+                continue
+            ts(lane(k, 0, m), bank(b5 if m < H else b0, m), mine(k), A.is_lt)
+            if k in KV[r]:
+                scan(v("junk", 256 * k + 256 - m, 256 * k + 256), v("one", 0, m), lane(k, 0, m), 0.0, A.mult, A.add)
+            else:
+                act(spare, lane(k, 0, m), accum_out=v("rsum", k, k + 1))
+        for q in QO:
+            qz("c", TO[q], TO[q] + TN[q], v("ct", 4 * TO[q], 4 * (TO[q] + TN[q])))
+            mm(b4, "s", 0, "c", TO[q], TN[q], q == 0, q == QO[-1])
+        tt(v("t1"), v("c0"), v("seg", 15, C, 16), A.subtract)
+        tt(v("t1"), v("t1"), v("junk", 255, 256 * 24, 256), A.subtract)
+        ahead(LEAD[5])
+        tt(v("cs2", 15, C, 16), v("t1"), v("rsum", 0, 24), A.subtract)
+        scan(v("f2"), bank(b4, C), v("cs2"), K, A.min, A.add)
         ts(v(PL), v("f2", 15, C, 16), -K, A.add)
-        ts(v("pi"), v("f2", 15, C, 16), -K, A.add)
         arrive([v(PN)], "ak%d" % r, 8, send([(prv, v(PL), v(PN), "ak%d" % r)]), LIST_LAG)
-        if r == 0:
-            for k, t, sg in ((1, 0, -B), (3, 0, B), (3, 2, B)):
-                act(lane_of(k, t), v("b8"), scale=sg)
-            dma("s", T.qw[:].bitcast(dt.uint8), T.wc[:], "dw", [v(PL)], [v("qw")])
-            dma("s", T.sw[:], T.ws[:], "dw2", [v(PL)], [v("sw")])
-            dma("s", T.vt[:], T.v[:], "dv", [v(PL)], [v("vt")])
-            for h in range(2):
-                act(v("mw", h * W, (h + 1) * W), v("slot", 0, W), F.Sign)
+        act(v("ma"), bank(b2, C), scale=DS)
         cp(at(v("oS"), v(PL)), v("iof"))
-        seat_of_place(0)
-        cp(half("y1", 0), at(v("oS"), L(LEO, 12)))
-        act(half("y1", 1), at(v("oS"), L(LEO + 12, 12)))
-        act(v("mb"), bank(3, C), scale=DS)
-        seat_of_place(1)
+        picked("y1", "oS", lambda h: L(LEO + 12 * h, 12))
         for h in range(2):
-            own_whole("fs", h, half("y1", h))
-        seat_of_place(2)
-        for h in range(2):
-            as_list(OW, "fs", h)
-            ahead(LEAD[3])
+            as_list(OW, "fs", "y1", H * h, H * h + H)
+            ahead(LEAD[2])
         call = send([(prv, v(OW), v(ON), "al%d" % r), (nxt, v(OW), v(OP), "ao%d" % r)])
         arrive([v(ON)], "al%d" % r, 8, call, 2 * LIST_LAG)
         arrive([v(OP)], "ao%d" % r, 8, call, 2 * LIST_LAG)
-        sl = lambda nm, s, m=WU: v(nm, s * W, s * W + m)
-        seat_of_place(3)
-        if r == 0:
-            lists_v()
-            constants_v()
-        for s in range(2):
-            part = lambda i: v("ta", H * i + 96 * s, H * i + 96 * s + 96)
-            act(part(1), at(v("ma"), v(OW, 12 * s, 12 * s + 6)), F.Identity, scale=col(9))
-            act(part(2), at(v("ma"), v(OW, 12 * s + 6, 12 * s + 12)), F.Identity, scale=col(3))
+        send_state(nxt, X, XP, "ap%d" % r, [(0, C)], [call])
+        m = 32 * NP
+        for s in range(NS):
+            part = lambda i: v("ta", H * i + m * s, H * i + m * s + m)
+            act(part(1), at(v("ma"), v(OW, 4 * NP * s, 4 * NP * s + 2 * NP)), F.Identity, scale=col(9))
+            act(part(2), at(v("ma"), v(OW, 4 * NP * s + 2 * NP, 4 * NP * (s + 1))), F.Identity, scale=col(3))
             tt(part(0), part(1), part(2), A.add)
+        for bk, a, b in ((b3, 0, PC[-1][0]), (b5, PC[-1][0], C)):
+            mm(bk, "us", 128, XN, a, b - a)
+            act(v("mb", a, b), bank(bk, b - a), scale=DS)
         cp(at(v("bS"), v(PN)), v("mb"))
-        for b in range(4):
-            decode_mm(XP, b)
+        for s in range(NS):
+            own("y2", "fb", m * s, m * (s + 1), at(v("bS"), L(LSW + 2 * NP * s, 2 * NP)))
+
+        def distances(u):
+            for s in range(NS):
+                for i in range(2 * NP):
+                    a, k = (2 * s + u) * W + 34 * (i // 2) + i % 2, 2 * NP * s + i
+                    act(v("dd", a + 2, a + 33, 2), v("ta", 16 * k, 16 * k + 16), F.Abs, scale=-1.0, bias=v("fb", H * u + 16 * k + 15, H * u + 16 * k + 16))
+
+        def in_the_sweeps():
+            for a in range(H, C, 64):
+                own("y2", "fb", a, a + 64, at(v("bS"), L(LSW + a // 16, 4)))
+            cp(v("pi"), v(PL))
+            distances(1)
+            ts(v("pj", 0, 24), v("pi"), 0, A.arith_shift_right, 8, A.bitwise_and)
+            ts(v("pj", 24, 48), v("pi"), 1, A.arith_shift_right, 248, A.bitwise_and)
+            ts(v("pj", 48, 72), v("pi"), 0, A.arith_shift_right, 7, A.bitwise_and)
+            ts(v("pj", 0, 24), v("pj", 0, 24), 24.0, A.mult)
+            tt(v("pj", 24, 48), v("pj", 24, 48), v("pj", 48, 72), A.add)
+            tt(v("pj", 72, 96), v("pj", 0, 24), v("pj", 24, 48), A.add)
+            cp(v("sp"), v("pj", 72, 96))
+            ahead(EARLY)
+
+        distances(0)
+
         if r == 0:
-            for q in range(3):
-                act(v("kb1", 34 * q, 34 * q + 34), v("ky", 0, 34), F.Identity, bias=-B)
-            act(v("rst"), v("mw"), F.Identity, scale=-B, bias=B)
-            act(v("kb", 0, WU), v("slot", 0, WU), F.Sign, bias=col(12))
-        for h in range(2):
-            own_mask("y2", h, at(v("bS"), L(LSW + 12 * h, 12)))
-            own_scan("y2", "fb", h)
-
-        def distances(s, u):
-            for i in range(6):
-                a, k = (2 * s + u) * W + 34 * (i // 2) + i % 2, 6 * s + i
-                act(v("dd", a + 2, a + 33, 2), v("ta", 16 * k, 16 * k + 16), F.Abs, scale=-1.0, bias=v("fb", 32 * k + 16 * u + 15, 32 * k + 16 * u + 16))
-
-        for s in range(2):
-            distances(s, 0)
-        later = []
+            dma("s", T.qw[:].bitcast(dt.uint8), T.wc[:], "dw", [v("q" + XP)], [v("qw")])
+            dma("s", T.sw[:], T.ws[:], "dw2", [v("q" + XP)], [v("sw")])
+            dma("s", T.vt[:], T.v[:], "dv", [v("q" + XP)], [v("vt")])
+            qz("v", 0, 128, v("vt"))
+            ahead(EARLY)
+        for src, dst in ((XN, "dn"), (XP, "gt"), ("g", "dp")):
+            for b in range(4):
+                mm(DB[b], "e", 128 * b, src, 0, C)
+                for h in range(2):
+                    out = v("gt", 4 * H * h + b, 4 * H * (h + 1), 4) if dst == "gt" else v(dst, b * C + H * h, b * C + H * h + H)
+                    act(out, bank(DB[b], H * h + H, H * h), scale=1 / 32)
+                    ahead(0.0 if dst == "gt" else EARLY)
+            if dst == "gt":
+                for i in range(3):
+                    qz("g", 128 * i, 128 * i + 128, v("gt", 512 * i, 512 * i + 512))
+        for row, lst, out, back in (("opr", OP, "opn", LEI), ("onr", ON, "ons", LES)):
+            for h in range(2):
+                act(half(row, h), at(v("iof"), lhalf(lst, h)))
+            for h in range(2):
+                act(half(out, h), at(v(row), L(back + 12 * h, 12)))
+                ahead(EARLY)
 
         def zl(s, t, a=0, b=WU, step=1):
-            return v("tt%d" % s, 8 + 4 * a + t, 8 + 4 * b, 4 * step)
+            return v("tt", 520 * s + 8 + 4 * a + t, 520 * s + 8 + 4 * b, 4 * step)
 
-        def head(w, s):
-            vL, dL, xL = sl("vv", 2 * s), sl("dd", 2 * s), bank(2 * s, WU)
-            if w == 0:
-                tt(vL, v("dd", 2 * s * W + 2, 2 * s * W + WU + 2), dL, A.is_lt)
-            elif w == 1:
-                tt(sl("yy", s), xL, v("kb1", 0, WU), A.add)
-                act(zl(s, 1), sl("yy", s), F.Identity, scale=1 / B, bias=-1.0)
-            else:
-                tt(vL, xL, dL, A.max)
-                if w == SW - 1:
-                    act(zl(s, 1), dL, scale=0.0)
-                else:
-                    act(zl(s, 1), xL, F.Identity, scale=1 / B, bias=-1.0)
-                    if w == 8:
-                        act(zl(s, 2), xL, F.Relu, scale=-1 / B, bias=-7.0)
-                    if w >= 8:
-                        act(zl(s, 3), xL, F.Identity, scale=1 / B, bias=7.0)
-            if w >= 9:
-                tt(sl("vv", 2 * s + 1), bank(2 * s + 1, WU), sl("dd", 2 * s + 1), A.max)
-
-        def body(w, s):
-            if w == 0:
-                tt(zl(s, 0), sl("vv", 2 * s), v("kb", 0, WU), A.is_gt)
-                return
-            if w == 1:
-                tt(sl("vv", 2 * s), sl("yy", s), sl("dd", 2 * s), A.max)
-            for u in range(2 if w >= 9 else 1):
-                o = (2 * s + u) * W
-                for par in range(2):
-                    scan(v("ff", o + par, o + WU, 2), v("rst", par, WU, 2), v("vv", o + par, o + WU, 2), 0.0, A.max, A.min)
-                for i, (par, q) in enumerate([(par, q) for par in range(2) for q in range(3)]):
-                    a = o + 34 * q + par
-                    out, x, last = zl(s, 2 * u, 34 * q + par, 34 * q + 34, 2), v("ff", a, a + 33, 2), v("ff", a + 32, a + 33)
-                    if i < NV:
-                        ts(out, x, last, A.is_gt, -1.0, A.mult)
-                    else:
-                        act(out, x, F.Sign, scale=-1.0, bias=last)
-
-        def tail(w, s):
-            nm = "t%d" % s
-            before = 128 if w <= 8 else 256
-            qz(nm, 0, 130, v("tt%d" % s))
-            if w == SW - 1:
-                mm(2 * s, "s", 768, nm, 0, 128, True, False)
-                mm(2 * s, "s", 896, nm, 2, 128, False, True)
-                mm(2 * s + 1, "s", 640, nm, 2, 128)
-                return
-            mm(2 * s, "s", before if w else 384, nm, 0, 128, True, False)
-            mm(2 * s, "s", 384 if w else before, nm, 2, 128, False, True)
-            if w == SW - 2 and s == 0:
-                ahead(LEAD[0])
-            if w >= 8:
-                mm(2 * s + 1, "s", before, nm, 0, 128, True, False)
-                mm(2 * s + 1, "s", 512, nm, 2, 128, False, True)
-
-        def unpack(dst, b, h, then=None):
-            def fn():
-                act(v(dst, b * C + H * h, b * C + H * h + H), bank(4 + b, H * h + H, H * h), scale=1 / 32)
-                if then and h:
-                    later.append((then, b))
-            return fn
-
-        def rows_of(out, win, lst, h):
-            return lambda: act(half(out, h), at(v(win), lst))
-
-        def whole(dst, b, then):
-            def fn():
-                act(v("gt", b, 4 * C, 4) if dst == "gt" else v(dst, b * C, b * C + C), bank(4 + b, C), scale=1 / 32)
-                later.append((then, b))
-            return fn
-
-        aside = [whole("gt", b, XN) for b in range(4)]
-        aside += [rows_of("opr", "iof", lhalf(OP, h), h) for h in range(2)] + [rows_of("opn", "opr", L(LEI + 12 * h, 12), h) for h in range(2)]
-        aside += [whole("dn", b, "g") for b in range(4)]
-        aside += [lambda: [distances(s, 1) for s in range(2)]]
-        aside += [lambda: [rows_of("onr", "iof", lhalf(ON, h), h)() for h in range(2)], lambda: [rows_of("ons", "onr", L(LES + 12 * h, 12), h)() for h in range(2)]]
-        aside += [unpack("dp", b, h) for b in range(4) for h in range(2)]
-        tiles = late_tiles() if r == 0 else []
-
-        def extras(t):
-            if t in (4, 5, 6):
-                qz("g", 128 * (t - 4), 128 * (t - 3), v("gt", 512 * (t - 4), 512 * (t - 3)))
-            if r:
-                return
-            if 9 <= t < 14:
-                k = (4, 2, 5, 6, 7)[t - 9]
-                qz("s", 128 * k, 128 * k + 128, v("st", 512 * k, 512 * k + 512))
-            if t in (14, 15):
-                s = t - 14
-                ms(v("ro", s * W + WU, (s + 1) * W), 0.0)
-            if t == 16:
-                ts(col(10), col(7), 1.0, A.add)
-                ts(col(11), col(3), 16.0, A.mult)
+        def product(bk, s, before, same):
+            mm(bk, "s", 128 * before, "f", 132 * s, 128, True, False)
+            mm(bk, "s", 128 * same, "f", 132 * s + 2, 128, False, True)
 
         for w in range(SW):
-            for s in range(2):
-                head(w, s)
-                if w + s:
-                    tail(w - 1 + s, 1 - s)
-                while later:
-                    decode_mm(*later.pop(0))
-                body(w, s)
-                extras(2 * w + s)
-                if aside:
-                    aside.pop(0)()
-                if tiles:
-                    tiles.pop(0)()
-        assert not aside
-
-        def fin(step, s):
-            if step == 0:
-                act(sl("rr", s), bank(2 * s, WU), F.Identity, scale=-1.0, bias=1.0)
-                act(sl("ep", s), bank(2 * s + 1, WU), F.Identity, bias=col(10))
-            elif step == 1:
-                for par in range(2):
-                    c = lambda nm: v(nm, s * W + par, s * W + WU, 2)
-                    scan(c("ro"), c("rr"), v("mw", par, WU, 2), 0.0, A.add, A.mult)
-            elif step == 2:
-                tt(sl("g2", s, W), at(sl("ep", s), L(LE, 7)), sl("ro", s, W), A.is_gt)
-            else:
-                u = step - 4
-                for par in range(2):
+            for s in range(NS):
+                vL, dL, xL, xU = sl("vv", 2 * s), sl("dd", 2 * s), bank(LB[s], WU), bank(UB[s], WU)
+                if w == 0:
+                    tt(vL, v("dd", 2 * s * W + 2, 2 * s * W + WU + 2), dL, A.is_lt)
+                    tt(zl(s, 2), vL, v("kb", 0, WU), A.is_gt)
+                    tt(sl("d1", s), dL, v("kb1", 0, WU), A.max)
+                elif w == 1:
+                    tt(vL, xL, sl("d1", s), A.max)
+                    tt(sl("yy", s), xU, v("kb1", 0, WU), A.add)
+                    act(zl(s, 1), sl("yy", s), F.Identity, scale=1 / B, bias=-1.0)
+                    act(zl(s, 2), v("iof", 0, WU), scale=0.0)
+                else:
+                    tt(vL, xL, dL, A.max)
+                    if w < SW - 1:
+                        act(zl(s, 1), xL, F.Identity, scale=1 / B, bias=-1.0)
+                    if w == 8:
+                        act(zl(s, 2), xL, F.Relu, scale=-1 / B, bias=-7.0)
+                    if 8 <= w < SW - 1:
+                        act(zl(s, 3), xL, F.Identity, scale=1 / B, bias=7.0)
+                if w >= 9:
+                    tt(sl("vv", 2 * s + 1), xU, sl("dd", 2 * s + 1), A.max)
+                for u in range(2 if w >= 9 else 1 if w else 0):
                     o = (2 * s + u) * W
-                    flags = v("g2", s * W + par, s * W + WU, 2) if u else zl(s, 0, par, WU, 2)
-                    scan(v("hs", o + par, o + WU, 2), v("cb", 136 * s + par, 136 * s + WU, 2), flags, -K, A.max, A.add if u else A.subtract)
-                    if s == 0:
-                        ahead(LEAD[2])
+                    for par in range(2):
+                        scan(v("ff", o + par, o + WU, 2), v("rst", par, WU, 2), v("vv", o + par, o + WU, 2), 0.0, A.max, A.min)
+                        for q in range(NP):
+                            a = o + 34 * q + par
+                            out, x, last = zl(s, 2 * u, 34 * q + par, 34 * q + 34, 2), v("ff", a, a + 33, 2), v("ff", a + 32, a + 33)
+                            if par == 0 or (q == 0 and w < 9):
+                                ts(out, x, last, A.is_gt, -1.0, A.mult)
+                            else:
+                                act(out, x, F.Sign, scale=-1.0, bias=last)
+                qz("f", 132 * s, 132 * s + 130, v("tt", 520 * s, 520 * s + 520))
+                if w == 1 and s == 0:
+                    in_the_sweeps()
+                if w == 0:
+                    product(LB[s], s, 7, 6)
+                    product(UB[s], s, 4, 2)
+                elif w < SW - 1:
+                    product(LB[s], s, 1 if w <= 8 else 2, 3)
+                    if w == SW - 2:
+                        ahead(LEAD[0] * (NS - 1 - s))
+                    if w >= 8:
+                        product(UB[s], s, 1 if w <= 8 else 2, 4)
+                else:
+                    product(LB[s], s, 6, 7)
+                    mm(UB[s], "s", 640, "f", 132 * s + 2, 128)
 
-        fin(0, 0)
-        tail(SW - 1, 1)
-        fin(0, 1)
-        for step, s in ((1, 0), (4, 0), (2, 0), (4, 1), (1, 1), (5, 0), (2, 1)):
-            fin(step, s)
-        if r + 1 < R:
-            ms(zl(0, 2), 0.0)
-            ms(zl(1, 2), 0.0)
-        else:
-            qz("v", 0, 128, v("vt"))
-        fin(5, 1)
-        ts(v(HW), at(v("hs"), L(LH, 2)), col(11), A.add)
-        arrive([v(HP)], "ah%d" % r, 8, send([(nxt, v(HW, 0, 24), v(HP), "ah%d" % r)]), LIST_LAG)
-        if r + 1 == R:
-            PC = LAST
-        bk = lambda h, b: (4 + b, b)[h]
-        width = lambda h: PC[h][1] - PC[h][0]
-        for h in range(2):
-            for b in range(4):
-                mm(bk(h, b), "e", 128 * b, X, PC[h][0], width(h), True, False)
-        cp(at(v("wr"), v(HW, 0, 24)), v("ons"))
-        cp(half("wj", 0), at(v("wr"), lhalf(PL, 0)))
-        act(half("wj", 1), at(v("wr"), lhalf(PL, 1)))
+        for s in range(NS):
+            act(sl("rr", s), bank(LB[s], WU), F.Identity, scale=-1 / B, bias=1.0)
+            act(sl("ep", s), bank(UB[s], WU), F.Identity, bias=col(10))
+            for par in range(2):
+                scan(v("ro", s * W + par, s * W + WU, 2), v("rr", s * W + par, s * W + WU, 2), v("mw", par, WU, 2), 0.0, A.add, A.mult)
+            tt(sl("g2", s, W), at(sl("ep", s), L(LE, W // 16)), sl("ro", s, W), A.is_gt)
+            for u in range(2):
+                for par in range(2):
+                    o = (NS * u + s) * W
+                    flags = v("g2", s * W + par, s * W + WU, 2) if u else zl(s, 0, par, WU, 2)
+                    scan(v("hs", o + par, o + WU, 2), v("cb", WU * s + par, WU * s + WU, 2), flags, -K, A.max, A.add if u else A.subtract)
+            if r + 1 < R:
+                act(zl(s, 0), v("iof", 0, WU), scale=0.0)
+                act(zl(s, 3), v("iof", 0, WU), scale=0.0)
+        for u in range(2):
+            ts(v(HW, 16 * u, 16 * u + 16), at(v("hs", NS * W * u, NS * W * (u + 1)), L(LH, 1)), col(11), A.add)
+            sem = "%s%d" % (("ah", "aj")[u], r)
+            arrive([v(HP, 16 * u, 16 * u + 12)], sem, 8, send([(nxt, v(HW, 16 * u, 16 * u + 12), v(HP, 16 * u, 16 * u + 12), sem)]), LIST_LAG)
+            for a, b in ((0, 12),) if u else ((0, 6), (6, 12)):
+                cp(at(v("wr"), v(HW, 16 * u + a, 16 * u + b)), v("ons", H * u + 16 * a, H * u + 16 * b))
+                ahead(0.0 if u else LEAD[4])
+        PC = LAST if r + 1 == R else MID
+        picked("wj", "wr", lambda h: lhalf(PL, h))
         if r + 1 == R:
             dma("s", T.ol[:], T.wj[0:128:16, :], "out_s", [v("wj")])
+        act(half("hr", 0), at(v("opn"), v(HP, 0, 12)))
+        cp(v("hr", H, H + 96), at(v("opn"), v(HP, 16, 22)))
+        act(v("hr", H + 96, C), at(v("opn"), v(HP, 22, 28)))
         for h in range(2):
-            own_whole("f2", h, half("wj", h))
-        for h in range(2):
-            as_list("wl", "f2", h)
-        act(half("hr", 1), at(v("opn"), lhalf(HP, 1)))
-        cp(half("hr", 0), at(v("opn"), lhalf(HP, 0)))
-        for h in range(2):
+            as_list("wl", "f2", "wj", H * h, H * h + H)
+        for h in range(len(PC)):
+            (cp, act)[h % 2](piece("y1", h), at(v("hr"), lpiece("sp", h)))
+            as_list("hl", "fs", "y1", PC[h][0], PC[h][1])
+            ahead(LEAD[3] * h)
+        for h in range(len(PC)):
+            bk = lambda b: (4 + b, b)[h % 2]
             for b in range(4):
+                mm(bk(b), "e", 128 * b, X, PC[h][0], width(h), True, False)
                 act(piece("vg", h, b * C), at(v("dn", b * C, (b + 1) * C), lpiece("wl", h)))
-        for h in range(2):
-            cp(half("y1", h), at(v("hr"), lhalf("sp", h)))
-        for h in range(2):
-            own_whole("fs", h, half("y1", h))
-        for h in range(2):
-            as_list("hl", "fs", h)
-        XO = "x%d" % (r + 1)
-        four = lambda nm, h: v(nm, 4 * PC[h][0], 4 * PC[h][1])
-        elem = lambda nm, h, b: v(nm, 4 * PC[h][0] + b, 4 * PC[h][1], 4)
-
-        def z_half(h, bs):
-            for b in bs:
                 tt(elem("zt", h, b), at(v("dp", b * C, (b + 1) * C), lpiece("hl", h)), piece("vg", h, b * C), A.max)
-
-        def w_half(h):
             qz("z", PC[h][0], PC[h][1], four("zt", h))
             for b in range(4):
-                mm(bk(h, b), "w", 128 * b, "z", PC[h][0], width(h), False, True)
-            for b in range(4):
-                if h == 0 or b not in XV:
-                    act(elem("xn", h, b), bank(bk(h, b), width(h)), scale=0.03125)
-
-        def x_own():
-            for b in XV:
-                ts(elem("xn", 1, b), bank(bk(1, b), width(1)), 0.03125, A.mult)
-
-        def x_half(h):
+                mm(bk(b), "w", 128 * b, "z", PC[h][0], width(h), False, True)
+                if h + 1 == len(PC) and b in XV:
+                    ts(elem("xn", h, b), bank(bk(b), width(h)), 0.03125, A.mult)
+                else:
+                    act(elem("xn", h, b), bank(bk(b), width(h)), scale=0.03125)
             qz(XO, PC[h][0], PC[h][1], four("xn", h))
-            if h == 0:
-                ahead(LEAD[1])
+            ahead(LEAD[1] * (len(PC) - 1 - h))
 
-        def store(h):
-            a, b = PC[h]
-            dma("s", T.oc[:, 4 * a:4 * b], T.qx2[:, a:b].bitcast(dt.uint8), "out_s", [piece("qx2", h)])
-
-        z_half(0, range(4))
-        z_half(1, [0])
-        w_half(0)
-        z_half(1, [1, 2, 3])
-        w_half(1)
-        x_half(0)
-        if r + 1 < R:
-            mm(5, "us", 0, XO, 0, width(0))
-            x_own()
-            tt(piece("y1", 0), bank(5, width(0)), piece("cap", 0), A.min)
-            x_half(1)
-            scan(piece("fs", 0), piece("rho", 0), piece("y1", 0), -BIG, A.min, A.max)
-        else:
-            mm(4, "v", 0, "x2", 0, width(0))
-            store(0)
-            x_own()
-            cp(piece("yo", 0), bank(4, width(0)))
-            dma("s", T.y[:, 0:width(0)], T.yo[:, 0:width(0)], "out_s", [piece("yo", 0)])
-            x_half(1)
-
-    mm(5, "v", 0, "x2", PC[1][0], width(1))
-    store(1)
-    cp(piece("yo", 1), bank(5, width(1)))
+    for h, (a, b) in enumerate(PC):
+        last = int(b == C)
+        dma("s", T.oc[:, 4 * a:4 * b], T.qx2[:, a:b].bitcast(dt.uint8), "out_s", [piece("qx2", h)])
+        mm(h, "v", 0, "x2", a, b - a)
+        (act, cp)[last](piece("yo", h), bank(h, b - a))
+        dma("sa"[last], T.y[:, a:b], T.yo[:, a:b], "out_" + "sa"[last], [piece("yo", h)])
     for k in range(4):
-        dma("a" if k % 2 else "s", T.osc[4 * k:4 * k + 4, :], T.sx2[32 * k:32 * k + 4, :], "out_a" if k % 2 else "out_s", [v("sx2")])
-    dma("a", T.y[:, PC[1][0]:C], T.yo[:, PC[1][0]:C], "out_a", [piece("yo", 1)])
+        dma("sa"[k % 2], T.osc[4 * k:4 * k + 4, :], T.sx2[32 * k:32 * k + 4, :], "out_" + "sa"[k % 2], [v("sx2")])
 
     free = lambda d, i: ops[d][3] == "-" or ops[d][0] == ops[i][0] == "t"
     gap = lambda d, i: ops[d][5] + ops[d][6] + (0.0 if free(d, i) else WAKE)
@@ -701,16 +583,15 @@ def rank_program(g, core, T, topo):
     for i, op in enumerate(ops):
         for d in op[2]:
             users[d].append(i)
-    ready, idle, order = [0.0] * len(ops), {e: 0.0 for e in ENG + ("x",)}, []
+    ready, idle, order = [HOLD * (i in held) for i in range(len(ops))], {e: 0.0 for e in ENG + ("x",)}, []
     open_ = {e: [i for i, op in enumerate(ops) if op[0] == e and not op[2]] for e in idle}
 
     def choice(e):
-        best, limit = None, 1e9
+        best, longest = None, max(chain[i] for q in open_.values() for i in q)
         for i in sorted(open_[e], key=lambda i: (-chain[i], i)):
             t = max(ready[i], idle[e])
-            if best is None or (t < best[0] and t + ops[i][5] <= limit + SLIP):
+            if best is None or (t < best[0] and t + ops[i][5] <= best[0] + (SLIP if chain[i] > longest - SOON else 0.0)):
                 best = (t, i)
-            limit = min(limit, t)
         return best
 
     while len(order) < len(ops):

from concourse.bass import DstId, RemoteDMATransfer
from concourse.mybir import dt, AluOpType, ActivationFunctionType

A = AluOpType
F = ActivationFunctionType
C = 384
H = 192
R = 2
SW = 12
NS = 2
NP = 6 // NS
WU = 34 * NP
W = WU + 16 - WU % 16
B = 2.0 ** 26
DS = 2.0 ** -46
BIG = 2.0 ** 90
K = 1024.0
TN = [384, 320, 256, 192, 128, 128]
TO = [0, 384, 704, 960, 1152, 1280]
QO = (0, 4, 5, 3, 2, 1)
KS = (23, 22, 21, 20, 19)
KV = ((16, 15, 14, 13, 12, 11), (16, 15, 14, 13))
FIRST = ((0, 128), (128, 256), (256, C))
MID = ((0, H), (H, C))
LAST = ((0, 128), (128, 256), (256, C))
XV = (0, 2)
LB, UB, DB = ((0, 2), (1, 3), (4, 5, 6, 7)) if NS == 2 else ((0, 1, 2), (3, 4, 5), (6, 7, 6, 7))
CYCLE, PE_CYCLE, GATHER, SCATTER, WAKE, DMA_LAG, LIST_LAG, TILE_LAG = 0.0009, 0.0006, 1.7, 3.8, 0.19, 3.0, 2.0, 7.6
ACT_START = 0
HOLD = 15.5
LOAD = (-0.5, -0.2, 0.1, -0.4, 0.4)
SLIP = 0.1
SOON = 4.0
EARLY = 1.0
LEAD = (1.0, 0.55, 1.0, 0.5, 1.0, 0.3)
LU, LP, LSW, LEO, LEI, LES, LE, LH = 0, 16, 40, 64, 88, 112, 136, 144

Q4, U8, F32, BF, I32, U16 = "float8_e4m3fn_x4", "uint8", "float32", "bfloat16", "int32", "uint16"
SCRATCH = {"ps": ("psum", [128, 4096], F32)}


def _sb(name, n, d):
    SCRATCH[name] = ("sbuf", [128, n], d)


for _n, _w in (("qu", 128), ("qus", 256), ("qv", 128), ("qw", 512), ("qx0", C), ("qx1", C), ("qx2", C), ("qn0", C), ("qn1", C),
               ("qp0", C), ("qp1", C), ("qg", C), ("qz", C), ("qc", 1408), ("qf", 132 * NS), ("qe", 512), ("qs", 1024)):
    _sb(_n, _w, Q4)
    _sb("s" + _n[1:], _w, U8)
for _n, _w in (("xt", 4 * C), ("ut", 512), ("vt", 512), ("xn", 4 * C), ("gt", 4 * C), ("zt", 4 * C), ("ct", 4 * 1408), ("tt", 520 * NS),
               ("et", 516), ("st", 4096), ("dn", 4 * C), ("dp", 4 * C), ("vg", 4 * C), ("copy", 4416), ("junk", 256 * 24), ("one", 256), ("mu", C), ("seg", C)):
    _sb(_n, _w, BF)
for _n, _w in (("iof", C), ("cap", C), ("rho", C), ("cs", C), ("cs2", C), ("bS", C), ("c0", 24), ("cf", 16), ("c16", 64), ("jm", 128), ("b16", 128), ("b8", 128),
               ("kb", W), ("kb1", W), ("kx", 96), ("ky", 144), ("slot", 136), ("rst", W), ("mw", W), ("cb", NS * WU), ("rows", 320),
               ("tf", 96), ("y1", C), ("fs", C), ("rsum", 48), ("t1", 24), ("y2", C), ("f2", C), ("fb", C), ("ma", C), ("mb", C), ("oS", C),
               ("onr", C), ("ons", C), ("opr", C), ("opn", C), ("ta", 3 * H), ("dd", 2 * NS * W), ("vv", 2 * NS * W), ("ff", 2 * NS * W),
               ("yy", NS * W), ("d1", NS * W), ("rr", NS * W), ("ro", NS * W), ("ep", NS * W), ("g2", NS * W), ("hs", 2 * NS * W),
               ("wr", C), ("wj", C), ("hr", C), ("yo", C)):
    _sb(_n, _w, F32)
for _n, _w in (("ci", 16), ("ti", 16), ("pi", 24), ("pj", 96)):
    _sb(_n, _w, I32)
for _n, _w in (("lst", 152), ("pl0", 24), ("pl1", 24), ("pn0", 24), ("pn1", 24), ("ow0", 24), ("ow1", 24), ("on0", 24), ("on1", 24), ("op0", 24), ("op1", 24),
               ("hw0", 32), ("hw1", 32), ("hp0", 32), ("hp1", 32), ("sp", 24), ("wl", 24), ("hl", 24)):
    _sb(_n, _w, U16)

ENG = ("v", "a", "t", "g", "s")
DMAS = ["dx0", "dx1", "dx2", "du", "dv", "dw", "dw2", "out_s", "out_a"]
ARR = ["an0", "an1", "ap0", "ap1", "an0z", "an1z", "ap0z", "ap1z", "al0", "al1", "ao0", "ao1", "ah0", "ah1", "aj0", "aj1", "ak0", "ak1"]
SEMAPHORES = ["ev", "ea", "et", "eg", "sent"] + DMAS + ARR


def v(name, a=0, b=None, step=1):
    return (name, a, SCRATCH[name][1][1] if b is None else b, step, None)


def at(win, offs):
    return win[:4] + (offs,)


def rank_program(g, core, T, topo):
    rank = T.rank_of(core)
    if rank is None:
        return
    n = len(T.cores)
    nxt, prv = T.cores[(rank + 1) % n], T.cores[(rank - 1) % n]
    Q = {"v": g.vector, "a": g.scalar, "t": g.tensor, "g": g, "s": g.sync}
    V, S, P = g.vector, g.scalar, g.tensor

    ops, seen, sent, lead, held = [], {}, [0], {}, set()

    def ahead(t):
        lead[len(ops) - 1] = t

    def ap(x, cast=None):
        if not isinstance(x, tuple):
            return x
        r = T[x[0]][:, x[1]:x[2]:x[3]] if x[3] > 1 else T[x[0]][:, x[1]:x[2]]
        if cast:
            r = r.bitcast(cast)
        return r.indirect(ap(x[4])) if x[4] else r

    def bits(x):
        if x[0] == "ps":
            return sum(1 << b for b in range(x[1] // 512, (x[2] - 1) // 512 + 1))
        return sum(1 << c for c in range(x[1], x[2], x[3]))

    def size(x):
        return 16 * (x[4][2] - x[4][1]) if x[4] else len(range(x[1], x[2], x[3]))

    def cost(out, ins, each=1.0, fast=True):
        if out[4] or ins[0][4]:
            return 0.06 + (SCATTER * size(out) if out[4] else GATHER * size(ins[0])) * CYCLE
        if fast and all(SCRATCH[x[0]][2] in (BF, U16) for x in [out] + ins):
            each /= 2
        return max(64, each * size(ins[0])) * CYCLE

    def add(eng, fn, rd=(), wr=(), sem=None, cnt=None, busy=0.06, lag=0.0, after=()):
        me, deps = len(ops), set(after)
        rd = [x for x in rd if isinstance(x, tuple)]
        rd += [x[4] for x in rd + list(wr) if x[4]]
        for x in rd:
            m = bits(x)
            deps.update(i for i, k, w in seen.get(x[0], ()) if k & m and (w or (x[0] == "ps" and ops[i][0] != eng)))
        for x in wr:
            m = bits(x)
            deps.update(i for i, k, w in seen.get(x[0], ()) if k & m)
        ops.append((eng, fn, deps, sem, cnt, busy, lag))
        for x in wr:
            m = bits(x)
            seen[x[0]] = [(i, k & ~m, w) for i, k, w in seen.get(x[0], ()) if k & ~m] + [(me, m, True)]
        for x in rd:
            seen.setdefault(x[0], []).append((me, bits(x), False))
        return me

    def arrive(views, sem, cnt, call, lag):
        add("x", None, (), views, sem, cnt, 0.001, lag, [call])

    def tt(out, a, b, op):
        add("v", lambda: V.tensor_tensor(ap(out), ap(a), ap(b), op), [a, b], [out], busy=cost(out, [a, b], 1.0 if "ps" in (a[0], b[0]) else 2.0, False))

    def ts(out, a, s1, op0, s2=None, op1=None):
        if op1 is None:
            add("v", lambda: V.tensor_scalar(ap(out), ap(a), ap(s1), None, op0), [a, s1], [out], busy=cost(out, [a]))
        else:
            add("v", lambda: V.tensor_scalar(ap(out), ap(a), ap(s1), ap(s2), op0, op1), [a, s1, s2], [out], busy=cost(out, [a]))

    def cp(out, a, cast=None):
        add("v", lambda: V.tensor_copy(ap(out, cast), ap(a, cast)), [a], [out], busy=cost(out, [a]))

    def scan(out, d0, d1, init, op0, op1):
        add("v", lambda: V.tensor_tensor_scan(ap(out), ap(d0), ap(d1), init, op0, op1), [d0, d1], [out], busy=cost(out, [d0, d1]))

    def ms(out, c, parts=1):
        k = (out[2] - out[1]) // parts
        for x in [out] if parts == 1 else [v(out[0], out[1] + k * i, out[1] + k * i + k) for i in range(parts)]:
            add("v", lambda x=x: V.memset(ap(x), c), (), [x], busy=cost(x, [x]))

    def act(out, a, f=F.Copy, **kw):
        acc = [kw["accum_out"]] if "accum_out" in kw else []
        add("a", lambda: S.activation(ap(out), ap(a), f, **{k: ap(x) for k, x in kw.items()}), [a, kw.get("bias"), kw.get("scale")], [out] + acc,
            busy=(cost(out, [a]) if a[4] else max(64, ACT_START + size(a)) * CYCLE) + 0.02 * len(acc))

    def qz(name, c0, c1, src):
        q, s = v("q" + name, c0, c1), v("s" + name, c0, c1)
        add("v", lambda: V.quantize_mx(ap(q), ap(s), ap(src)), [src], [q, s], busy=0.012 + 0.00022 * size(src))

    def bank(b, m, a=0):
        return v("ps", 512 * b + a, 512 * b + m)

    def mm(bk, st, s0, mv, m0, m, start=True, stop=True):
        x = [v("q" + st, s0, s0 + 128), v("s" + st, s0, s0 + 128), v("q" + mv, m0, m0 + m), v("s" + mv, m0, m0 + m)]
        add("t", lambda: P.matmul_mx(ap(bank(bk, m)), ap(x[0]), ap(x[1]), ap(x[2]), ap(x[3]), start, stop), x, [bank(bk, m)],
            busy=(m + 16) * PE_CYCLE)

    def iota(out, pat, base, cm=0):
        busy = 0.13 + 2 * size(out) * CYCLE
        if SCRATCH[out[0]][2] == I32:
            add("g", lambda: g.iota(ap(out), pat, base, cm), (), [out], busy=busy)
        else:
            add("g", lambda: g.iota(ap(out), pat, base, cm, allow_small_or_imprecise_dtypes=True), (), [out], busy=busy)

    def sel(out, a, pat, op, fill, base, cm):
        add("g", lambda: g.affine_select(ap(out), ap(a), pat, op, fill, base, cm), [a], [out], busy=0.17 + 2 * size(out) * CYCLE)

    def dma(eng, out, a, sem, rd=(), wr=(), more=0.0):
        add(eng, lambda: Q[eng].dma_start(out, a), rd, wr, sem, 16, lag=DMA_LAG + more)

    def L(c, k):
        return v("lst", c, c + k)

    first, second = sorted((prv, nxt), key=lambda d: len(topo.engines(core, d)))
    e1 = topo.engines(core, first)[:8]
    e2 = [e for e in topo.engines(core, second) if e not in e1][:8]
    mask = {first: sum(1 << e for e in e1), second: sum(1 << e for e in e2)}
    assert len(e1) == 8 and len(e2) == 8

    def send(items, cast=None, after=()):
        def fn():
            tr = []
            for dst, src, land, sem in items:
                rid, pid, _se = topo.addr(dst)
                tr.append(RemoteDMATransfer(dst_ids=[DstId(rid=rid, pnc=pid)], dma_engine_mask=mask[dst], remote_sem=T.sem[sem],
                                            src=ap(src, cast), dst=ap(land, cast)))
            g.remote_dma_fused(tr, local_sem=T.sem.sent)
        sent[0] += 8 * len(items)
        return add("g", fn, [x[1] for x in items], (), "-", busy=0.4 if sent[0] > 8 else 1.4, after=after)

    def send_state(dst, src, land, sem, cuts, after=(), more=0.0):
        for a, b in cuts[:-1]:
            after = [send([(dst, v("q" + src, a, b), v("q" + land, a, b), sem)], dt.uint8, after)]
        a, b = cuts[-1]
        call = send([(dst, v("s" + src), v("s" + land), sem)], None, after)
        arrive([v("q" + land, 0, a), v("s" + land)], sem, 8 * len(cuts), call, TILE_LAG + more - 1.5)
        call = send([(dst, v("q" + src, a, b), v("q" + land, a, b), sem + "z")], dt.uint8, [call])
        arrive([v("q" + land, a, b)], sem + "z", 8, call, TILE_LAG + more - 0.4)

    PC = FIRST
    col = lambda i: v("cf", i, i + 1)
    lane_of = lambda k, t: v("st", 512 * k + t, 512 * (k + 1), 4)
    half = lambda nm, h: v(nm, H * h, H * h + H)
    lhalf = lambda nm, h: v(nm, 12 * h, 12 * h + 12)
    piece = lambda nm, h, o=0: v(nm, o + PC[h][0], o + PC[h][1])
    lpiece = lambda nm, h: v(nm, PC[h][0] // 16, PC[h][1] // 16)
    width = lambda h: PC[h][1] - PC[h][0]
    four = lambda nm, h: v(nm, 4 * PC[h][0], 4 * PC[h][1])
    elem = lambda nm, h, b: v(nm, 4 * PC[h][0] + b, 4 * PC[h][1], 4)
    sl = lambda nm, s, m=WU: v(nm, s * W, s * W + m)

    def own(y, f, a, b, src):
        tt(v(y, a, b), src, v("cap", a, b), A.min)
        scan(v(f, a, b), v("rho", a, b), v(y, a, b), -BIG, A.min, A.max)

    def as_list(out, f, row, a, b):
        scan(v(f, a, b), v(row, a, b), v("cs", a, b), K, A.min, A.add)
        ts(v(out, a // 16, b // 16), v(f, a + 15, b, 16), -K, A.add)

    def picked(out, win, lst):
        cp(half(out, 0), at(v(win), lst(0)))
        act(half(out, 1), at(v(win), lst(1)))

    lane = lambda k, a, b: v("ct", 4 * (TO[(24 - k) // 4] + a) + (24 - k) % 4, 4 * (TO[(24 - k) // 4] + b), 4)
    mine = lambda k: v("fs", 16 * k + 15, 16 * k + 16)

    for h, (a, b) in enumerate(PC):
        dma("ssa"[h], T.xt[:, 4 * a:4 * b], T.x[:, 4 * a:4 * b], "dx%d" % h, (), [four("xt", h)], LOAD[h])
        ahead(2.0 - h)
    dma("a", T.ut[:], T.u[:], "du", (), [v("ut")], LOAD[3])
    ahead(3.0)

    iota(v("ci", 0, 1), [[0, 1]], 0, 1)
    for i, (sh, an) in enumerate(((0, 15), (4, 7), (3, 1), (0, 1), (1, 1), (2, 1), (0, 7))):
        ts(v("ci", i + 1, i + 2), v("ci", 0, 1), sh, A.arith_shift_right, an, A.bitwise_and)
    cp(v("cf", 0, 8), v("ci", 0, 8))
    ts(col(8), col(3), 8.0, A.mult, col(1), A.add)
    ts(col(9), col(3), -1.0, A.mult, 1.0, A.add)
    ts(col(10), col(7), 1.0, A.add)
    ts(col(11), col(3), 16.0, A.mult)
    ts(col(12), col(7), -2.0, A.mult, -1.0, A.add)
    ts(col(13), col(3), 32.0 * NP, A.mult, col(7), A.add)
    iota(v("iof"), [[1, C]], 0)
    iota(v("c16", 0, 16), [[1, 16]], 0)
    iota(v("c0"), [[16, 24]], 15)
    ms(v("mu"), 1.0)
    ms(v("one"), 1.0)
    ms(v("mu", 0, C, 16), 0.0)
    ms(v("c16", 48, 64), 0.0)
    ms(v("c16", 63, 64), 2 * K)
    act(v("rho"), v("mu"), F.Identity, scale=2 * BIG, bias=-BIG)
    ts(v("c16", 16, 32), v("c16", 0, 16), col(1), A.is_equal)
    ts(v("c16", 32, 48), v("c16", 0, 16), col(1), A.is_lt)
    ts(L(LP, 24), v("c0"), 0.0, A.mult, col(1), A.add)
    tt(v("c16", 32, 48), v("c16", 32, 48), v("c16", 16, 32), A.subtract)
    ts(v("c16", 32, 48), v("c16", 32, 48), K, A.mult)
    tt(v("c16", 32, 48), v("c16", 32, 48), v("c16", 48, 64), A.add)
    act(v("cap"), at(v("c16", 16, 32), L(LP, 24)), F.Identity, scale=2 * BIG, bias=-BIG)
    act(v("cs"), at(v("c16", 32, 48), L(LP, 24)))
    act(v("cs2"), v("cs"))
    ts(v("c0"), v("c0"), col(1), A.subtract, v("c16", 47, 48), A.add)
    ms(v("rsum"), 0.0)
    ms(v("junk", 255, 256 * 24, 256), 0.0)
    for q in range(6):
        lo = TN[q] - (112 if q == 5 else 48)
        ms(v("ct", 4 * (TO[q] + lo), 4 * (TO[q] + TN[q])), 0.0)
    iota(v("ti"), [[1, 2], [16, 8]], 0)
    cp(L(LU, 16), v("ti"))
    for i, (c, pat, k) in enumerate(((LSW, [[8, 2], [32, 12]], 8), (LEO, [[64 * NP, NS], [16, 2], [32, 2 * NP]], 1),
                                     (LEI, [[64 * NP, NS], [16, 2 * NP], [32 * NP, 2]], 1), (LES, [[8, 2], [64 * NP, NS], [16, 2 * NP]], 13))):
        iota(v("tf", 24 * i, 24 * i + 24), pat, 0)
        ts(L(c, 24), v("tf", 24 * i, 24 * i + 24), col(k), A.add)
    iota(v("rows", 0, WU), [[34, NP], [0, 17], [1, 2]], 0)
    iota(v("rows", WU, W), [[0, W - WU]], 0)
    iota(v("rows", W, W + 12), [[W, NS], [34, NP], [1, 2]], 32)
    iota(v("rows", W + 12, W + 16), [[0, 4]], 32)
    scan(v("rows", 160, 176 + W), v("rows", 0, W + 16), v("cs", 0, W + 16), K, A.min, A.add)
    ts(L(LE, W // 16), v("rows", 175, 160 + W, 16), -K, A.add)
    ts(L(LH, 1), v("rows", 175 + W, 176 + W), -K, A.add)
    iota(v("slot"), [[0, 4], [1, 17], [0, 2]], 0)
    act(v("mw"), v("slot", 0, W), F.Sign)
    act(v("rst"), v("mw"), F.Identity, scale=-B, bias=B)
    act(v("kb", 0, WU), v("slot", 0, WU), F.Sign, bias=col(12))
    iota(v("cb"), [[64, 6], [0, 17], [32, 2]], -1)
    held.add(len(ops) - 1)
    sel(v("cb"), v("cb"), [[0, 6], [1, 17], [0, 2]], A.is_equal, -K, 0, 0)
    ms(v("ky", 0, 2), 0.0)
    for b, pat in enumerate(([[0, 4], [1, 2], [0, 4]], [[0, 2], [1, 2], [0, 8]], [[1, 2], [0, 16]])):
        iota(v("kx", 32 * b, 32 * b + 32), pat, 0)
        ts(v("ky", 36 * b + 2, 36 * b + 34), v("kx", 32 * b, 32 * b + 32), col(4 + b), A.not_equal, B * 2 ** b, A.mult)
    tt(v("ky", 2, 34), v("ky", 2, 34), v("ky", 38, 70), A.add)
    tt(v("ky", 2, 34), v("ky", 2, 34), v("ky", 74, 106), A.add)
    for q in range(NP):
        act(v("kb1", 34 * q, 34 * q + 34), v("ky", 0, 34), F.Identity, bias=-B)
    for s in range(2 * NS):
        act(sl("dd", s, W), v("iof", 0, W), F.Identity, scale=0.0, bias=2 * B)
        act(v("tt", 260 * s, 260 * s + 260), v("iof", 0, 260), scale=0.0)
    for s in range(NS):
        ms(v("ro", s * W + WU, (s + 1) * W), 0.0)
    eye = [[-1, 128]]
    iota(v("jm"), [[1, 8], [0, 16]], 0)
    ts(v("b16"), v("jm"), col(2), A.is_equal)
    for t in range(4):
        act(lane_of(0, t), v("b16"))
    ms(v("b8"), 0.0)
    sel(v("b8"), v("b8"), [[8, 16], [0, 8]], A.is_gt, 1.0, 0, -1)
    sel(v("b8"), v("b8"), [[8, 16], [0, 8]], A.is_ge, 0.0, 7, -1)
    sel(v("jm"), v("b8"), [[1, 128]], A.is_ge, 0.0, 0, -1)
    for k, first_flags, second_flags in ((1, -B, 0.0), (2, -B, -B), (3, B, B), (4, B, B), (5, 0.0, None), (6, -B, -B), (7, B, B)):
        act(lane_of(k, 0), v("b8"), scale=first_flags)
        if second_flags is not None:
            act(lane_of(k, 2), v("b8"), scale=second_flags)
        act(v("st", 512 * k + 1, 512 * k + 512, 2), v("iof", 0, 256), scale=0.0)
    for k, t, x in ((3, 1, B), (4, 3, B), (6, 2, 16 * B), (7, 2, -16 * B)):
        sel(lane_of(k, t), lane_of(k, t), eye, A.not_equal, x, 0, 1)
    sel(lane_of(5, 2), v("jm"), eye, A.not_equal, -8.0, 0, 1)
    for k in range(8):
        qz("s", 128 * k, 128 * k + 128, v("st", 512 * k, 512 * k + 512))
    for h in range(2):
        act(v("et", 258 * h, 258 * h + 258), v("iof", 0, 258), scale=0.0)
    sel(v("et", 3, 515, 4), v("et", 3, 515, 4), eye, A.not_equal, 32.0, 0, 1)
    for b in range(4):
        qz("e", 128 * b, 128 * b + 128, v("et", 3 - b, 515 - b))

    for x in (v("qe"), v("qs", 640, 768), L(LEI, 48), L(LE, 16), v("cb"), v("ro"), v("cf", 10, 12)):
        lead.update({i: 2 * EARLY for i, k, w in seen[x[0]] if w and k & bits(x)})
    for x in (v("tf", 48, 96), v("rows", 0, W + 16), v("jm"), v("et", 3, 515, 4)):
        held.update(i for i, k, w in seen[x[0]] if w and k & bits(x))

    qz("u", 0, 128, v("ut"))
    for i in range(2):
        cp(v("qus", 128 * i, 128 * i + 128), at(v("qu"), L(LU + 8 * i, 8)), dt.uint32)
        ahead(0.5 - 0.5 * i)
        act(v("sus", 128 * i, 128 * i + 128), at(v("su"), L(LU + 8 * i, 8)))
    for h in range(len(PC)):
        qz("x0", PC[h][0], PC[h][1], four("xt", h))

    for r in range(R):
        X, XN, XP, XO = "x%d" % r, "n%d" % r, "p%d" % r, "x%d" % (r + 1)
        PL, PN, OW, ON, OP, HW, HP = ["%s%d" % (nm, r) for nm in ("pl", "pn", "ow", "on", "op", "hw", "hp")]
        send_state(prv, X, XN, "an%d" % r, PC, (), 0.0 if r else LOAD[4])
        b0, b1, b2, b3, b4, b5 = range(6)
        if r:
            ms(v("junk", 255, 256 * 24, 256), 0.0)
            ms(v("rsum"), 0.0)
        mm(b5, "us", 0, X, 0, H)
        own("y1", "fs", 0, H, bank(b5, H))
        mm(b0, "us", 0, X, 0, C)
        mm(b1, "us", 0, X, 0, C)
        mm(b2, "us", 128, X, 0, C)
        own("y1", "fs", H, C, bank(b0, C, H))
        tt(lane(24, 0, C), v("fs"), bank(b0, C), A.is_ge)
        scan(v("seg"), v("mu"), lane(24, 0, C), 0.0, A.mult, A.add)
        for k in range(23, 0, -1):
            m, spare = 16 * k, v("copy", 8 * k * (k - 1), 8 * k * (k + 1))
            if k in KS:
                act(spare, bank(b1, m), F.Sign, scale=-1.0, bias=mine(k))
                act(lane(k, 0, m), spare, F.Relu, accum_out=v("rsum", k, k + 1))
                continue
            ts(lane(k, 0, m), bank(b5 if m < H else b0, m), mine(k), A.is_lt)
            if k in KV[r]:
                scan(v("junk", 256 * k + 256 - m, 256 * k + 256), v("one", 0, m), lane(k, 0, m), 0.0, A.mult, A.add)
            else:
                act(spare, lane(k, 0, m), accum_out=v("rsum", k, k + 1))
        for q in QO:
            qz("c", TO[q], TO[q] + TN[q], v("ct", 4 * TO[q], 4 * (TO[q] + TN[q])))
            mm(b4, "s", 0, "c", TO[q], TN[q], q == 0, q == QO[-1])
        tt(v("t1"), v("c0"), v("seg", 15, C, 16), A.subtract)
        tt(v("t1"), v("t1"), v("junk", 255, 256 * 24, 256), A.subtract)
        ahead(LEAD[5])
        tt(v("cs2", 15, C, 16), v("t1"), v("rsum", 0, 24), A.subtract)
        scan(v("f2"), bank(b4, C), v("cs2"), K, A.min, A.add)
        ts(v(PL), v("f2", 15, C, 16), -K, A.add)
        arrive([v(PN)], "ak%d" % r, 8, send([(prv, v(PL), v(PN), "ak%d" % r)]), LIST_LAG)
        act(v("ma"), bank(b2, C), scale=DS)
        cp(at(v("oS"), v(PL)), v("iof"))
        picked("y1", "oS", lambda h: L(LEO + 12 * h, 12))
        for h in range(2):
            as_list(OW, "fs", "y1", H * h, H * h + H)
            ahead(LEAD[2])
        call = send([(prv, v(OW), v(ON), "al%d" % r), (nxt, v(OW), v(OP), "ao%d" % r)])
        arrive([v(ON)], "al%d" % r, 8, call, 2 * LIST_LAG)
        arrive([v(OP)], "ao%d" % r, 8, call, 2 * LIST_LAG)
        send_state(nxt, X, XP, "ap%d" % r, [(0, C)], [call])
        m = 32 * NP
        for s in range(NS):
            part = lambda i: v("ta", H * i + m * s, H * i + m * s + m)
            act(part(1), at(v("ma"), v(OW, 4 * NP * s, 4 * NP * s + 2 * NP)), F.Identity, scale=col(9))
            act(part(2), at(v("ma"), v(OW, 4 * NP * s + 2 * NP, 4 * NP * (s + 1))), F.Identity, scale=col(3))
            tt(part(0), part(1), part(2), A.add)
        for bk, a, b in ((b3, 0, PC[-1][0]), (b5, PC[-1][0], C)):
            mm(bk, "us", 128, XN, a, b - a)
            act(v("mb", a, b), bank(bk, b - a), scale=DS)
        cp(at(v("bS"), v(PN)), v("mb"))
        for s in range(NS):
            own("y2", "fb", m * s, m * (s + 1), at(v("bS"), L(LSW + 2 * NP * s, 2 * NP)))

        def distances(u):
            for s in range(NS):
                for i in range(2 * NP):
                    a, k = (2 * s + u) * W + 34 * (i // 2) + i % 2, 2 * NP * s + i
                    act(v("dd", a + 2, a + 33, 2), v("ta", 16 * k, 16 * k + 16), F.Abs, scale=-1.0, bias=v("fb", H * u + 16 * k + 15, H * u + 16 * k + 16))

        def in_the_sweeps():
            for a in range(H, C, 64):
                own("y2", "fb", a, a + 64, at(v("bS"), L(LSW + a // 16, 4)))
            cp(v("pi"), v(PL))
            distances(1)
            ts(v("pj", 0, 24), v("pi"), 0, A.arith_shift_right, 8, A.bitwise_and)
            ts(v("pj", 24, 48), v("pi"), 1, A.arith_shift_right, 248, A.bitwise_and)
            ts(v("pj", 48, 72), v("pi"), 0, A.arith_shift_right, 7, A.bitwise_and)
            ts(v("pj", 0, 24), v("pj", 0, 24), 24.0, A.mult)
            tt(v("pj", 24, 48), v("pj", 24, 48), v("pj", 48, 72), A.add)
            tt(v("pj", 72, 96), v("pj", 0, 24), v("pj", 24, 48), A.add)
            cp(v("sp"), v("pj", 72, 96))
            ahead(EARLY)

        distances(0)

        if r == 0:
            dma("s", T.qw[:].bitcast(dt.uint8), T.wc[:], "dw", [v("q" + XP)], [v("qw")])
            dma("s", T.sw[:], T.ws[:], "dw2", [v("q" + XP)], [v("sw")])
            dma("s", T.vt[:], T.v[:], "dv", [v("q" + XP)], [v("vt")])
            qz("v", 0, 128, v("vt"))
            ahead(EARLY)
        for src, dst in ((XN, "dn"), (XP, "gt"), ("g", "dp")):
            for b in range(4):
                mm(DB[b], "e", 128 * b, src, 0, C)
                for h in range(2):
                    out = v("gt", 4 * H * h + b, 4 * H * (h + 1), 4) if dst == "gt" else v(dst, b * C + H * h, b * C + H * h + H)
                    act(out, bank(DB[b], H * h + H, H * h), scale=1 / 32)
                    ahead(0.0 if dst == "gt" else EARLY)
            if dst == "gt":
                for i in range(3):
                    qz("g", 128 * i, 128 * i + 128, v("gt", 512 * i, 512 * i + 512))
        for row, lst, out, back in (("opr", OP, "opn", LEI), ("onr", ON, "ons", LES)):
            for h in range(2):
                act(half(row, h), at(v("iof"), lhalf(lst, h)))
            for h in range(2):
                act(half(out, h), at(v(row), L(back + 12 * h, 12)))
                ahead(EARLY)

        def zl(s, t, a=0, b=WU, step=1):
            return v("tt", 520 * s + 8 + 4 * a + t, 520 * s + 8 + 4 * b, 4 * step)

        def product(bk, s, before, same):
            mm(bk, "s", 128 * before, "f", 132 * s, 128, True, False)
            mm(bk, "s", 128 * same, "f", 132 * s + 2, 128, False, True)

        for w in range(SW):
            for s in range(NS):
                vL, dL, xL, xU = sl("vv", 2 * s), sl("dd", 2 * s), bank(LB[s], WU), bank(UB[s], WU)
                if w == 0:
                    tt(vL, v("dd", 2 * s * W + 2, 2 * s * W + WU + 2), dL, A.is_lt)
                    tt(zl(s, 2), vL, v("kb", 0, WU), A.is_gt)
                    tt(sl("d1", s), dL, v("kb1", 0, WU), A.max)
                elif w == 1:
                    tt(vL, xL, sl("d1", s), A.max)
                    tt(sl("yy", s), xU, v("kb1", 0, WU), A.add)
                    act(zl(s, 1), sl("yy", s), F.Identity, scale=1 / B, bias=-1.0)
                    act(zl(s, 2), v("iof", 0, WU), scale=0.0)
                else:
                    tt(vL, xL, dL, A.max)
                    if w < SW - 1:
                        act(zl(s, 1), xL, F.Identity, scale=1 / B, bias=-1.0)
                    if w == 8:
                        act(zl(s, 2), xL, F.Relu, scale=-1 / B, bias=-7.0)
                    if 8 <= w < SW - 1:
                        act(zl(s, 3), xL, F.Identity, scale=1 / B, bias=7.0)
                if w >= 9:
                    tt(sl("vv", 2 * s + 1), xU, sl("dd", 2 * s + 1), A.max)
                for u in range(2 if w >= 9 else 1 if w else 0):
                    o = (2 * s + u) * W
                    for par in range(2):
                        scan(v("ff", o + par, o + WU, 2), v("rst", par, WU, 2), v("vv", o + par, o + WU, 2), 0.0, A.max, A.min)
                        for q in range(NP):
                            a = o + 34 * q + par
                            out, x, last = zl(s, 2 * u, 34 * q + par, 34 * q + 34, 2), v("ff", a, a + 33, 2), v("ff", a + 32, a + 33)
                            if par == 0 or (q == 0 and w < 9):
                                ts(out, x, last, A.is_gt, -1.0, A.mult)
                            else:
                                act(out, x, F.Sign, scale=-1.0, bias=last)
                qz("f", 132 * s, 132 * s + 130, v("tt", 520 * s, 520 * s + 520))
                if w == 1 and s == 0:
                    in_the_sweeps()
                if w == 0:
                    product(LB[s], s, 7, 6)
                    product(UB[s], s, 4, 2)
                elif w < SW - 1:
                    product(LB[s], s, 1 if w <= 8 else 2, 3)
                    if w == SW - 2:
                        ahead(LEAD[0] * (NS - 1 - s))
                    if w >= 8:
                        product(UB[s], s, 1 if w <= 8 else 2, 4)
                else:
                    product(LB[s], s, 6, 7)
                    mm(UB[s], "s", 640, "f", 132 * s + 2, 128)

        for s in range(NS):
            act(sl("rr", s), bank(LB[s], WU), F.Identity, scale=-1 / B, bias=1.0)
            act(sl("ep", s), bank(UB[s], WU), F.Identity, bias=col(10))
            for par in range(2):
                scan(v("ro", s * W + par, s * W + WU, 2), v("rr", s * W + par, s * W + WU, 2), v("mw", par, WU, 2), 0.0, A.add, A.mult)
            tt(sl("g2", s, W), at(sl("ep", s), L(LE, W // 16)), sl("ro", s, W), A.is_gt)
            for u in range(2):
                for par in range(2):
                    o = (NS * u + s) * W
                    flags = v("g2", s * W + par, s * W + WU, 2) if u else zl(s, 0, par, WU, 2)
                    scan(v("hs", o + par, o + WU, 2), v("cb", WU * s + par, WU * s + WU, 2), flags, -K, A.max, A.add if u else A.subtract)
            if r + 1 < R:
                act(zl(s, 0), v("iof", 0, WU), scale=0.0)
                act(zl(s, 3), v("iof", 0, WU), scale=0.0)
        for u in range(2):
            ts(v(HW, 16 * u, 16 * u + 16), at(v("hs", NS * W * u, NS * W * (u + 1)), L(LH, 1)), col(11), A.add)
            sem = "%s%d" % (("ah", "aj")[u], r)
            arrive([v(HP, 16 * u, 16 * u + 12)], sem, 8, send([(nxt, v(HW, 16 * u, 16 * u + 12), v(HP, 16 * u, 16 * u + 12), sem)]), LIST_LAG)
            for a, b in ((0, 12),) if u else ((0, 6), (6, 12)):
                cp(at(v("wr"), v(HW, 16 * u + a, 16 * u + b)), v("ons", H * u + 16 * a, H * u + 16 * b))
                ahead(0.0 if u else LEAD[4])
        PC = LAST if r + 1 == R else MID
        picked("wj", "wr", lambda h: lhalf(PL, h))
        if r + 1 == R:
            dma("s", T.ol[:], T.wj[0:128:16, :], "out_s", [v("wj")])
        act(half("hr", 0), at(v("opn"), v(HP, 0, 12)))
        cp(v("hr", H, H + 96), at(v("opn"), v(HP, 16, 22)))
        act(v("hr", H + 96, C), at(v("opn"), v(HP, 22, 28)))
        for h in range(2):
            as_list("wl", "f2", "wj", H * h, H * h + H)
        for h in range(len(PC)):
            (cp, act)[h % 2](piece("y1", h), at(v("hr"), lpiece("sp", h)))
            as_list("hl", "fs", "y1", PC[h][0], PC[h][1])
            ahead(LEAD[3] * h)
        for h in range(len(PC)):
            bk = lambda b: (4 + b, b)[h % 2]
            for b in range(4):
                mm(bk(b), "e", 128 * b, X, PC[h][0], width(h), True, False)
                act(piece("vg", h, b * C), at(v("dn", b * C, (b + 1) * C), lpiece("wl", h)))
                tt(elem("zt", h, b), at(v("dp", b * C, (b + 1) * C), lpiece("hl", h)), piece("vg", h, b * C), A.max)
            qz("z", PC[h][0], PC[h][1], four("zt", h))
            for b in range(4):
                mm(bk(b), "w", 128 * b, "z", PC[h][0], width(h), False, True)
                if h + 1 == len(PC) and b in XV:
                    ts(elem("xn", h, b), bank(bk(b), width(h)), 0.03125, A.mult)
                else:
                    act(elem("xn", h, b), bank(bk(b), width(h)), scale=0.03125)
            qz(XO, PC[h][0], PC[h][1], four("xn", h))
            ahead(LEAD[1] * (len(PC) - 1 - h))

    for h, (a, b) in enumerate(PC):
        last = int(b == C)
        dma("s", T.oc[:, 4 * a:4 * b], T.qx2[:, a:b].bitcast(dt.uint8), "out_s", [piece("qx2", h)])
        mm(h, "v", 0, "x2", a, b - a)
        (act, cp)[last](piece("yo", h), bank(h, b - a))
        dma("sa"[last], T.y[:, a:b], T.yo[:, a:b], "out_" + "sa"[last], [piece("yo", h)])
    for k in range(4):
        dma("sa"[k % 2], T.osc[4 * k:4 * k + 4, :], T.sx2[32 * k:32 * k + 4, :], "out_" + "sa"[k % 2], [v("sx2")])

    free = lambda d, i: ops[d][3] == "-" or ops[d][0] == ops[i][0] == "t"
    gap = lambda d, i: ops[d][5] + ops[d][6] + (0.0 if free(d, i) else WAKE)
    chain = [op[5] + op[6] for op in ops]
    for i in reversed(range(len(ops))):
        chain[i] += lead.get(i, 0.0)
        for d in ops[i][2]:
            chain[d] = max(chain[d], gap(d, i) + chain[i])
    left, users = [len(op[2]) for op in ops], [[] for op in ops]
    for i, op in enumerate(ops):
        for d in op[2]:
            users[d].append(i)
    ready, idle, order = [HOLD * (i in held) for i in range(len(ops))], {e: 0.0 for e in ENG + ("x",)}, []
    open_ = {e: [i for i, op in enumerate(ops) if op[0] == e and not op[2]] for e in idle}

    def choice(e):
        best, longest = None, max(chain[i] for q in open_.values() for i in q)
        for i in sorted(open_[e], key=lambda i: (-chain[i], i)):
            t = max(ready[i], idle[e])
            if best is None or (t < best[0] and t + ops[i][5] <= best[0] + (SLIP if chain[i] > longest - SOON else 0.0)):
                best = (t, i)
        return best

    while len(order) < len(ops):
        t, i = min(choice(e) for e in open_ if open_[e])
        e = ops[i][0]
        open_[e].remove(i)
        idle[e] = t + ops[i][5]
        order.append(i)
        for u in users[i]:
            ready[u] = max(ready[u], t + gap(i, u))
            left[u] -= 1
            if not left[u]:
                open_[ops[u][0]].append(u)
    new = {i: k for k, i in enumerate(order)}
    ops = [ops[i][:2] + ({new[d] for d in ops[i][2] if not free(d, i)},) + ops[i][3:5] for i in order]

    chan = lambda i: ops[i][3] if ops[i][3] else "e" + ops[i][0]
    known = {e: {} for e in ENG}
    snap, waits, needed = {}, {}, set()
    for i, (eng, fn, deps, sem, cnt) in enumerate(ops):
        if eng == "x":
            snap[i] = {}
            continue
        kn, w = known[eng], []
        for d in sorted(deps, reverse=True):
            if kn.get(chan(d), -1) >= d:
                continue
            w.append(d)
            needed.add(d)
            kn[chan(d)] = d
            for c, val in snap[d].items():
                if kn.get(c, -1) < val:
                    kn[c] = val
        waits[i], snap[i] = w, dict(kn)
    total, value = {}, {}
    for i, (eng, fn, deps, sem, cnt) in enumerate(ops):
        c = chan(i)
        if eng == "x":
            total[c] = value[i] = cnt
            continue
        for d in waits[i]:
            Q[eng].wait_ge(T.sem[chan(d)], value[d])
        ins = fn()
        if sem == "-":
            continue
        if sem or i in needed:
            k = cnt or 1
            ins.then_inc(T.sem[c], k)
            total[c] = value[i] = total.get(c, 0) + k
    total["sent"] = sent[0]
    for c in sorted(total, key=lambda c: c.startswith("out")):
        g.wait_ge(T.sem[c], total[c])
